import numpy as np, ml_dtypes
CORES = [24,25,26,27,28,29,30,31]
N = 8
import mx_ref
BF = ml_dtypes.bfloat16
def gentries(a):
    return np.ascontiguousarray(a.reshape(8, 16, -1).transpose(0, 2, 1)).reshape(8, -1)
def gtable(e):
    e = np.asarray(e); return np.ascontiguousarray(e.reshape(8, -1, 16).transpose(0, 2, 1)).reshape(128, -1).astype(np.int32)
def gcols(t, e):
    v = np.concatenate([t.reshape(8, 16, -1, 4), np.zeros((8, 16, 1, 4), BF)], axis=2)
    return np.ascontiguousarray(np.stack([v[g][:, e[g]] for g in range(8)])).reshape(128, -1)
def tile(rs):
    return np.stack(rs, axis=2).reshape(128, -1).astype(BF)
def pick(q, e):
    c = np.concatenate([q[0].reshape(128, -1, 4), np.zeros((128, 1, 4), np.uint8)], axis=1); s = np.concatenate([q[1], np.ones((16, 1), np.uint8)], axis=1)
    return (np.ascontiguousarray(c[:, e].reshape(128, -1)), np.ascontiguousarray(s[:, e]))
def join(*qs):
    return (np.concatenate([q[0] for q in qs], axis=1), np.concatenate([q[1] for q in qs], axis=1))
def put(q, e, v):
    c, s = q[0].reshape(128, -1, 4).copy(), q[1].copy(); c[:, e] = v[0].reshape(128, -1, 4); s[:, e] = v[1]
    return (c.reshape(128, -1), s)
def pk(c, s):
    return (np.ascontiguousarray(c), mx_ref.live(s))
def emit(q):
    return q[0], q[1]
def packed(v, rng):
    q = [mx_ref.quantize(np.ascontiguousarray(v[r])) for r in range(N)]
    return np.stack([a for a, b in q]), np.stack([mx_ref.plane(b, rng) for a, b in q])
def values_of_codes():
    e, c = np.zeros((128, 128, 4), np.float32), np.zeros((128, 2, 4), np.uint8)
    e[np.arange(128), np.arange(128), 0] = 1
    c[:127, :, 0] = np.arange(256).reshape(2, 128).T[:127]
    return mx_ref.matmul(mx_ref.quantize(e.reshape(128, 512).astype(BF)), (c.reshape(128, 8), np.full((16, 2), 127, np.uint8))).T.reshape(-1).astype(np.float64)
CODE_VALUE, SCALE_VALUE = values_of_codes(), 2.0 ** (np.arange(256) - 127.0)
def decode(q):
    return (CODE_VALUE[q[0]].reshape(16, 8, -1, 4) * SCALE_VALUE[q[1]][:, None, :, None] + 0.0).reshape(128, -1).astype(np.float32)
def f(rng, *shape):
    return mx_ref.flush((rng.standard_normal(shape, dtype=np.float32) * np.exp2(rng.integers(-2, 3, shape[:-1] + (1,)))).astype(BF))
def wide(rng, *shape, cols=0):
    v = rng.standard_normal(shape, dtype=np.float32) * np.exp2(rng.integers(-12, 13, shape)).astype(np.float32)
    if cols: v *= np.repeat(np.exp2(rng.integers(-cols, cols + 1, shape[:-2] + (1, shape[-1] // 4))) * (rng.random(shape[:-2] + (1, shape[-1] // 4)) > 0.0625), 4, axis=-1).astype(np.float32)
    return mx_ref.flush(v.astype(BF))
C, H, R = 448, 256, 3
def follow(copies, far):
    e = np.tile(np.arange(H + C), (8, 1))
    e[:, H:] -= np.where(copies, far, 0)
    for i in range(C.bit_length()): e = np.take_along_axis(e, e, axis=1)
    return e[:, H:]
def alike(a):
    return np.stack([a] * N)
def trim(v):
    v = v.astype(np.float32)
    v[np.abs(v) < np.float32(2.0 ** -16)] = 0
    return v.astype(BF)
def weights(rng, shut=np.zeros(128, bool)):
    w = trim(f(rng, 128, 2048)).reshape(128, 4, 128, 4)
    w[shut] = 0
    w[:, :, shut] = 0
    c, p = packed(alike(w.reshape(128, 2048)), rng)
    return {"wc": c, "ws": p}
def numbers_of(rng):
    return {"x": trim(f(rng, N, 128, 4 * C)), "u": alike(np.array(f(rng, 128, 512))), "v": np.array(f(rng, N, 128, 512)), "dist": alike(gtable(rng.integers(1, H + 1, (8, C))))}
def first():
    return np.arange(128) % 16 < 8
def heads(d, s, a, b):
    x = d["x"].reshape(N, 8, 16, C, 4)
    x[:, :, :8] = (s * a).astype(np.float32).astype(BF)[:, :, None, :, None]
    u = d["u"].reshape(N, 8, 16, 8, 16, 4)
    u[:, :, :, :, 0] = 0
    for g in range(8): u[:, g, :8, g, 0] = b[g]
    return {**d, "x": x.reshape(N, 128, 4 * C), "u": u.reshape(N, 128, 512)}
def setup_inputs(rng):
    return {**numbers_of(rng), **weights(rng)}
def setup_inputs_deep(rng):
    d = numbers_of(rng)
    k = rng.permutation(8)
    far = rng.integers(1, H + 1, (8, C))
    far[k[:4]] = 1
    far[k[4:6]] = H
    s = rng.permuted(np.tile(np.arange(C) % 2 * 2.0 - 1.0, (N, 8, 1)), axis=2)
    for i in (0, 1, 2, 4, 6): s[:, k[i]] = -1
    s[:, k[1], 0] = 1
    for r in range(N): s[r, k[2], rng.permutation(C)[:3]] = 1
    s[:, k[3]] = (rng.permutation(N) % 2 * 2.0 - 1.0)[:, None]
    d["dist"] = alike(gtable(far))
    return {**heads(d, s, 1.0, [1.0] * 8), **weights(rng, first())}
def setup_inputs_near(rng):
    d = numbers_of(rng)
    s = rng.permuted(np.tile(np.arange(C) % 3 - 1.0, (N, 8, 1)), axis=2)
    k = rng.permutation(8)
    h = int(rng.integers(8))
    d = heads(d, s, np.where(k < 6, 2.0 ** -23, 2.0 ** -30)[:, None], [1.0 if k[g] < 4 else 2.0 ** -25 if k[g] < 6 else 2.0 ** -30 for g in range(8)])
    x = d["x"].reshape(N, 8, 16, C, 4)
    x[:, :, 1:8] = 0
    x[:, :, 0, :, 1:] = 0
    x[:, h, 8:] = 0
    x[:, h, 8, :, 0] = 1
    x[:, h, 9, :, 0] = -1
    u = d["u"].reshape(N, 8, 16, 8, 16, 4)
    for g in range(8):
        if k[g] < 4: u[:, h, 8:10, g, 0, 0] = 1
    shut = first()
    shut[16 * h:16 * h + 16] = True
    return {**d, "x": x.reshape(N, 128, 4 * C), "u": u.reshape(N, 128, 512), **weights(rng, shut)}
def setup_inputs_sums(rng):
    d = numbers_of(rng)
    g = 4 + 2 * int(rng.integers(2))
    blk = np.array([4, 5, 6, 7, 2 * g, 2 * g + 1, 2 * g + 2, 2 * g + 3])
    rest = rng.permutation(np.setdiff1d(np.arange(16), blk))
    x = np.zeros((N, 16, 8, C, 4), np.float32)
    w = np.zeros((128, 4, 128, 4), np.float32)
    u = d["u"].reshape(N, 128, 128, 4)
    u[:, :, ::16] = 0
    r, j = np.arange(N)[:, None], np.arange(C)
    o = np.argsort(rng.random((N, C, 8)), axis=2)
    for h in range(8):
        p, b = h // 4, h % 4
        i = np.take_along_axis(o[:, :, :4], np.argsort(rng.random((N, C, 4)), axis=2), axis=2)
        s = np.take_along_axis(o[:, :, 4:], rng.integers(0, 4, (N, C, 1)), axis=2)
        x[r, blk[i[:, :, 0]], p, j, b] = 1
        x[r, blk[i[:, :, 1]], p, j, b] = -1
        x[r, blk[s[:, :, 0]], p, j, b] = rng.choice([-1.0, 1.0], (N, C)) * 2.0 ** -26
        x[:, rest[h], 0, :, 0] = rng.integers(1, 9, (N, C)) * rng.choice([-1.0, 1.0], (N, C)) * 2.0 ** -26
        u[:, 8 * blk + p, 16 * h, b] = 1
        w[8 * blk + p, 0, 8 * rest[h], b] = 64
    c, q = packed(alike(w.reshape(128, 2048).astype(BF)), rng)
    return {**d, "x": x.reshape(N, 128, 4 * C).astype(BF), "u": u.reshape(N, 128, 512), "wc": c, "ws": q}
def setup_inputs_huge(rng):
    d = numbers_of(rng)
    s = rng.permuted(np.tile(np.arange(C) % 2 * 2.0 - 1.0, (N, 8, 1)), axis=2)
    k = rng.permutation(8)
    s[:, k[0]] = -1
    s[:, k[1]] = 1
    return {**heads(d, s, 2.0 ** 30, [2.0 ** 30] * 8), **weights(rng, first())}
def setup_inputs_spread(rng):
    d = setup_inputs(rng)
    d["x"] = trim(wide(rng, N, 128, 4 * C, cols=6))
    return d
def check_inputs(d):
    b = []
    for k in ("x", "u", "v"):
        a = np.abs(d[k].astype(np.float32))
        if not (np.isfinite(a).all() and ((a == 0) | (a >= 2.0 ** -30) & (a <= 2.0 ** 30)).all()): b.append("a value of " + k)
    for k in ("u", "wc", "dist"):
        if (d[k] != d[k][:1]).any(): b.append(k + " differs between ranks")
    s = [mx_ref.live(p) for p in d["ws"]]
    if any((p != s[0]).any() for p in s): b.append("ws differs between ranks")
    if ((d["wc"] == 127) | (d["wc"] == 255)).any(): b.append("a code of wc")
    if (d["dist"] < 1).any() or (d["dist"] > H).any(): b.append("a number of dist")
    return b
def reference(x, u, v, dist, wc, ws):
    w, qu, far = pk(wc[0], ws[0]), mx_ref.quantize(u[0]), gentries(dist[0])
    now = [x[r] for r in range(N)]
    for t in range(R):
        q = [mx_ref.quantize(now[r]) for r in range(N)]
        full = [decode(q[r]) for r in range(N)]
        roots = []
        for r in range(N):
            e = follow(mx_ref.matmul(qu, q[r])[::16] < 0, far)
            halo = full[r - 1][:, 4 * (C - H):] if r > 0 else np.zeros((128, 4 * H), np.float32)
            z = mx_ref.quantize(gcols(np.concatenate([halo, full[r]], axis=1).astype(BF), e))
            now[r] = tile([full[r][:, b::4] + mx_ref.matmul(pick(w, np.arange(128 * b, 128 * b + 128)), z) * np.float32(0.015625) for b in range(4)])
            roots.append(e - H)
    y, ol = np.zeros((N, 128, C), np.float32), np.zeros((N, 8, C), np.float32)
    oc, osc = np.zeros((N, 128, 4 * C), np.uint8), np.zeros((N, 16, C), np.uint8)
    for r in range(N):
        last = mx_ref.quantize(now[r])
        y[r] = mx_ref.matmul(mx_ref.quantize(v[r]), last)
        ol[r] = roots[r]
        oc[r], osc[r] = emit(last)
    return {"y": y, "ol": ol, "oc": oc, "osc": osc}

@@ -1,0 +1,452 @@
+from concourse.mybir import AluOpType as Op, ActivationFunctionType as Act, dt
+
+F32, B16, I32, U16, U8, X4 = "float32", "bfloat16", "int32", "uint16", "uint8", "float8_e4m3fn_x4"
+C, H, R = 448, 256, 3
+LO = C - H
+SPLIT = 192
+PARTS = ((0, SPLIT), (SPLIT, C))
+HEAD = ("oA2 oB2 U01 U02 oA1 U03 oA0 U1v U1s U11 oA3 U12 oB0 U13 U2s oB1 oB3 h0 h1 h2 U2v h3 U21 e1 U22 e0 U23 E0 E3 E1 E2 "
+        "e2 e3")
+ROUND = ("m0 m1 m2 m3 c0:3 lA m4 m5 m6 gA3s gA1s c3:6 gA2s c6:7 gA0v lB zA gB2v gB3s wA3 wA1 gB0s fA1s wA2 wA0 gB1v zB v "
+         "fA2s wB3 wB1 fB3v wB0 fA0s fA3s wB2 fB1s qA fB0v uA fB2v qB x dAs pA uB dBv pB")
+OWN = (6, 7, 4, 5)
+LEVELS = (4, 16, 64)
+RUN, D = C // 4, 16
+
+SCRATCH = {
+    "z": ("sbuf", [128, 4 * C], B16), "xt": ("sbuf", [128, 4 * C], B16),
+    "zq": ("sbuf", [128, C], X4), "zs": ("sbuf", [128, C], U8),
+    "wq": ("sbuf", [128, 512], X4), "wp": ("sbuf", [128, 512], U8),
+    "ut": ("sbuf", [128, 512], B16), "vt": ("sbuf", [128, 512], B16),
+    "ua": ("sbuf", [128, 128], X4), "uas": ("sbuf", [128, 128], U8),
+    "uq": ("sbuf", [128, 128], X4), "us": ("sbuf", [128, 128], U8),
+    "vq": ("sbuf", [128, 128], X4), "vs": ("sbuf", [128, 128], U8),
+    "one": ("sbuf", [128, 516], B16), "et": ("sbuf", [128, 516], B16), "eq": ("sbuf", [128, 512], X4), "es": ("sbuf", [128, 512], U8),
+    "MN": ("sbuf", [128, H + C], F32), "ff": ("sbuf", [128, C], F32),
+    "ex": ("sbuf", [128, C], F32), "exs": ("sbuf", [128, 384], F32), "exn": ("sbuf", [128, C], F32),
+    "ki": ("sbuf", [128, H], F32), "kt": ("sbuf", [128, RUN], I32), "kb": ("sbuf", [128, RUN], I32), "kd": ("sbuf", [128, RUN], F32),
+    "p1": ("sbuf", [128, C], F32), "db": ("sbuf", [128, C], I32),
+    "pa": ("sbuf", [128, 2], I32), "pm": ("sbuf", [128, 2], I32), "pm3": ("sbuf", [128, 2], I32), "pm4": ("sbuf", [128, 2], I32),
+    "pf": ("sbuf", [128, 2], F32), "p3": ("sbuf", [128, 2], F32), "pe": ("sbuf", [128, 2], F32),
+    "c1": ("sbuf", [128, 28], F32), "gn": ("sbuf", [128, 24], F32), "nn": ("sbuf", [128, 24], F32),
+    "ul": ("sbuf", [128, 8], I32), "lu": ("sbuf", [128, 8], U16),
+    "coli": ("sbuf", [128, 2], F32), "colm": ("sbuf", [128, 2], F32),
+    "lc": ("sbuf", [128, 28], U16), "lz": ("sbuf", [128, 28], U16), "L3": ("sbuf", [128, 28], U16),
+    "yt": ("sbuf", [128, C], F32), "olt": ("sbuf", [128, C], F32),
+    "ps": ("psum", [128, 4096], F32),
+}
+for _i in range(3):
+    SCRATCH["U%d" % _i] = ("sbuf", [128, D + C], F32)
+    SCRATCH["X%d" % _i] = ("sbuf", [128, D + C], F32)
+    SCRATCH["L%d" % _i] = ("sbuf", [128, 24], U16)
+    for _n in ("ra", "tb", "td", "te", "cc"):
+        SCRATCH["%s%d" % (_n, _i)] = ("sbuf", [128, 24], F32)
+    SCRATCH["ti%d" % _i] = ("sbuf", [128, 24], I32)
+    SCRATCH["hq%d" % _i] = ("sbuf", [128, H], X4)
+    SCRATCH["hs%d" % _i] = ("sbuf", [128, H], U8)
+for _i in range(4):
+    SCRATCH["F%d" % _i] = ("sbuf", [128, H + C], B16)
+    SCRATCH["q%d" % _i] = ("sbuf", [128, C], X4)
+    SCRATCH["s%d" % _i] = ("sbuf", [128, C], U8)
+for _i in range(1, R + 1):
+    SCRATCH["t%d" % _i] = ("sbuf", [128, 4 * C], B16)
+
+SEMAPHORES = ["cv", "cs", "ct", "cp", "sent", "arr0", "arr1", "arr2", "ldxa", "ldxb", "ldu", "ldw", "ldb", "ldv", "out"]
+
+
+def rank_program(g, core, T, topo):
+    rank = T.rank_of(core)
+    if rank is None:
+        return
+    n_ranks = len(T.cores)
+    queue = {"v": g.vector, "s": g.scalar, "t": g.tensor, "p": g, "y": g.sync}
+    total = {s: 0 for s in SEMAPHORES}
+    clock = {q: {} for q in queue}
+    log = {}
+
+    def know(q, tok):
+        sem, n, snap = tok
+        if clock[q].get(sem, 0) >= n:
+            return
+        queue[q].wait_ge(T.sem[sem], n)
+        for s, m in snap.items():
+            clock[q][s] = max(clock[q].get(s, 0), m)
+        clock[q][sem] = n
+
+    def depend(q, outs, ins):
+        need = {}
+        for acc, write in [(a, True) for a in outs] + [(a, False) for a in ins]:
+            name, a, b = acc
+            for (c, d, w, oq, tok) in log.get(name, []):
+                if not (a < d and c < b):
+                    continue
+                if name == "ps":
+                    if oq == q and (q == "t" or not (w or write)):
+                        continue
+                elif not (w or write):
+                    continue
+                old = need.get(tok[0])
+                if old is None or old[1] < tok[1]:
+                    need[tok[0]] = tok
+        for tok in sorted(need.values(), key=lambda t: -len(t[2])):
+            know(q, tok)
+
+    def note(q, outs, ins, tok):
+        for acc, write in [(a, True) for a in outs] + [(a, False) for a in ins]:
+            name, a, b = acc
+            old = log.setdefault(name, [])
+            if write:
+                old[:] = [e for e in old if not (a <= e[0] and e[1] <= b)]
+            old.append((a, b, write, q, tok))
+
+    def emit(q, outs, ins, call):
+        depend(q, outs, ins)
+        sem = "c" + q
+        call(queue[q]).then_inc(T.sem[sem], 1)
+        total[sem] += 1
+        note(q, outs, ins, (sem, total[sem], dict(clock[q])))
+
+    def load(q, out, acc, in_, sem, upto):
+        queue[q].dma_start(out, in_).then_inc(T.sem[sem], 16)
+        total[sem] += 16
+        note(q, [acc], [], (sem, upto, dict(clock[q])))
+
+    def store(q, out, in_, acc):
+        depend(q, [], [acc])
+        queue[q].dma_start(out, in_).then_inc(T.sem["out"], 16)
+        total["out"] += 16
+
+    def copy(q, out, oacc, in_, iacc, scale, bias=0.0):
+        if q == "v":
+            emit("v", [oacc], [iacc], lambda e: e.tensor_scalar(out, in_, scale, None, Op.mult))
+        else:
+            emit("s", [oacc], [iacc], lambda e: e.activation(out, in_, Act.Copy, bias=bias, scale=scale))
+
+    def whole(name):
+        return (name, 0, SCRATCH[name][1][1])
+
+    def affine(out, in_, scale, bias=0.0):
+        copy("s", T[out][:], whole(out), T[in_][:], whole(in_), scale, bias)
+
+    def plus(out, in_, col):
+        emit("s", [whole(out)], [whole(in_), whole(col)], lambda e: e.activation(T[out][:], T[in_][:], Act.Identity, bias=T[col][:, 0:1]))
+
+    def small(out, in_, s1, s2, *ops):
+        a1 = T[s1][:, 0:1] if isinstance(s1, str) else s1
+        ins = [whole(in_)] + ([whole(s1)] if isinstance(s1, str) else [])
+        emit("v", [whole(out)], ins, lambda e: e.tensor_scalar(T[out][:], T[in_][:], a1, s2, *ops))
+
+    def both(out, a, b, op):
+        emit("v", [whole(out)], [whole(a), whole(b)], lambda e: e.tensor_tensor(T[out][:], T[a][:], T[b][:], op))
+
+    def cast(out, in_):
+        emit("v", [whole(out)], [whole(in_)], lambda e: e.tensor_copy(T[out][:], T[in_][:]))
+
+    def quant(qn, sn, tn, a, b):
+        emit("v", [(qn, a, b), (sn, a, b)], [(tn, 4 * a, 4 * b)],
+             lambda e: e.quantize_mx(T[qn][:, a:b], T[sn][:, a:b], T[tn][:, 4 * a:4 * b]))
+
+    def psum(bank):
+        return ("ps", 512 * bank, 512 * bank + 512)
+
+    def product(bank, st, c0, mv, a, b, start=True, stop=True):
+        n = b - a
+        emit("t", [psum(bank)], [(st[0], c0, c0 + 128), (st[1], c0, c0 + 128), (mv[0], a, b), (mv[1], a, b)],
+             lambda e: e.matmul_mx(T.ps[:, 512 * bank:512 * bank + n], T[st[0]][:, c0:c0 + 128], T[st[1]][:, c0:c0 + 128],
+                                   T[mv[0]][:, a:b], T[mv[1]][:, a:b], start, stop))
+
+    def unpack(b, c, d, bank):
+        n = d - c
+        copy("s", T["F%d" % b][:, c:d], ("F%d" % b, c, d), T.ps[:, 512 * bank:512 * bank + n], psum(bank), 2.0 ** -6)
+
+    def iota(name, pattern, base, mult, b=None):
+        b = b or SCRATCH[name][1][1]
+        if SCRATCH[name][2] == I32:
+            emit("p", [(name, 0, b)], [], lambda e: e.iota(T[name][:, 0:b], pattern, base, mult))
+        else:
+            emit("p", [(name, 0, b)], [], lambda e: e.iota(T[name][:, 0:b], pattern, base, mult, allow_small_or_imprecise_dtypes=True))
+
+    E, W, U, V = ("eq", "es"), ("wq", "wp"), ("uq", "us"), ("vq", "vs")
+
+    for i in range(16):
+        load("ys"[i % 2], T.db[i:128:16, :], ("db", 0, C), T.dist[:], "ldb", 256)
+    load("y", T.xt[:, 0:4 * SPLIT], ("xt", 0, 4 * SPLIT), T.x[:, 0:4 * SPLIT], "ldxa", 16)
+    load("s", T.ut[:], ("ut", 0, 512), T.u[:], "ldu", 16)
+    load("s", T.xt[:, 4 * SPLIT:4 * C], ("xt", 4 * SPLIT, 4 * C), T.x[:, 4 * SPLIT:4 * C], "ldxb", 16)
+    load("y", T.wq[:].bitcast(dt.uint8), ("wq", 0, 512), T.wc[:], "ldw", 32)
+    load("y", T.wp[:], ("wp", 0, 512), T.ws[:], "ldw", 32)
+    load("y", T.vt[:], ("vt", 0, 512), T.v[:], "ldv", 16)
+
+    iota("pa", [[0, 2]], 0, 1)
+    iota("c1", [[28, 4], [4, 7]], 0, 0)
+    iota("gn", [[0, 3], [16, 8]], 0, 0)
+    iota("kt", [[0, 7], [1, 16]], 128, -1)
+    iota("ul", [[16, 8]], 0, 0)
+    iota("p1", [[1, 4], [4, RUN]], H, 0)
+    iota("one", [[0, 516]], 64, 0)
+    emit("p", [whole("et")], [whole("one")], lambda e: e.affine_select(T.et[:], T.one[:], [[-1, 516]], Op.is_equal, 0.0, 3, 4))
+    iota("MN", [[1, H]], 0, 0, H)
+    small("pm3", "pa", 3, None, Op.bitwise_and)
+    small("pm4", "pa", 15, 2, Op.bitwise_and, Op.arith_shift_right)
+    small("pm", "pa", 15, None, Op.bitwise_and)
+    small("p3", "pm3", float(RUN), None, Op.mult)
+    cast("pf", "pm")
+    both("pe", "p3", "pm4", Op.add)
+    small("lc", "c1", "pe", None, Op.add)
+    small("kb", "kt", 15, None, Op.bitwise_and)
+    small("kd", "kb", 1.0, 1.0 - 2.0 ** -10, Op.min, Op.subtract)
+    cast("lu", "ul")
+    if rank == 0:
+        for b in range(4):
+            emit("v", [("F%d" % b, 0, H)], [], lambda e: e.memset(T["F%d" % b][:, 0:H], 0.0))
+
+    def nothing(name, value):
+        copy("s", T[name][:, 0:D], (name, 0, D), T.c1[:, 0:D], whole("c1"), 0.0, value)
+
+    def keep(a):
+        n = min(RUN, H - a)
+        copy("s", T.ki[:, a:a + n], ("ki", a, a + n), T.kd[:, 0:n], whole("kd"), 2.0 ** 20)
+
+    COUNTS = ((0, RUN), (1, RUN // 4), (2, RUN // 16))
+    plus("nn", "gn", "pf")
+    affine("colm", "pf", 1024.0, -15360.0)
+    keep(0)
+    copy("s", T.exs[:, 127:384:128], whole("exs"), T.c1[:, 0:3], whole("c1"), 0.0)
+    for i, k in COUNTS:
+        affine("td%d" % i, "nn", (C - 1.0) / k, (k * H - D - 0.25) / k)
+        plus("te%d" % i if i else "cc0", "td%d" % i, "colm")
+    nothing("X0", -30000.0)
+    for i, k in COUNTS[1:]:
+        small("ti%d" % i, "nn", -(k - 1) / 2.0, 1.0 / k, Op.add, Op.mult)
+        small("tb%d" % i, "ti%d" % i, -(C - 1.0), None, Op.mult)
+    for i, k in COUNTS[1:]:
+        both("cc%d" % i, "te%d" % i, "tb%d" % i, Op.add)
+
+    def send(t):
+        if rank + 1 == n_ranks:
+            return
+        dst = T.cores[rank + 1]
+        rid, pid = topo.addr(dst)[:2]
+        depend("p", [], [("q%d" % t, LO, C), ("s%d" % t, LO, C)])
+        for out, in_ in ((T["hq%d" % t][:].bitcast(dt.uint8), T["q%d" % t][:, LO:C].bitcast(dt.uint8)), (T["hs%d" % t][:], T["s%d" % t][:, LO:C])):
+            g.remote_dma(out, in_, T.sem["arr%d" % t], T.sem.sent, pid, rid, topo.mask(core, dst))
+            total["sent"] += len(topo.engines(core, dst))
+
+    def arrives(t):
+        n = len(topo.engines(T.cores[rank - 1], core))
+        for name in ("hq%d" % t, "hs%d" % t):
+            log[name] = [(0, H, True, "far", ("arr%d" % t, 2 * n, {}))]
+
+    def row(i):
+        for s in range(1, 4):
+            a, c = D + RUN * s, 128 * s - 128
+            src = T.X0[:, a:a + RUN] if i is None else T["X%d" % i][:, D + s:D + C:4]
+            emit("v", [("exs", c, c + RUN)], [("ki", 0, RUN), ("X%d" % (i or 0), D, D + C)],
+                 lambda e: e.tensor_tensor_scan(T.exs[:, c:c + RUN], T.ki[:, 0:RUN], src, 0.0, Op.add, Op.max))
+
+    def listing(i, k, between=None):
+        emit("v", [whole("ra%d" % i)], [whole("exs"), whole("cc%d" % i)],
+             lambda e: e.tensor_tensor(T["ra%d" % i][:], T.exs[:, 15:384:16], T["cc%d" % i][:], Op.add))
+        if between:
+            between()
+        small("L%d" % i, "ra%d" % i, -float(k), None, Op.mult)
+
+    def merge(kind, i, s):
+        dst, src = "%s%d" % (kind, i), "%s%d" % (kind, i - 1)
+        a = D + RUN * s
+        out, oacc = T[dst][:, a:a + RUN], (dst, a, a + RUN)
+        if i == 0:
+            old, iacc = out, oacc
+        else:
+            old, iacc = T[src][:, D + s:D + C:4], (src, D, D + C)
+        emit("v", [oacc], [(dst, 0, a), whole("L%d" % i), iacc],
+             lambda e: e.tensor_tensor(out, T[dst][:, 0:a].indirect(T["L%d" % i][:, 8 * s - 8:8 * s - 1]), old, Op.max))
+
+    def first(kind, i, qn, r0, r1):
+        dst, src = "%s%d" % (kind, i), "%s%d" % (kind, i - 1)
+        a, b, c, d = D + RUN // 4 * r0, D + RUN // 4 * r1, D + RUN * r0, D + RUN * r1
+        copy(qn, T[dst][:, a:b], (dst, a, b), T[src][:, c:d:4], (src, c, d), 1.0)
+
+    def decide(h, qn):
+        a, b = PARTS[h]
+        in_, bank = T.ps[:, 2048 + 512 * h:2048 + 512 * h + b - a], psum(4 + h)
+        if qn == "v":
+            emit("v", [("ff", a, b)], [bank], lambda e: e.tensor_scalar(T.ff[:, a:b], in_, 0.0, None, Op.is_ge))
+        else:
+            emit("s", [("ff", a, b)], [bank], lambda e: e.activation(T.ff[:, a:b], in_, Act.Sign, bias=2.0 ** -100))
+
+    def places(h):
+        a, b = PARTS[h]
+        for s in range(4):
+            c, d = RUN * s + a // 4, RUN * s + b // 4
+            emit("v", [("U0", D + c, D + d)], [("ff", a, b), ("p1", c, d)],
+                 lambda e: e.tensor_tensor_scan(T.U0[:, D + c:D + d], T.p1[:, c:d], T.ff[:, a + s:b:4], 0.0, Op.max, Op.mult))
+
+    emit("v", [("X0", D, D + C)], [whole("db"), whole("lc"), whole("p1")],
+         lambda e: e.tensor_tensor(T.X0[:, D:D + C], T.db[:].indirect(T.lc[:]), T.p1[:], Op.subtract))
+    row(None)
+    listing(0, RUN)
+    quant("ua", "uas", "ut", 0, 128)
+    emit("s", [whole("us")], [whole("uas"), whole("lu")], lambda e: e.activation(T.us[:], T.uas[:].indirect(T.lu[:]), Act.Copy))
+    quant("q0", "s0", "xt", 0, SPLIT)
+    nothing("U0", -1.0)
+    keep(RUN)
+    for i in (1, 2):
+        nothing("X%d" % i, -30000.0)
+        nothing("U%d" % i, -1.0)
+    affine("coli", "pf", -1024.0, 15360.0)
+    emit("v", [whole("uq")], [whole("ua"), whole("lu")],
+         lambda e: e.tensor_copy(T.uq[:].bitcast(dt.uint32), T.ua[:].bitcast(dt.uint32).indirect(T.lu[:])))
+    keep(2 * RUN)
+    product(4, U, 0, ("q0", "s0"), 0, SPLIT)
+    decide(0, "s")
+    quant("q0", "s0", "xt", SPLIT, C)
+    send(0)
+    product(5, U, 0, ("q0", "s0"), SPLIT, C)
+    merge("X", 0, 1)
+    for b in range(4):
+        c = 128 * b
+        emit("v", [("eq", c, c + 128), ("es", c, c + 128)], [whole("et")],
+             lambda e: e.quantize_mx(T.eq[:, c:c + 128], T.es[:, c:c + 128], T.et[:, 3 - b:515 - b]))
+    places(0)
+    decide(1, "v")
+    places(1)
+
+    for t in range(R):
+        q = ("q%d" % t, "s%d" % t)
+        land = ("hq%d" % t, "hs%d" % t)
+        new = "t%d" % (t + 1)
+        last = t + 1 == R
+        if rank > 0:
+            arrives(t)
+
+        def head(step):
+            k, h, b = step[0], "AB".find(step[1]), step[2] if step[0] in "oU" else step[1]
+            if k == "U":
+                if b == "s":
+                    first("U", int(step[1]), "s", 0, 3)
+                elif b == "v":
+                    first("U", int(step[1]), "v", 3, 4)
+                else:
+                    merge("U", int(step[1]), int(b))
+                return
+            b = int(b)
+            if k == "o":
+                a, e1 = PARTS[h]
+                bank = b if h else OWN[b]
+                product(bank, E, 128 * b, q, a, e1)
+                unpack(b, H + a, H + e1, bank)
+            elif k == "h" and rank > 0:
+                product(4 + b, E, 128 * b, land, 0, H)
+                unpack(b, 0, H, 4 + b)
+            elif k == "e":
+                product(4 + b, E, 128 * b, q, 0, SPLIT, True, False)
+            elif k == "E":
+                product(b, E, 128 * b, q, SPLIT, C, True, False)
+
+        if t == 0:
+            for i in range(3):
+                if i > 0:
+                    first("X", i, "s", 0, 4)
+                    first("U", i, "s", 0, 4)
+                for s in range(1, 4):
+                    if (i, s) != (0, 1):
+                        merge("X", i, s)
+                    if s < 3 or i == 2:
+                        merge("U", i, s)
+                if i < 2:
+                    row(i)
+                    listing(i + 1, RUN // LEVELS[i], lambda: merge("U", i, 3))
+                if i > 0:
+                    for b in range(4):
+                        head("o" + " AB"[i] + str(b))
+            for s in range(7):
+                emit("v", [("exn", 64 * s, 64 * s + 64)], [("ki", 0, 64), ("X2", D, D + C)],
+                     lambda e: e.tensor_tensor_scan(T.exn[:, 64 * s:64 * s + 64], T.ki[:, 0:64], T.X2[:, D + s:D + C:7], 0.0, Op.add, Op.max))
+            emit("v", [whole("L3")], [whole("exn"), whole("coli")],
+                 lambda e: e.tensor_scalar(T.L3[:], T.exn[:, 15:C:16], T.coli[:, 0:1], -1.0, Op.subtract, Op.mult))
+            for k in "heE":
+                for b in range(4):
+                    head(k + str(b))
+        else:
+            for step in HEAD.split():
+                head(step)
+
+        def block(i):
+            c = H + 64 * i
+            emit("v", [("MN", c, c + 64)], [("MN", 0, c), ("L3", 4 * i, 4 * i + 4), ("U2", D, D + C)],
+                 lambda e: e.tensor_tensor(T.MN[:, c:c + 64], T.MN[:, 0:c].indirect(T.L3[:, 4 * i:4 * i + 4]), T.U2[:, D + i:D + C:7], Op.max))
+
+        def collect(a, b):
+            emit("v", [("ex", a, b)], [("ki", 0, b - a), ("MN", H + a, H + b)],
+                 lambda e: e.tensor_tensor_scan(T.ex[:, a:b], T.ki[:, 0:b - a], T.MN[:, H + a:H + b], 0.0, Op.add, Op.max))
+
+        def listed(a, b):
+            emit("v", [("lz", a // 16, b // 16)], [("ex", a, b), whole("coli")],
+                 lambda e: e.tensor_scalar(T.lz[:, a // 16:b // 16], T.ex[:, a + 15:b:16], T.coli[:, 0:1], None, Op.subtract))
+
+        def gather(qn, b, h):
+            a, e1 = PARTS[h]
+            out, src = T.z[:, 4 * a + b:4 * e1:4], T["F%d" % b][:, 0:H + C].indirect(T.lz[:, a // 16:e1 // 16])
+            outs, ins = [("z", 4 * a + b, 4 * a + b + 1)], [whole("F%d" % b), ("lz", a // 16, e1 // 16)]
+            if qn == "v":
+                emit("v", outs, ins, lambda e: e.tensor_copy(out, src))
+            else:
+                emit("s", outs, ins, lambda e: e.activation(out, src, Act.Copy))
+
+        def finish(qn, h, b):
+            a, e1 = PARTS[h]
+            bank = 4 - 4 * h + b
+            copy(qn, T[new][:, 4 * a + b:4 * e1:4], (new, 4 * a + b, 4 * a + b + 1), T.ps[:, 512 * bank:512 * bank + e1 - a], psum(bank), 2.0 ** -6)
+
+        q = ("q%d" % (t + 1), "s%d" % (t + 1))
+        for step in ROUND.split():
+            k = step[0]
+            if k == "m":
+                block(int(step[1:]))
+                continue
+            if k == "c":
+                a, b = step[1:].split(":")
+                collect(64 * int(a), 64 * int(b))
+                continue
+            if k == "x" or k == "v":
+                if k == "v" and last:
+                    quant("vq", "vs", "vt", 0, 128)
+                elif k == "x" and not last:
+                    send(t + 1)
+                continue
+            h = "AB".index(step[1])
+            a, b = PARTS[h]
+            if k == "l":
+                listed(a, b)
+            elif k == "g":
+                gather(step[3], int(step[2]), h)
+            elif k == "z":
+                quant("zq", "zs", "z", a, b)
+            elif k == "w":
+                n = int(step[2])
+                product(4 - 4 * h + n, W, 128 * n, ("zq", "zs"), a, b, False, True)
+            elif k == "f":
+                finish(step[3], h, int(step[2]))
+            elif k == "q":
+                quant(q[0], q[1], new, a, b)
+                if last:
+                    store("y", T.oc[:, 4 * a:4 * b], T[q[0]][:, a:b].bitcast(dt.uint8), (q[0], a, b))
+            elif k == "u":
+                product(4 + h, V if last else U, 0, q, a, b)
+            elif k == "d" and last:
+                c = 2048 + 512 * h
+                copy(step[2], T.yt[:, a:b], ("yt", a, b), T.ps[:, c:c + b - a], psum(4 + h), 1.0)
+                store("sy"[h], T.y[:, a:b], T.yt[:, a:b], ("yt", a, b))
+            elif k == "d":
+                decide(h, step[2])
+            elif k == "p" and not last:
+                places(h)
+
+    copy("s", T.olt[:], whole("olt"), T.MN[:, H:H + C], ("MN", H, H + C), 1.0, -float(H))
+    store("s", T.ol[:], T.olt[0:128:16, :], whole("olt"))
+    for k in range(4):
+        store("y" if k < 2 else "s", T.osc[4 * k:4 * k + 4, :], T[q[1]][32 * k:32 * k + 4, :], (q[1], 0, C))
+    for sem in SEMAPHORES:
+        if total[sem]:
+            g.wait_ge(T.sem[sem], total[sem])

@@ -5,13 +5,16 @@ C, H, R = 448, 256, 3
 LO = C - H
 SPLIT = 192
 PARTS = ((0, SPLIT), (SPLIT, C))
-HEAD = ("oA2 oB2 U01 U02 oA1 U03 oA0 U1v U1s U11 oA3 U12 oB0 U13 U2s oB1 oB3 h0 h1 h2 U2v h3 U21 e1 U22 e0 U23 E0 E3 E1 E2 "
-        "e2 e3")
-ROUND = ("m0 m1 m2 m3 c0:3 lA m4 m5 m6 gA3s gA1s c3:6 gA2s c6:7 gA0v lB zA gB2v gB3s wA3 wA1 gB0s fA1s wA2 wA0 gB1v zB v "
-         "fA2s wB3 wB1 fB3v wB0 fA0s fA3s wB2 fB1s qA fB0v uA fB2v qB x dAs pA uB dBv pB")
+START = ("XA02 XB02 UA01 XA03 XB03 UA02 rA1 XA1s UB01 rB1 XB1s aA1 UA03 aB1 LA1 UB02 LB1 UA1s XA11 UB03 XB11 UB1s oA0 oA1 oA2 oA3 "
+         "XA12 UA11 XB12 XA13 UB11 XB13 rA2 XA2s UA12 rB2 XB2s aA2 UB12 aB2 LA2 UA13 LB2 UA2s XA21 UB13 XB21 UB2s oB0 oB1 oB2 oB3 "
+         "XA22 UA21 XB22 XA23 UB21 XB23 rA3 UA22 rB3 LA3 UB22 LB3 UA23 h0 h1 h2 h3 m0 UB23 e0 e1 e2 e3 E0 E1 E2 E3 m1")
+HEAD = ("oA2 oB2 oA1 oA0 oA3 oB0 oB1 oB3 h0 h1 h2 h3 e1 e0 E0 E3 E1 E2 e2 e3 "
+        "UA03 UB01 UA10 UB02 UA11 UB03 UA12 UB10 UA13 UB11 UA20 UB12 UA21 UB13 UA22 UB20 UA23 UB21 m0 UB22 m1 UB23")
+ROUND = ("m2 m3 c0:3 m4 lA m5 gA3s gA1s gA2s gA0v m6 c3:6 c6:7 lB zA gB2v gB3s wA3 wA1 gB0s fA1s wA2 wA0 gB1v zB v "
+         "fA2s wB3 wB1 fB3v wB0 fA0s fA3s wB2 fB1s qA fB0v uA fB2v qB x dAs pA uB UA01 dBv UA02 pB")
 OWN = (6, 7, 4, 5)
 LEVELS = (4, 16, 64)
-RUN, D = C // 4, 16
+D, GAP = 16, 64
 
 SCRATCH = {
     "z": ("sbuf", [128, 4 * C], B16), "xt": ("sbuf", [128, 4 * C], B16),
@@ -23,25 +26,28 @@ SCRATCH = {
     "vq": ("sbuf", [128, 128], X4), "vs": ("sbuf", [128, 128], U8),
     "one": ("sbuf", [128, 516], B16), "et": ("sbuf", [128, 516], B16), "eq": ("sbuf", [128, 512], X4), "es": ("sbuf", [128, 512], U8),
     "MN": ("sbuf", [128, H + C], F32), "ff": ("sbuf", [128, C], F32),
-    "ex": ("sbuf", [128, C], F32), "exs": ("sbuf", [128, 384], F32), "exn": ("sbuf", [128, C], F32),
-    "ki": ("sbuf", [128, H], F32), "kt": ("sbuf", [128, RUN], I32), "kb": ("sbuf", [128, RUN], I32), "kd": ("sbuf", [128, RUN], F32),
-    "p1": ("sbuf", [128, C], F32), "db": ("sbuf", [128, C], I32),
-    "pa": ("sbuf", [128, 2], I32), "pm": ("sbuf", [128, 2], I32), "pm3": ("sbuf", [128, 2], I32), "pm4": ("sbuf", [128, 2], I32),
-    "pf": ("sbuf", [128, 2], F32), "p3": ("sbuf", [128, 2], F32), "pe": ("sbuf", [128, 2], F32),
-    "c1": ("sbuf", [128, 28], F32), "gn": ("sbuf", [128, 24], F32), "nn": ("sbuf", [128, 24], F32),
+    "ex": ("sbuf", [128, C], F32), "exn": ("sbuf", [128, C], F32),
+    "ki": ("sbuf", [128, H], F32), "kt": ("sbuf", [128, 64], I32), "kb": ("sbuf", [128, 64], I32), "kd": ("sbuf", [128, 64], F32),
+    "pn": ("sbuf", [128, C], F32), "wn": ("sbuf", [128, H], F32), "xn": ("sbuf", [128, C], F32),
+    "dl": ("sbuf", [128, 28], I32), "du": ("sbuf", [128, 28], U16),
+    "pa": ("sbuf", [128, 2], I32), "pm": ("sbuf", [128, 2], I32), "pf": ("sbuf", [128, 2], F32),
+    "c1": ("sbuf", [128, 16], F32), "gn": ("sbuf", [128, 12], F32), "nn": ("sbuf", [128, 12], F32),
     "ul": ("sbuf", [128, 8], I32), "lu": ("sbuf", [128, 8], U16),
     "coli": ("sbuf", [128, 2], F32), "colm": ("sbuf", [128, 2], F32),
-    "lc": ("sbuf", [128, 28], U16), "lz": ("sbuf", [128, 28], U16), "L3": ("sbuf", [128, 28], U16),
+    "lz": ("sbuf", [128, 28], U16), "L3": ("sbuf", [128, 28], U16),
     "yt": ("sbuf", [128, C], F32), "olt": ("sbuf", [128, C], F32),
     "ps": ("psum", [128, 4096], F32),
 }
+for _p, (_a, _b) in zip("AB", PARTS):
+    SCRATCH["exs" + _p] = ("sbuf", [128, 3 * GAP], F32)
+    for _i in range(3):
+        SCRATCH["U%s%d" % (_p, _i)] = ("sbuf", [128, D + _b - _a], F32)
+        SCRATCH["X%s%d" % (_p, _i)] = ("sbuf", [128, D + _b - _a], F32)
+        SCRATCH["L%s%d" % (_p, _i)] = ("sbuf", [128, 12], U16)
+        for _n in ("ra", "tb", "td", "cc"):
+            SCRATCH["%s%s%d" % (_n, _p, _i)] = ("sbuf", [128, 12], F32)
+        SCRATCH["ti%s%d" % (_p, _i)] = ("sbuf", [128, 12], I32)
 for _i in range(3):
-    SCRATCH["U%d" % _i] = ("sbuf", [128, D + C], F32)
-    SCRATCH["X%d" % _i] = ("sbuf", [128, D + C], F32)
-    SCRATCH["L%d" % _i] = ("sbuf", [128, 24], U16)
-    for _n in ("ra", "tb", "td", "te", "cc"):
-        SCRATCH["%s%d" % (_n, _i)] = ("sbuf", [128, 24], F32)
-    SCRATCH["ti%d" % _i] = ("sbuf", [128, 24], I32)
     SCRATCH["hq%d" % _i] = ("sbuf", [128, H], X4)
     SCRATCH["hs%d" % _i] = ("sbuf", [128, H], U8)
 for _i in range(4):
@@ -128,13 +134,10 @@ def rank_program(g, core, T, topo):
     def affine(out, in_, scale, bias=0.0):
         copy("s", T[out][:], whole(out), T[in_][:], whole(in_), scale, bias)
 
-    def plus(out, in_, col):
-        emit("s", [whole(out)], [whole(in_), whole(col)], lambda e: e.activation(T[out][:], T[in_][:], Act.Identity, bias=T[col][:, 0:1]))
-
     def small(out, in_, s1, s2, *ops):
-        a1 = T[s1][:, 0:1] if isinstance(s1, str) else s1
-        ins = [whole(in_)] + ([whole(s1)] if isinstance(s1, str) else [])
-        emit("v", [whole(out)], ins, lambda e: e.tensor_scalar(T[out][:], T[in_][:], a1, s2, *ops))
+        a1, a2 = [T[s][:, 0:1] if isinstance(s, str) else s for s in (s1, s2)]
+        ins = [whole(in_)] + [whole(s) for s in (s1, s2) if isinstance(s, str)]
+        emit("v", [whole(out)], ins, lambda e: e.tensor_scalar(T[out][:], T[in_][:], a1, a2, *ops))
 
     def both(out, a, b, op):
         emit("v", [whole(out)], [whole(a), whole(b)], lambda e: e.tensor_tensor(T[out][:], T[a][:], T[b][:], op))
@@ -159,17 +162,15 @@ def rank_program(g, core, T, topo):
         n = d - c
         copy("s", T["F%d" % b][:, c:d], ("F%d" % b, c, d), T.ps[:, 512 * bank:512 * bank + n], psum(bank), 2.0 ** -6)
 
-    def iota(name, pattern, base, mult, b=None):
-        b = b or SCRATCH[name][1][1]
+    def iota(name, pattern, base, mult):
         if SCRATCH[name][2] == I32:
-            emit("p", [(name, 0, b)], [], lambda e: e.iota(T[name][:, 0:b], pattern, base, mult))
+            emit("p", [whole(name)], [], lambda e: e.iota(T[name][:], pattern, base, mult))
         else:
-            emit("p", [(name, 0, b)], [], lambda e: e.iota(T[name][:, 0:b], pattern, base, mult, allow_small_or_imprecise_dtypes=True))
+            emit("p", [whole(name)], [], lambda e: e.iota(T[name][:], pattern, base, mult, allow_small_or_imprecise_dtypes=True))
 
     E, W, U, V = ("eq", "es"), ("wq", "wp"), ("uq", "us"), ("vq", "vs")
 
-    for i in range(16):
-        load("ys"[i % 2], T.db[i:128:16, :], ("db", 0, C), T.dist[:], "ldb", 256)
+    load("y", T.dl[:], whole("dl"), T.dist[:], "ldb", 16)
     load("y", T.xt[:, 0:4 * SPLIT], ("xt", 0, 4 * SPLIT), T.x[:, 0:4 * SPLIT], "ldxa", 16)
     load("s", T.ut[:], ("ut", 0, 512), T.u[:], "ldu", 16)
     load("s", T.xt[:, 4 * SPLIT:4 * C], ("xt", 4 * SPLIT, 4 * C), T.x[:, 4 * SPLIT:4 * C], "ldxb", 16)
@@ -178,49 +179,55 @@ def rank_program(g, core, T, topo):
     load("y", T.vt[:], ("vt", 0, 512), T.v[:], "ldv", 16)
 
     iota("pa", [[0, 2]], 0, 1)
-    iota("c1", [[28, 4], [4, 7]], 0, 0)
-    iota("gn", [[0, 3], [16, 8]], 0, 0)
-    iota("kt", [[0, 7], [1, 16]], 128, -1)
+    iota("gn", [[0, 3], [16, 4]], 0, 0)
+    iota("kt", [[0, 4], [1, 16]], 128, -1)
+    iota("wn", [[1, H]], 1, 0)
     iota("ul", [[16, 8]], 0, 0)
-    iota("p1", [[1, 4], [4, RUN]], H, 0)
     iota("one", [[0, 516]], 64, 0)
     emit("p", [whole("et")], [whole("one")], lambda e: e.affine_select(T.et[:], T.one[:], [[-1, 516]], Op.is_equal, 0.0, 3, 4))
-    iota("MN", [[1, H]], 0, 0, H)
-    small("pm3", "pa", 3, None, Op.bitwise_and)
-    small("pm4", "pa", 15, 2, Op.bitwise_and, Op.arith_shift_right)
-    small("pm", "pa", 15, None, Op.bitwise_and)
-    small("p3", "pm3", float(RUN), None, Op.mult)
-    cast("pf", "pm")
-    both("pe", "p3", "pm4", Op.add)
-    small("lc", "c1", "pe", None, Op.add)
-    small("kb", "kt", 15, None, Op.bitwise_and)
-    small("kd", "kb", 1.0, 1.0 - 2.0 ** -10, Op.min, Op.subtract)
-    cast("lu", "ul")
+    emit("v", [whole("c1")], [], lambda e: e.memset(T.c1[:], 0.0))
     if rank == 0:
         for b in range(4):
             emit("v", [("F%d" % b, 0, H)], [], lambda e: e.memset(T["F%d" % b][:, 0:H], 0.0))
+    small("pm", "pa", 15, None, Op.bitwise_and)
+    cast("pf", "pm")
+    small("kb", "kt", 15, None, Op.bitwise_and)
+    small("nn", "gn", "pf", None, Op.add)
+    small("colm", "pf", 1024.0, -15360.0, Op.mult, Op.add)
+    small("kd", "kb", 1.0, 1.0 - 2.0 ** -10, Op.min, Op.subtract)
 
     def nothing(name, value):
         copy("s", T[name][:, 0:D], (name, 0, D), T.c1[:, 0:D], whole("c1"), 0.0, value)
 
     def keep(a):
-        n = min(RUN, H - a)
-        copy("s", T.ki[:, a:a + n], ("ki", a, a + n), T.kd[:, 0:n], whole("kd"), 2.0 ** 20)
+        copy("s", T.ki[:, a:a + 64], ("ki", a, a + 64), T.kd[:], whole("kd"), 2.0 ** 20)
 
-    COUNTS = ((0, RUN), (1, RUN // 4), (2, RUN // 16))
-    plus("nn", "gn", "pf")
-    affine("colm", "pf", 1024.0, -15360.0)
+    def count(h, i):
+        return (PARTS[h][1] - PARTS[h][0]) // LEVELS[i]
+
+    pairs = [(h, i) for i in range(3) for h in range(2)]
+    for h, i in pairs:
+        k, (a, b) = count(h, i), PARTS[h]
+        small("td%s%d" % ("AB"[h], i), "nn", (b - a - 1.0) / k, (k * (H + a) - D - 0.25) / k, Op.mult, Op.add)
+    for h, i in pairs:
+        k, n = count(h, i), "AB"[h] + str(i)
+        if i == 0:
+            small("cc" + n, "td" + n, "colm", None, Op.add)
+        else:
+            small("ti" + n, "nn", -(k - 1) / 2.0, 1.0 / k, Op.add, Op.mult)
+    nothing("XA0", -30000.0)
+    nothing("XB0", -30000.0)
+    copy("s", T.exsA[:, GAP - 1:3 * GAP:GAP], whole("exsA"), T.c1[:, 0:3], whole("c1"), 0.0)
     keep(0)
-    copy("s", T.exs[:, 127:384:128], whole("exs"), T.c1[:, 0:3], whole("c1"), 0.0)
-    for i, k in COUNTS:
-        affine("td%d" % i, "nn", (C - 1.0) / k, (k * H - D - 0.25) / k)
-        plus("te%d" % i if i else "cc0", "td%d" % i, "colm")
-    nothing("X0", -30000.0)
-    for i, k in COUNTS[1:]:
-        small("ti%d" % i, "nn", -(k - 1) / 2.0, 1.0 / k, Op.add, Op.mult)
-        small("tb%d" % i, "ti%d" % i, -(C - 1.0), None, Op.mult)
-    for i, k in COUNTS[1:]:
-        both("cc%d" % i, "te%d" % i, "tb%d" % i, Op.add)
+    copy("s", T.pn[:, 0:H], ("pn", 0, H), T.wn[:], whole("wn"), 1.0, H - 1.0)
+    copy("s", T.pn[:, H:C], ("pn", H, C), T.wn[:, 0:C - H], whole("wn"), 1.0, 2 * H - 1.0)
+    for h, i in pairs[2:]:
+        n = "AB"[h] + str(i)
+        small("tb" + n, "ti" + n, -(PARTS[h][1] - PARTS[h][0] - 1.0), "colm", Op.mult, Op.add)
+    cast("lu", "ul")
+    for h, i in pairs[2:]:
+        n = "AB"[h] + str(i)
+        both("cc" + n, "td" + n, "tb" + n, Op.add)
 
     def send(t):
         if rank + 1 == n_ranks:
@@ -237,35 +244,56 @@ def rank_program(g, core, T, topo):
         for name in ("hq%d" % t, "hs%d" % t):
             log[name] = [(0, H, True, "far", ("arr%d" % t, 2 * n, {}))]
 
-    def row(i):
-        for s in range(1, 4):
-            a, c = D + RUN * s, 128 * s - 128
-            src = T.X0[:, a:a + RUN] if i is None else T["X%d" % i][:, D + s:D + C:4]
-            emit("v", [("exs", c, c + RUN)], [("ki", 0, RUN), ("X%d" % (i or 0), D, D + C)],
-                 lambda e: e.tensor_tensor_scan(T.exs[:, c:c + RUN], T.ki[:, 0:RUN], src, 0.0, Op.add, Op.max))
-
-    def listing(i, k, between=None):
-        emit("v", [whole("ra%d" % i)], [whole("exs"), whole("cc%d" % i)],
-             lambda e: e.tensor_tensor(T["ra%d" % i][:], T.exs[:, 15:384:16], T["cc%d" % i][:], Op.add))
-        if between:
-            between()
-        small("L%d" % i, "ra%d" % i, -float(k), None, Op.mult)
-
-    def merge(kind, i, s):
-        dst, src = "%s%d" % (kind, i), "%s%d" % (kind, i - 1)
-        a = D + RUN * s
-        out, oacc = T[dst][:, a:a + RUN], (dst, a, a + RUN)
+    def before(kind, h, i, s):
+        a, b = PARTS[h]
         if i == 0:
-            old, iacc = out, oacc
-        else:
-            old, iacc = T[src][:, D + s:D + C:4], (src, D, D + C)
-        emit("v", [oacc], [(dst, 0, a), whole("L%d" % i), iacc],
-             lambda e: e.tensor_tensor(out, T[dst][:, 0:a].indirect(T["L%d" % i][:, 8 * s - 8:8 * s - 1]), old, Op.max))
+            return T.xn[:, a + s:b:4], ("xn", a, b)
+        src = "%s%s%d" % (kind, "AB"[h], i - 1)
+        return T[src][:, D + s:D + b - a:4], (src, D, D + b - a)
 
-    def first(kind, i, qn, r0, r1):
-        dst, src = "%s%d" % (kind, i), "%s%d" % (kind, i - 1)
-        a, b, c, d = D + RUN // 4 * r0, D + RUN // 4 * r1, D + RUN * r0, D + RUN * r1
-        copy(qn, T[dst][:, a:b], (dst, a, b), T[src][:, c:d:4], (src, c, d), 1.0)
+    def row(h, i):
+        p, (a, b) = "AB"[h], PARTS[h]
+        if i == 3:
+            k = count(h, 2)
+            for s in range(k):
+                c = a + 64 * s
+                emit("v", [("exn", c, c + 64)], [("ki", 0, 64), whole("X%s2" % p)],
+                     lambda e: e.tensor_tensor_scan(T.exn[:, c:c + 64], T.ki[:, 0:64], T["X%s2" % p][:, D + s:D + b - a:k], 0.0, Op.add, Op.max))
+            return
+        run = (b - a) // 4
+        for s in range(1, 4):
+            c = GAP * (s - 1)
+            src, acc = before("X", h, i, s)
+            emit("v", [("exs" + p, c, c + run)], [("ki", 0, run), acc],
+                 lambda e: e.tensor_tensor_scan(T["exs" + p][:, c:c + run], T.ki[:, 0:run], src, 0.0, Op.add, Op.max))
+
+    def sums(h, i):
+        n = "AB"[h] + str(i)
+        emit("v", [whole("ra" + n)], [whole("exs" + n[0]), whole("cc" + n)],
+             lambda e: e.tensor_tensor(T["ra" + n][:], T["exs" + n[0]][:, 15:3 * GAP:16], T["cc" + n][:], Op.add))
+
+    def listing(h, i):
+        if i == 3:
+            a, b = PARTS[h]
+            emit("v", [("L3", a // 16, b // 16)], [("exn", a, b), whole("coli")],
+                 lambda e: e.tensor_scalar(T.L3[:, a // 16:b // 16], T.exn[:, a + 15:b:16], T.coli[:, 0:1], -1.0, Op.subtract, Op.mult))
+        else:
+            n = "AB"[h] + str(i)
+            small("L" + n, "ra" + n, -float(count(h, i)), None, Op.mult)
+
+    def merge(kind, h, i, s):
+        n = "AB"[h] + str(i)
+        dst, run = kind + n, (PARTS[h][1] - PARTS[h][0]) // 4
+        if s in "0s":
+            old, iacc = before(kind, h, i, 0)
+            copy("v" if s == "0" else "s", T[dst][:, D:D + run], (dst, D, D + run), old, iacc, 1.0)
+            return
+        s = int(s)
+        a = D + run * s
+        out, oacc = T[dst][:, a:a + run], (dst, a, a + run)
+        old, iacc = (out, oacc) if kind + str(i) == "U0" else before(kind, h, i, s)
+        emit("v", [oacc], [(dst, 0, a), whole("L" + n), iacc],
+             lambda e: e.tensor_tensor(out, T[dst][:, 0:a].indirect(T["L" + n][:, 4 * s - 4:4 * s - 4 + run // 16]), old, Op.max))
 
     def decide(h, qn):
         a, b = PARTS[h]
@@ -277,33 +305,42 @@ def rank_program(g, core, T, topo):
 
     def places(h):
         a, b = PARTS[h]
+        dst, run = "U%s0" % "AB"[h], (b - a) // 4
         for s in range(4):
-            c, d = RUN * s + a // 4, RUN * s + b // 4
-            emit("v", [("U0", D + c, D + d)], [("ff", a, b), ("p1", c, d)],
-                 lambda e: e.tensor_tensor_scan(T.U0[:, D + c:D + d], T.p1[:, c:d], T.ff[:, a + s:b:4], 0.0, Op.max, Op.mult))
+            c = D + run * s
+            emit("v", [(dst, c, c + run)], [("ff", a, b), ("pn", a, b)],
+                 lambda e: e.tensor_tensor_scan(T[dst][:, c:c + run], T.pn[:, a + s:b:4], T.ff[:, a + s:b:4], 0.0, Op.max, Op.mult))
 
-    emit("v", [("X0", D, D + C)], [whole("db"), whole("lc"), whole("p1")],
-         lambda e: e.tensor_tensor(T.X0[:, D:D + C], T.db[:].indirect(T.lc[:]), T.p1[:], Op.subtract))
-    row(None)
-    listing(0, RUN)
+    small("du", "dl", -1.0, None, Op.add)
+    for a, b in PARTS:
+        emit("v", [("xn", a, b)], [whole("wn"), whole("du"), ("pn", a, b)],
+             lambda e: e.tensor_tensor(T.xn[:, a:b], T.wn[:].indirect(T.du[:, a // 16:b // 16]), T.pn[:, a:b], Op.subtract))
+    row(0, 0)
+    merge("X", 0, 0, "s")
+    row(1, 0)
+    merge("X", 1, 0, "s")
+    sums(0, 0)
     quant("ua", "uas", "ut", 0, 128)
     emit("s", [whole("us")], [whole("uas"), whole("lu")], lambda e: e.activation(T.us[:], T.uas[:].indirect(T.lu[:]), Act.Copy))
     quant("q0", "s0", "xt", 0, SPLIT)
-    nothing("U0", -1.0)
-    keep(RUN)
-    for i in (1, 2):
-        nothing("X%d" % i, -30000.0)
-        nothing("U%d" % i, -1.0)
-    affine("coli", "pf", -1024.0, 15360.0)
+    sums(1, 0)
+    listing(0, 0)
+    nothing("UA0", -1.0)
+    nothing("UB0", -1.0)
     emit("v", [whole("uq")], [whole("ua"), whole("lu")],
          lambda e: e.tensor_copy(T.uq[:].bitcast(dt.uint32), T.ua[:].bitcast(dt.uint32).indirect(T.lu[:])))
-    keep(2 * RUN)
+    listing(1, 0)
     product(4, U, 0, ("q0", "s0"), 0, SPLIT)
     decide(0, "s")
     quant("q0", "s0", "xt", SPLIT, C)
     send(0)
     product(5, U, 0, ("q0", "s0"), SPLIT, C)
-    merge("X", 0, 1)
+    for i in (1, 2):
+        for p in "AB":
+            nothing("X%s%d" % (p, i), -30000.0)
+            nothing("U%s%d" % (p, i), -1.0)
+    merge("X", 0, 0, "1")
+    merge("X", 1, 0, "1")
     for b in range(4):
         c = 128 * b
         emit("v", [("eq", c, c + 128), ("es", c, c + 128)], [whole("et")],
@@ -311,6 +348,10 @@ def rank_program(g, core, T, topo):
     places(0)
     decide(1, "v")
     places(1)
+    affine("coli", "pf", -1024.0, 15360.0)
+    for a in (64, 128):
+        keep(a)
+    copy("s", T.MN[:, 0:H], ("MN", 0, H), T.wn[:], whole("wn"), 1.0, -1.0)
 
     for t in range(R):
         q = ("q%d" % t, "s%d" % t)
@@ -320,18 +361,24 @@ def rank_program(g, core, T, topo):
         if rank > 0:
             arrives(t)
 
+        def block(i):
+            c, h = H + 64 * i, int(64 * i >= SPLIT)
+            src, s = "U%s2" % "AB"[h], i - PARTS[h][0] // 64
+            old = T[src][:, D + s:D + PARTS[h][1] - PARTS[h][0]:count(h, 2)]
+            emit("v", [("MN", c, c + 64)], [("MN", 0, c), ("L3", 4 * i, 4 * i + 4), whole(src)],
+                 lambda e: e.tensor_tensor(T.MN[:, c:c + 64], T.MN[:, 0:c].indirect(T.L3[:, 4 * i:4 * i + 4]), old, Op.max))
+
         def head(step):
-            k, h, b = step[0], "AB".find(step[1]), step[2] if step[0] in "oU" else step[1]
-            if k == "U":
-                if b == "s":
-                    first("U", int(step[1]), "s", 0, 3)
-                elif b == "v":
-                    first("U", int(step[1]), "v", 3, 4)
-                else:
-                    merge("U", int(step[1]), int(b))
+            k, h, b = step[0], "AB".find(step[1]), step[2] if step[0] in "oraL" else step[1]
+            if k in "UX":
+                merge(k, h, int(step[2]), step[3])
                 return
             b = int(b)
-            if k == "o":
+            if k in "raL":
+                {"r": row, "a": sums, "L": listing}[k](h, b)
+            elif k == "m":
+                block(b)
+            elif k == "o":
                 a, e1 = PARTS[h]
                 bank = b if h else OWN[b]
                 product(bank, E, 128 * b, q, a, e1)
@@ -344,38 +391,8 @@ def rank_program(g, core, T, topo):
             elif k == "E":
                 product(b, E, 128 * b, q, SPLIT, C, True, False)
 
-        if t == 0:
-            for i in range(3):
-                if i > 0:
-                    first("X", i, "s", 0, 4)
-                    first("U", i, "s", 0, 4)
-                for s in range(1, 4):
-                    if (i, s) != (0, 1):
-                        merge("X", i, s)
-                    if s < 3 or i == 2:
-                        merge("U", i, s)
-                if i < 2:
-                    row(i)
-                    listing(i + 1, RUN // LEVELS[i], lambda: merge("U", i, 3))
-                if i > 0:
-                    for b in range(4):
-                        head("o" + " AB"[i] + str(b))
-            for s in range(7):
-                emit("v", [("exn", 64 * s, 64 * s + 64)], [("ki", 0, 64), ("X2", D, D + C)],
-                     lambda e: e.tensor_tensor_scan(T.exn[:, 64 * s:64 * s + 64], T.ki[:, 0:64], T.X2[:, D + s:D + C:7], 0.0, Op.add, Op.max))
-            emit("v", [whole("L3")], [whole("exn"), whole("coli")],
-                 lambda e: e.tensor_scalar(T.L3[:], T.exn[:, 15:C:16], T.coli[:, 0:1], -1.0, Op.subtract, Op.mult))
-            for k in "heE":
-                for b in range(4):
-                    head(k + str(b))
-        else:
-            for step in HEAD.split():
-                head(step)
-
-        def block(i):
-            c = H + 64 * i
-            emit("v", [("MN", c, c + 64)], [("MN", 0, c), ("L3", 4 * i, 4 * i + 4), ("U2", D, D + C)],
-                 lambda e: e.tensor_tensor(T.MN[:, c:c + 64], T.MN[:, 0:c].indirect(T.L3[:, 4 * i:4 * i + 4]), T.U2[:, D + i:D + C:7], Op.max))
+        for step in (HEAD if t else START).split():
+            head(step)
 
         def collect(a, b):
             emit("v", [("ex", a, b)], [("ki", 0, b - a), ("MN", H + a, H + b)],
@@ -387,8 +404,8 @@ def rank_program(g, core, T, topo):
 
         def gather(qn, b, h):
             a, e1 = PARTS[h]
-            out, src = T.z[:, 4 * a + b:4 * e1:4], T["F%d" % b][:, 0:H + C].indirect(T.lz[:, a // 16:e1 // 16])
-            outs, ins = [("z", 4 * a + b, 4 * a + b + 1)], [whole("F%d" % b), ("lz", a // 16, e1 // 16)]
+            out, src = T.z[:, 4 * a + b:4 * e1:4], T["F%d" % b][:, 0:H + e1].indirect(T.lz[:, a // 16:e1 // 16])
+            outs, ins = [("z", 4 * a + b, 4 * a + b + 1)], [("F%d" % b, 0, H + e1), ("lz", a // 16, e1 // 16)]
             if qn == "v":
                 emit("v", outs, ins, lambda e: e.tensor_copy(out, src))
             else:
@@ -405,6 +422,10 @@ def rank_program(g, core, T, topo):
             if k == "m":
                 block(int(step[1:]))
                 continue
+            if k == "U":
+                if not last:
+                    head(step)
+                continue
             if k == "c":
                 a, b = step[1:].split(":")
                 collect(64 * int(a), 64 * int(b))
@@ -414,6 +435,11 @@ def rank_program(g, core, T, topo):
                     quant("vq", "vs", "vt", 0, 128)
                 elif k == "x" and not last:
                     send(t + 1)
+                elif k == "x":
+                    copy("s", T.olt[:], whole("olt"), T.MN[:, H:H + C], ("MN", H, H + C), 1.0, -float(H))
+                    store("s", T.ol[:], T.olt[0:128:16, :], whole("olt"))
+                    for n in range(4):
+                        store("y", T.osc[4 * n:4 * n + 4, :], T[q[1]][32 * n:32 * n + 4, :], (q[1], 0, C))
                 continue
             h = "AB".index(step[1])
             a, b = PARTS[h]
@@ -437,16 +463,12 @@ def rank_program(g, core, T, topo):
             elif k == "d" and last:
                 c = 2048 + 512 * h
                 copy(step[2], T.yt[:, a:b], ("yt", a, b), T.ps[:, c:c + b - a], psum(4 + h), 1.0)
-                store("sy"[h], T.y[:, a:b], T.yt[:, a:b], ("yt", a, b))
+                store("s", T.y[:, a:b], T.yt[:, a:b], ("yt", a, b))
             elif k == "d":
                 decide(h, step[2])
             elif k == "p" and not last:
                 places(h)
 
-    copy("s", T.olt[:], whole("olt"), T.MN[:, H:H + C], ("MN", H, H + C), 1.0, -float(H))
-    store("s", T.ol[:], T.olt[0:128:16, :], whole("olt"))
-    for k in range(4):
-        store("y" if k < 2 else "s", T.osc[4 * k:4 * k + 4, :], T[q[1]][32 * k:32 * k + 4, :], (q[1], 0, C))
     for sem in SEMAPHORES:
         if total[sem]:
             g.wait_ge(T.sem[sem], total[sem])

@@ -5,13 +5,25 @@ C, H, R = 448, 256, 3
 LO = C - H
 SPLIT = 192
 PARTS = ((0, SPLIT), (SPLIT, C))
-START = ("XA02 XB02 UA01 XA03 XB03 UA02 rA1 XA1s UB01 rB1 XB1s aA1 UA03 aB1 LA1 UB02 LB1 UA1s XA11 UB03 XB11 UB1s oA0 oA1 oA2 oA3 "
-         "XA12 UA11 XB12 XA13 UB11 XB13 rA2 XA2s UA12 rB2 XB2s aA2 UB12 aB2 LA2 UA13 LB2 UA2s XA21 UB13 XB21 UB2s oB0 oB1 oB2 oB3 "
-         "XA22 UA21 XB22 XA23 UB21 XB23 rA3 UA22 rB3 LA3 UB22 LB3 UA23 h0 h1 h2 h3 m0 UB23 e0 e1 e2 e3 E0 E1 E2 E3 m1")
-HEAD = ("oA2 oB2 oA1 oA0 oA3 oB0 oB1 oB3 h0 h1 h2 h3 e1 e0 E0 E3 E1 E2 e2 e3 "
-        "UA03 UB01 UA10 UB02 UA11 UB03 UA12 UB10 UA13 UB11 UA20 UB12 UA21 UB13 UA22 UB20 UA23 UB21 m0 UB22 m1 UB23")
-ROUND = ("m2 m3 c0:3 m4 lA m5 gA3s gA1s gA2s gA0v m6 c3:6 c6:7 lB zA gB2v gB3s wA3 wA1 gB0s fA1s wA2 wA0 gB1v zB v "
-         "fA2s wB3 wB1 fB3v wB0 fA0s fA3s wB2 fB1s qA fB0v uA fB2v qB x dAs pA uB UA01 dBv UA02 pB")
+ORDER = (
+    "0D 0i0 0nA 0XA0s 0nB 0rA0 0i2 0aA0 0rB0 0qB 0aB0 0XB0s 0i1 0LA0 0uB 0qA 0uA 0LB0 0x 0dAs 0E-3 0dBs 0oA3 0OA3s 0XA01 0XB01 "
+    "0E-2 0XA02 0XB02 0oB2 0E-0 0OB2s 0XA03 0pA 0E-1 0pB 0oA2 0XB03 0rA1 0UA01 0rB1 0oB0 0OB0s 0oA1 0UB01 0UA02 0aA1 0XB1s 0aB1 "
+    "0UB02 0LA1 0OA1s 0XA1s 0OA2s 0LB1 0UA03 0XA11 0h-0 0XB11 0XA12 0UB03 0oA0 0XB12 0XA13 0UA1s 0UA11 0XB13 0rA2 0UB1s 0h-3 "
+    "0h-1 0rB2 0aA2 0UA12 0eB0 0UB11 0XA2s 0LA2 0UA13 0OA0s 0H-3s 0aB2 0XA21 0UB12 0H-1s 0UA2s 0LB2 0XA22 0eA3 0UA21 0XB2s "
+    "0UB13 0UB2s 0XA23 0h-2 0H-2s 0XB21 0UA22 0rA3 0UB21 0UA23 0LA3 0XB22 0oB3 0OB3s 0UB22 0m0 0XB23 0m1 0rB3 0m2 0UB23 0LB3 "
+    "0c03 0m3 0oB1 0OB1s 0eB1 0lA 0m4 0m5 0H-0s 0gA0s 0gA3v 0eA1 0gA1s 0gA2s 0m6 0c36 0eB2 0eA0 0c67 0lB 0eA2 0gB3s 0gB0s 0zA "
+    "0wA2 0wA3 0fA2s 0gB1v 0wA0 0eB3 0wA1 0gB2v 0zB 0fA0v 0fA1s 0wB3 0wB0 0fB3s 0wB2 0wB1 0fA3v 0fB2s 1qA 1uA 0fB0v 0fB1v "
+    "1qB 1dAs 1uB 1oA1 1oB2 1dBs 1oB0 1pA 1UA01 1UA02 1UA03 1UA1s 1oA2 1OB0s 1oB3 1pB 1UB01 1OA2s 1UA11 1UB02 1OB3s 1oB1 1oA0 "
+    "1oA3 1UA12 1UB03 1OA3s 1eB3 1UA13 1UB10 1UA20 1UB11 1UA21 1UB12 1UA22 1UB13 1OA1s 1OA0s 1UA23 1UB20 1m0 1x 1h-3 1OB1s "
+    "1h-2 1UB21 1h-0 1m1 1UB22 1h-1 1OB2s 1m2 1UB23 1c03 1m3 1lA 1H-3s 1H-2s 1m4 1gA3v 1eA2 1m5 1m6 1H-1s 1H-0s 1c36 1c67 "
+    "1gA2s 1lB 1gA0s 1eB0 1gA1s 1zA 1eA0 1eA3 1wA3 1eB2 1eB1 1gB2v 1gB1v 1wA2 1fA3v 1gB3s 1wA0 1eA1 1gB0s 1zB 1wA1 1fA0v "
+    "1fA1v 1fA2s 2qA 1wB0 1fB0s 1wB2 1wB3 1fB2v 1fB3s 1wB1 2uA 2dAs 2oA0 1fB1v "
+    "2qB 2pA 2UA01 2UA02 2uB 2dBs 2oB0 2UA03 2oB1 2OB0s 2pB 2UB01 2UA1s 2UA11 2UB02 2UA12 2x 2UB03 2UA13 2UB10 2oB3 2UA20 "
+    "2oA3 2OA3s 2oA2 2UB11 2oA1 2oB2 2UA21 2OB2s 2OA2s 2UB12 2UA22 2UB13 2OA1s 2UA23 2m0 2eB2 2OA0s 2h-2 2UB2s 2UB21 2h-3 "
+    "2m1 2UB22 2OB1s 2H-2s 2h-0 2h-1 2H-0s 2m2 2H-1s 2UB23 2c03 2m3 2eA1 2lA 2H-3s 2m4 2gA1s 2eB1 2gA3s 2gA0v 2m5 2m6 2c36 "
+    "2c67 2eA2 3v 2gA2s 2eB0 2OB3s 2eB3 2eA3 2lB 2gB0s 2eA0 2gB3s 2zA 2gB1v 2wA1 2gB2v 2R 2zB 2wA0 2wA3 2fA3s 2wA2 2fA2s "
+    "2fA0s 2wB1 2fB1v 2wB3 2fB3v 2wB2 2wB0 2fB0v 2fA1s 3qA 2fB2s 3qB 3S-3s 3uA 3yAv 3CAy 3S-2s 3S-0s 3T-y 3uB 3YAy 3CBy "
+    "3yBv 3YBy 3S-1s")
 OWN = (6, 7, 4, 5)
 LEVELS = (4, 16, 64)
 D, GAP = 16, 64
@@ -158,9 +170,9 @@ def rank_program(g, core, T, topo):
              lambda e: e.matmul_mx(T.ps[:, 512 * bank:512 * bank + n], T[st[0]][:, c0:c0 + 128], T[st[1]][:, c0:c0 + 128],
                                    T[mv[0]][:, a:b], T[mv[1]][:, a:b], start, stop))
 
-    def unpack(b, c, d, bank):
+    def unpack(qn, b, c, d, bank):
         n = d - c
-        copy("s", T["F%d" % b][:, c:d], ("F%d" % b, c, d), T.ps[:, 512 * bank:512 * bank + n], psum(bank), 2.0 ** -6)
+        copy(qn, T["F%d" % b][:, c:d], ("F%d" % b, c, d), T.ps[:, 512 * bank:512 * bank + n], psum(bank), 2.0 ** -6)
 
     def iota(name, pattern, base, mult):
         if SCRATCH[name][2] == I32:
@@ -215,8 +227,10 @@ def rank_program(g, core, T, topo):
             small("cc" + n, "td" + n, "colm", None, Op.add)
         else:
             small("ti" + n, "nn", -(k - 1) / 2.0, 1.0 / k, Op.add, Op.mult)
-    nothing("XA0", -30000.0)
-    nothing("XB0", -30000.0)
+    for i in range(3):
+        for p in "AB":
+            nothing("X%s%d" % (p, i), -30000.0)
+            nothing("U%s%d" % (p, i), -1.0)
     copy("s", T.exsA[:, GAP - 1:3 * GAP:GAP], whole("exsA"), T.c1[:, 0:3], whole("c1"), 0.0)
     keep(0)
     copy("s", T.pn[:, 0:H], ("pn", 0, H), T.wn[:], whole("wn"), 1.0, H - 1.0)
@@ -228,6 +242,10 @@ def rank_program(g, core, T, topo):
     for h, i in pairs[2:]:
         n = "AB"[h] + str(i)
         both("cc" + n, "td" + n, "tb" + n, Op.add)
+    affine("coli", "pf", -1024.0, 15360.0)
+    for a in (64, 128):
+        keep(a)
+    copy("s", T.MN[:, 0:H], ("MN", 0, H), T.wn[:], whole("wn"), 1.0, -1.0)
 
     def send(t):
         if rank + 1 == n_ranks:
@@ -239,10 +257,10 @@ def rank_program(g, core, T, topo):
             g.remote_dma(out, in_, T.sem["arr%d" % t], T.sem.sent, pid, rid, topo.mask(core, dst))
             total["sent"] += len(topo.engines(core, dst))
 
-    def arrives(t):
-        n = len(topo.engines(T.cores[rank - 1], core))
-        for name in ("hq%d" % t, "hs%d" % t):
-            log[name] = [(0, H, True, "far", ("arr%d" % t, 2 * n, {}))]
+    if rank > 0:
+        for t in range(R):
+            for name in ("hq%d" % t, "hs%d" % t):
+                log[name] = [(0, H, True, "far", ("arr%d" % t, 2 * len(topo.engines(T.cores[rank - 1], core)), {}))]
 
     def before(kind, h, i, s):
         a, b = PARTS[h]
@@ -311,163 +329,115 @@ def rank_program(g, core, T, topo):
             emit("v", [(dst, c, c + run)], [("ff", a, b), ("pn", a, b)],
                  lambda e: e.tensor_tensor_scan(T[dst][:, c:c + run], T.pn[:, a + s:b:4], T.ff[:, a + s:b:4], 0.0, Op.max, Op.mult))
 
-    small("du", "dl", -1.0, None, Op.add)
-    for a, b in PARTS:
-        emit("v", [("xn", a, b)], [whole("wn"), whole("du"), ("pn", a, b)],
-             lambda e: e.tensor_tensor(T.xn[:, a:b], T.wn[:].indirect(T.du[:, a // 16:b // 16]), T.pn[:, a:b], Op.subtract))
-    row(0, 0)
-    merge("X", 0, 0, "s")
-    row(1, 0)
-    merge("X", 1, 0, "s")
-    sums(0, 0)
-    quant("ua", "uas", "ut", 0, 128)
-    emit("s", [whole("us")], [whole("uas"), whole("lu")], lambda e: e.activation(T.us[:], T.uas[:].indirect(T.lu[:]), Act.Copy))
-    quant("q0", "s0", "xt", 0, SPLIT)
-    sums(1, 0)
-    listing(0, 0)
-    nothing("UA0", -1.0)
-    nothing("UB0", -1.0)
-    emit("v", [whole("uq")], [whole("ua"), whole("lu")],
-         lambda e: e.tensor_copy(T.uq[:].bitcast(dt.uint32), T.ua[:].bitcast(dt.uint32).indirect(T.lu[:])))
-    listing(1, 0)
-    product(4, U, 0, ("q0", "s0"), 0, SPLIT)
-    decide(0, "s")
-    quant("q0", "s0", "xt", SPLIT, C)
-    send(0)
-    product(5, U, 0, ("q0", "s0"), SPLIT, C)
-    for i in (1, 2):
-        for p in "AB":
-            nothing("X%s%d" % (p, i), -30000.0)
-            nothing("U%s%d" % (p, i), -1.0)
-    merge("X", 0, 0, "1")
-    merge("X", 1, 0, "1")
-    for b in range(4):
-        c = 128 * b
-        emit("v", [("eq", c, c + 128), ("es", c, c + 128)], [whole("et")],
-             lambda e: e.quantize_mx(T.eq[:, c:c + 128], T.es[:, c:c + 128], T.et[:, 3 - b:515 - b]))
-    places(0)
-    decide(1, "v")
-    places(1)
-    affine("coli", "pf", -1024.0, 15360.0)
-    for a in (64, 128):
-        keep(a)
-    copy("s", T.MN[:, 0:H], ("MN", 0, H), T.wn[:], whole("wn"), 1.0, -1.0)
+    def block(i):
+        c, h = H + 64 * i, int(64 * i >= SPLIT)
+        src, s = "U%s2" % "AB"[h], i - PARTS[h][0] // 64
+        old = T[src][:, D + s:D + PARTS[h][1] - PARTS[h][0]:count(h, 2)]
+        emit("v", [("MN", c, c + 64)], [("MN", 0, c), ("L3", 4 * i, 4 * i + 4), whole(src)],
+             lambda e: e.tensor_tensor(T.MN[:, c:c + 64], T.MN[:, 0:c].indirect(T.L3[:, 4 * i:4 * i + 4]), old, Op.max))
 
-    for t in range(R):
+    def collect(a, b):
+        emit("v", [("ex", a, b)], [("ki", 0, b - a), ("MN", H + a, H + b)],
+             lambda e: e.tensor_tensor_scan(T.ex[:, a:b], T.ki[:, 0:b - a], T.MN[:, H + a:H + b], 0.0, Op.add, Op.max))
+
+    def listed(a, b):
+        emit("v", [("lz", a // 16, b // 16)], [("ex", a, b), whole("coli")],
+             lambda e: e.tensor_scalar(T.lz[:, a // 16:b // 16], T.ex[:, a + 15:b:16], T.coli[:, 0:1], None, Op.subtract))
+
+    def gather(qn, b, h):
+        a, e1 = PARTS[h]
+        out, src = T.z[:, 4 * a + b:4 * e1:4], T["F%d" % b][:, 0:H + e1].indirect(T.lz[:, a // 16:e1 // 16])
+        outs, ins = [("z", 4 * a + b, 4 * a + b + 1)], [("F%d" % b, 0, H + e1), ("lz", a // 16, e1 // 16)]
+        if qn == "v":
+            emit("v", outs, ins, lambda e: e.tensor_copy(out, src))
+        else:
+            emit("s", outs, ins, lambda e: e.activation(out, src, Act.Copy))
+
+    def finish(qn, new, h, b):
+        a, e1 = PARTS[h]
+        bank = 4 - 4 * h + b
+        copy(qn, T[new][:, 4 * a + b:4 * e1:4], (new, 4 * a + b, 4 * a + b + 1), T.ps[:, 512 * bank:512 * bank + e1 - a], psum(bank), 2.0 ** -6)
+
+    def step(word):
+        t, name = int(word[0]), word[1:]
         q = ("q%d" % t, "s%d" % t)
-        land = ("hq%d" % t, "hs%d" % t)
-        new = "t%d" % (t + 1)
-        last = t + 1 == R
-        if rank > 0:
-            arrives(t)
+        k, h = name[0], "AB".find(name[1:2])
+        a, b = PARTS[h]
+        n = int(name[2]) if name[2:3].isdigit() else None
+        if k in "UX":
+            merge(k, h, n, name[3])
+        elif k in "raL":
+            {"r": row, "a": sums, "L": listing}[k](h, n)
+        elif k == "m":
+            block(int(name[1]))
+        elif k == "c":
+            collect(64 * int(name[1]), 64 * n)
+        elif k == "l":
+            listed(a, b)
+        elif k == "o":
+            product(n if h else OWN[n], E, 128 * n, q, a, b)
+        elif k == "O":
+            unpack(name[3], n, H + a, H + b, n if h else OWN[n])
+        elif k == "h":
+            if rank > 0:
+                product(4 + n, E, 128 * n, ("hq%d" % t, "hs%d" % t), 0, H)
+        elif k == "H":
+            if rank > 0:
+                unpack(name[3], n, 0, H, 4 + n)
+        elif k == "e":
+            product(4 - 4 * h + n, E, 128 * n, q, a, b, True, False)
+        elif k == "g":
+            gather(name[3], n, h)
+        elif k == "z":
+            quant("zq", "zs", "z", a, b)
+        elif k == "w":
+            product(4 - 4 * h + n, W, 128 * n, ("zq", "zs"), a, b, False, True)
+        elif k == "f":
+            finish(name[3], "t%d" % (t + 1), h, n)
+        elif k == "q":
+            quant(q[0], q[1], "t%d" % t if t else "xt", a, b)
+        elif k == "x":
+            send(t)
+        elif k == "u":
+            product(4 + h, V if t == R else U, 0, q, a, b)
+        elif k == "d":
+            decide(h, name[2])
+        elif k == "p":
+            places(h)
+        elif k == "y":
+            c = 2048 + 512 * h
+            copy(name[2], T.yt[:, a:b], ("yt", a, b), T.ps[:, c:c + b - a], psum(4 + h), 1.0)
+        elif k == "Y":
+            store(name[2], T.y[:, a:b], T.yt[:, a:b], ("yt", a, b))
+        elif k == "C":
+            store(name[2], T.oc[:, 4 * a:4 * b], T[q[0]][:, a:b].bitcast(dt.uint8), (q[0], a, b))
+        elif k == "S":
+            store(name[3], T.osc[4 * n:4 * n + 4, :], T[q[1]][32 * n:32 * n + 4, :], (q[1], 0, C))
+        elif k == "R":
+            copy("s", T.olt[:], whole("olt"), T.MN[:, H:H + C], ("MN", H, H + C), 1.0, -float(H))
+        elif k == "T":
+            store(name[2], T.ol[:], T.olt[0:128:16, :], whole("olt"))
+        elif k == "v":
+            quant("vq", "vs", "vt", 0, 128)
+        elif k == "D":
+            small("du", "dl", -1.0, None, Op.add)
+        elif k == "n":
+            emit("v", [("xn", a, b)], [whole("wn"), whole("du"), ("pn", a, b)],
+                 lambda e: e.tensor_tensor(T.xn[:, a:b], T.wn[:].indirect(T.du[:, a // 16:b // 16]), T.pn[:, a:b], Op.subtract))
+        elif name == "i0":
+            quant("ua", "uas", "ut", 0, 128)
+        elif name == "i1":
+            emit("s", [whole("us")], [whole("uas"), whole("lu")], lambda e: e.activation(T.us[:], T.uas[:].indirect(T.lu[:]), Act.Copy))
+        elif name == "i2":
+            emit("v", [whole("uq")], [whole("ua"), whole("lu")],
+                 lambda e: e.tensor_copy(T.uq[:].bitcast(dt.uint32), T.ua[:].bitcast(dt.uint32).indirect(T.lu[:])))
+        elif k == "E":
+            c = 128 * n
+            emit("v", [("eq", c, c + 128), ("es", c, c + 128)], [whole("et")],
+                 lambda e: e.quantize_mx(T.eq[:, c:c + 128], T.es[:, c:c + 128], T.et[:, 3 - n:515 - n]))
 
-        def block(i):
-            c, h = H + 64 * i, int(64 * i >= SPLIT)
-            src, s = "U%s2" % "AB"[h], i - PARTS[h][0] // 64
-            old = T[src][:, D + s:D + PARTS[h][1] - PARTS[h][0]:count(h, 2)]
-            emit("v", [("MN", c, c + 64)], [("MN", 0, c), ("L3", 4 * i, 4 * i + 4), whole(src)],
-                 lambda e: e.tensor_tensor(T.MN[:, c:c + 64], T.MN[:, 0:c].indirect(T.L3[:, 4 * i:4 * i + 4]), old, Op.max))
-
-        def head(step):
-            k, h, b = step[0], "AB".find(step[1]), step[2] if step[0] in "oraL" else step[1]
-            if k in "UX":
-                merge(k, h, int(step[2]), step[3])
-                return
-            b = int(b)
-            if k in "raL":
-                {"r": row, "a": sums, "L": listing}[k](h, b)
-            elif k == "m":
-                block(b)
-            elif k == "o":
-                a, e1 = PARTS[h]
-                bank = b if h else OWN[b]
-                product(bank, E, 128 * b, q, a, e1)
-                unpack(b, H + a, H + e1, bank)
-            elif k == "h" and rank > 0:
-                product(4 + b, E, 128 * b, land, 0, H)
-                unpack(b, 0, H, 4 + b)
-            elif k == "e":
-                product(4 + b, E, 128 * b, q, 0, SPLIT, True, False)
-            elif k == "E":
-                product(b, E, 128 * b, q, SPLIT, C, True, False)
-
-        for step in (HEAD if t else START).split():
-            head(step)
-
-        def collect(a, b):
-            emit("v", [("ex", a, b)], [("ki", 0, b - a), ("MN", H + a, H + b)],
-                 lambda e: e.tensor_tensor_scan(T.ex[:, a:b], T.ki[:, 0:b - a], T.MN[:, H + a:H + b], 0.0, Op.add, Op.max))
-
-        def listed(a, b):
-            emit("v", [("lz", a // 16, b // 16)], [("ex", a, b), whole("coli")],
-                 lambda e: e.tensor_scalar(T.lz[:, a // 16:b // 16], T.ex[:, a + 15:b:16], T.coli[:, 0:1], None, Op.subtract))
-
-        def gather(qn, b, h):
-            a, e1 = PARTS[h]
-            out, src = T.z[:, 4 * a + b:4 * e1:4], T["F%d" % b][:, 0:H + e1].indirect(T.lz[:, a // 16:e1 // 16])
-            outs, ins = [("z", 4 * a + b, 4 * a + b + 1)], [("F%d" % b, 0, H + e1), ("lz", a // 16, e1 // 16)]
-            if qn == "v":
-                emit("v", outs, ins, lambda e: e.tensor_copy(out, src))
-            else:
-                emit("s", outs, ins, lambda e: e.activation(out, src, Act.Copy))
-
-        def finish(qn, h, b):
-            a, e1 = PARTS[h]
-            bank = 4 - 4 * h + b
-            copy(qn, T[new][:, 4 * a + b:4 * e1:4], (new, 4 * a + b, 4 * a + b + 1), T.ps[:, 512 * bank:512 * bank + e1 - a], psum(bank), 2.0 ** -6)
-
-        q = ("q%d" % (t + 1), "s%d" % (t + 1))
-        for step in ROUND.split():
-            k = step[0]
-            if k == "m":
-                block(int(step[1:]))
-                continue
-            if k == "U":
-                if not last:
-                    head(step)
-                continue
-            if k == "c":
-                a, b = step[1:].split(":")
-                collect(64 * int(a), 64 * int(b))
-                continue
-            if k == "x" or k == "v":
-                if k == "v" and last:
-                    quant("vq", "vs", "vt", 0, 128)
-                elif k == "x" and not last:
-                    send(t + 1)
-                elif k == "x":
-                    copy("s", T.olt[:], whole("olt"), T.MN[:, H:H + C], ("MN", H, H + C), 1.0, -float(H))
-                    store("s", T.ol[:], T.olt[0:128:16, :], whole("olt"))
-                    for n in range(4):
-                        store("y", T.osc[4 * n:4 * n + 4, :], T[q[1]][32 * n:32 * n + 4, :], (q[1], 0, C))
-                continue
-            h = "AB".index(step[1])
-            a, b = PARTS[h]
-            if k == "l":
-                listed(a, b)
-            elif k == "g":
-                gather(step[3], int(step[2]), h)
-            elif k == "z":
-                quant("zq", "zs", "z", a, b)
-            elif k == "w":
-                n = int(step[2])
-                product(4 - 4 * h + n, W, 128 * n, ("zq", "zs"), a, b, False, True)
-            elif k == "f":
-                finish(step[3], h, int(step[2]))
-            elif k == "q":
-                quant(q[0], q[1], new, a, b)
-                if last:
-                    store("y", T.oc[:, 4 * a:4 * b], T[q[0]][:, a:b].bitcast(dt.uint8), (q[0], a, b))
-            elif k == "u":
-                product(4 + h, V if last else U, 0, q, a, b)
-            elif k == "d" and last:
-                c = 2048 + 512 * h
-                copy(step[2], T.yt[:, a:b], ("yt", a, b), T.ps[:, c:c + b - a], psum(4 + h), 1.0)
-                store("s", T.y[:, a:b], T.yt[:, a:b], ("yt", a, b))
-            elif k == "d":
-                decide(h, step[2])
-            elif k == "p" and not last:
-                places(h)
+    for word in ORDER.split():
+        step(word)
 
     for sem in SEMAPHORES:
         if total[sem]:

@@ -5,31 +5,25 @@ C, H, R = 448, 256, 3
 LO = C - H
 SPLIT = 192
 PARTS = ((0, SPLIT), (SPLIT, C))
+SPANS = (2, 2)
+PIECES = 2
+NB = C // 16
+EPS, BIG, HOLD = 2.0 ** -11, 2.0 ** 64, 2048.0
 ORDER = (
-    "0D 0i0 0nA 0XA0s 0nB 0rA0 0i2 0aA0 0rB0 0qB 0aB0 0XB0s 0i1 0LA0 0uB 0qA 0uA 0LB0 0x 0dAs 0E-3 0dBs 0oA3 0OA3s 0XA01 0XB01 "
-    "0E-2 0XA02 0XB02 0oB2 0E-0 0OB2s 0XA03 0pA 0E-1 0pB 0oA2 0XB03 0rA1 0UA01 0rB1 0oB0 0OB0s 0oA1 0UB01 0UA02 0aA1 0XB1s 0aB1 "
-    "0UB02 0LA1 0OA1s 0XA1s 0OA2s 0LB1 0UA03 0XA11 0h-0 0XB11 0XA12 0UB03 0oA0 0XB12 0XA13 0UA1s 0UA11 0XB13 0rA2 0UB1s 0h-3 "
-    "0h-1 0rB2 0aA2 0UA12 0eB0 0UB11 0XA2s 0LA2 0UA13 0OA0s 0H-3s 0aB2 0XA21 0UB12 0H-1s 0UA2s 0LB2 0XA22 0eA3 0UA21 0XB2s "
-    "0UB13 0UB2s 0XA23 0h-2 0H-2s 0XB21 0UA22 0rA3 0UB21 0UA23 0LA3 0XB22 0oB3 0OB3s 0UB22 0m0 0XB23 0m1 0rB3 0m2 0UB23 0LB3 "
-    "0c03 0m3 0oB1 0OB1s 0eB1 0lA 0m4 0m5 0H-0s 0gA0s 0gA3v 0eA1 0gA1s 0gA2s 0m6 0c36 0eB2 0eA0 0c67 0lB 0eA2 0gB3s 0gB0s 0zA "
-    "0wA2 0wA3 0fA2s 0gB1v 0wA0 0eB3 0wA1 0gB2v 0zB 0fA0v 0fA1s 0wB3 0wB0 0fB3s 0wB2 0wB1 0fA3v 0fB2s 1qA 1uA 0fB0v 0fB1v "
-    "1qB 1dAs 1uB 1oA1 1oB2 1dBs 1oB0 1pA 1UA01 1UA02 1UA03 1UA1s 1oA2 1OB0s 1oB3 1pB 1UB01 1OA2s 1UA11 1UB02 1OB3s 1oB1 1oA0 "
-    "1oA3 1UA12 1UB03 1OA3s 1eB3 1UA13 1UB10 1UA20 1UB11 1UA21 1UB12 1UA22 1UB13 1OA1s 1OA0s 1UA23 1UB20 1m0 1x 1h-3 1OB1s "
-    "1h-2 1UB21 1h-0 1m1 1UB22 1h-1 1OB2s 1m2 1UB23 1c03 1m3 1lA 1H-3s 1H-2s 1m4 1gA3v 1eA2 1m5 1m6 1H-1s 1H-0s 1c36 1c67 "
-    "1gA2s 1lB 1gA0s 1eB0 1gA1s 1zA 1eA0 1eA3 1wA3 1eB2 1eB1 1gB2v 1gB1v 1wA2 1fA3v 1gB3s 1wA0 1eA1 1gB0s 1zB 1wA1 1fA0v "
-    "1fA1v 1fA2s 2qA 1wB0 1fB0s 1wB2 1wB3 1fB2v 1fB3s 1wB1 2uA 2dAs 2oA0 1fB1v "
-    "2qB 2pA 2UA01 2UA02 2uB 2dBs 2oB0 2UA03 2oB1 2OB0s 2pB 2UB01 2UA1s 2UA11 2UB02 2UA12 2x 2UB03 2UA13 2UB10 2oB3 2UA20 "
-    "2oA3 2OA3s 2oA2 2UB11 2oA1 2oB2 2UA21 2OB2s 2OA2s 2UB12 2UA22 2UB13 2OA1s 2UA23 2m0 2eB2 2OA0s 2h-2 2UB2s 2UB21 2h-3 "
-    "2m1 2UB22 2OB1s 2H-2s 2h-0 2h-1 2H-0s 2m2 2H-1s 2UB23 2c03 2m3 2eA1 2lA 2H-3s 2m4 2gA1s 2eB1 2gA3s 2gA0v 2m5 2m6 2c36 "
-    "2c67 2eA2 3v 2gA2s 2eB0 2OB3s 2eB3 2eA3 2lB 2gB0s 2eA0 2gB3s 2zA 2gB1v 2wA1 2gB2v 2R 2zB 2wA0 2wA3 2fA3s 2wA2 2fA2s "
-    "2fA0s 2wB1 2fB1v 2wB3 2fB3v 2wB2 2wB0 2fB0v 2fA1s 3qA 2fB2s 3qB 3S-3s 3uA 3yAv 3CAy 3S-2s 3S-0s 3T-y 3uB 3YAy 3CBy "
-    "3yBv 3YBy 3S-1s")
-OWN = (6, 7, 4, 5)
-LEVELS = (4, 16, 64)
-D, GAP = 16, 64
+    "-c1 -pa -tabi -two -one -tab0 -kb -dl -taB -xB -ut -pm -sd -pf -pd -tab1 -ul -xA -zcA -pg -top -k16 -pw0 -k16a 0D -tbB 0n0s -ca -p4 -pw1 -raA 0n1v 0C9s -cb 0C5s -et -wn 0Wa -p4f 0C11s 0qB 0C7s 0j10 0a14s -rbB 0j12 0j6 -litB 0Wb 0J10 0J12 0C1s 0j8 0Wc -k16w192 -lu 0j2 0C13s -vt 0E0 0Wd 0x 0C3s 0J8 -id512 0K12s 0i0 0We 0j4 0J2 -zaA 0F12 0a13s 0K2s 0B12 0i2 0K10s 0w12 0qA 0B10 -sdA 0F10 -raB -k16w128 0J6 0E3 -nil -sdB -ka 0w10 0a12s 0E2 -sbB 0K8s 0i1 0F8 0a10s 0B8 -saB 0b10 0K6s -farA0 -taA 0J4 0o2 0w8 0E1 0C0s -c16 0F6 0B6 -rbA 0uB 0a8s -k4 -jbB -id0 0K4s 0a6s 0M10 0w6 0b12 0b8 -pb -farB0 -tbA 0F4 -wq 0B4 0h3 0b6 0o3 0a4s 0M8 0b4 0w4 0O2s -saA 0M6 -k4a -ap -farB4 0uA 0o1 0a2s 0a9s 0M12 0F2 -rcA 0B2 0a5s 0M4 0a7s 0b2 -c4 -farA10 0w2 0a11s 0M2 0Wf 0a3s 0a0s -jaA 0a1s -tA -tB 0Wg 0dB 0H3s 0dA 0Wh 0sB 0Wi 0O1s 0sA 0O3s 0tB -k16w64 -litA -wp -jaB -sbA 0h1 0eB2 0tA 0o0 0LB 0O0s 0LA 0GB0v 0GA0v 0GB1v 0GA1v 0GB2v -k4w192 0GA2v 0GB3v 0h0 0eB3 0GA3v 0eA3 0H1s -k4w64 -jbA 0eA1 0GA4v -rcB 0GB4s -k4w128 0H0s 0eB0 0GB5v 0h2 0GA5v 0GB6v 0H2s 0eA0 0GB7s 0cA 0lA 0cB 0gA01s 0eA2 0gA00v 0lB 0gA10s 0gA11v -scA 0gB00v 0gB01s 0gB11s 0zA 0mA3 0gB10v 0mA1 0fA1s 0fA3s 0mA2 0mA0 0eB1 0fA2s 0zB 0mB2 0mB0 0fA0v 0fB0s -scB 0mB3 "
+    "1qA 0mB1 1uA 0fB2v 0fB1v 0fB3s 1dA 1qB 1sA 1uB 1o2 1tA 1dB 1LA 1x 1o0 1sB 1o1 1GA0s 1GA1s 1tB 1LB 1o3 1GA2v 1GB0v -jcB 1O0s 1h2 1h0 1GA3v 1GB1v 1O3v 1O2s 1h3 1GA4s 1GB2s 1GA5v 1O1s 1h1 1GB3v 1cA 1GB4s 1H0s 1H2v 1GB5v 1H3s 1lA 1eA2 1H1v 1eB1 1eA1 1gA00v 1GB6s 1eB3 1eB0 1GB7s 1cB 1gA01s -id256 1gA10s 1gA11v 1eA3 1lB -jcA 1eA0 1gB00s 1gB01v 1eB2 1zA 1mA1 1gB11v 1gB10s 1mA2 1mA3 1zB 1fA2s 1fA1v 1fA3s 1mA0 1fA0v 1mB3 2v 1mB2 1mB1 1mB0 "
+    "2qA 2uA 1fB3s 1fB2v 1fB0s 1fB1v 2dA 2qB 2uB 2o1 2o0 2sA 2dB 2tA 2x 2sB 2o3 2o2 2h0 2O1s 2LA 2tB 2GA0v 2h1 2LB 2GA1v 2O3s 2GB0v 2O0s 2GA2v 2GB1v 2GA3v 2O2v 2GB2s 2GA4s 2h2 2GB3s 2h3 2GB4s 2GA5v 2H0v 2eA0 2cA 2GB5v 2GB6v 2H1s 2H2s 2H3s 2lA 2eA3 2rA 2GB7s 2gA00s 2eA2 2gA01v 2gA10s 2eA1 2cB 2eB0 2gA11v 2lB 2gB01s 2eB3 2eB2 2eB1 2gB00v 2zA 2mA2 2gB11v 2mA0 2gB10s 2RA 2zB 2mA1 2rB 2fA1v 2RB 2mA3 2pA0s 2fA2s 2fA0s 2pA1s 2mB2 2fA3s 2fB2v 2mB3 2mB1 2fB3v 2mB0 2fB1v 2fB0s "
+    "3qA 3uA 3CAy 3qB 2pB0s 3yAs 3CBy 3S2s 3YAy 3S0s 3S1s 3uB 2pB1v 3S3s 3yBv 2Ty 3YBy")
+
+
+def shape(h):
+    a, b = PARTS[h]
+    n, k = b - a, SPANS[h]
+    return a, b, n, k, n // 16 // k, n // k, k + k % 2, n + 2 * H
+
 
 SCRATCH = {
-    "z": ("sbuf", [128, 4 * C], B16), "xt": ("sbuf", [128, 4 * C], B16),
+    "fz": ("sbuf", [128, 4 * (H + 2 * C)], B16), "xt": ("sbuf", [128, 4 * C], B16),
     "zq": ("sbuf", [128, C], X4), "zs": ("sbuf", [128, C], U8),
     "wq": ("sbuf", [128, 512], X4), "wp": ("sbuf", [128, 512], U8),
     "ut": ("sbuf", [128, 512], B16), "vt": ("sbuf", [128, 512], B16),
@@ -37,39 +31,43 @@ SCRATCH = {
     "uq": ("sbuf", [128, 128], X4), "us": ("sbuf", [128, 128], U8),
     "vq": ("sbuf", [128, 128], X4), "vs": ("sbuf", [128, 128], U8),
     "one": ("sbuf", [128, 516], B16), "et": ("sbuf", [128, 516], B16), "eq": ("sbuf", [128, 512], X4), "es": ("sbuf", [128, 512], U8),
-    "MN": ("sbuf", [128, H + C], F32), "ff": ("sbuf", [128, C], F32),
-    "ex": ("sbuf", [128, C], F32), "exn": ("sbuf", [128, C], F32),
-    "ki": ("sbuf", [128, H], F32), "kt": ("sbuf", [128, 64], I32), "kb": ("sbuf", [128, 64], I32), "kd": ("sbuf", [128, 64], F32),
-    "pn": ("sbuf", [128, C], F32), "wn": ("sbuf", [128, H], F32), "xn": ("sbuf", [128, C], F32),
-    "dl": ("sbuf", [128, 28], I32), "du": ("sbuf", [128, 28], U16),
+    "c1": ("sbuf", [128, H], F32), "two": ("sbuf", [128, 16], F32), "wn": ("sbuf", [128, H], F32),
+    "tab": ("sbuf", [128, H + 16], F32), "tab0": ("sbuf", [128, H], F32),
+    "pe": ("sbuf", [128, 7 * 64], F32), "pd": ("sbuf", [128, 2 * NB], F32),
+    "k4": ("sbuf", [128, H], F32), "k16": ("sbuf", [128, H], F32), "ka": ("sbuf", [128, 64], F32), "kb": ("sbuf", [128, 64], F32),
+    "dl": ("sbuf", [128, NB], I32), "du": ("sbuf", [128, NB], U16),
     "pa": ("sbuf", [128, 2], I32), "pm": ("sbuf", [128, 2], I32), "pf": ("sbuf", [128, 2], F32),
-    "c1": ("sbuf", [128, 16], F32), "gn": ("sbuf", [128, 12], F32), "nn": ("sbuf", [128, 12], F32),
+    "p4": ("sbuf", [128, 2], I32), "p4f": ("sbuf", [128, 2], F32), "pb": ("sbuf", [128, 2], F32),
+    "top": ("sbuf", [128, 2], F32), "ca": ("sbuf", [128, 2], F32), "cb": ("sbuf", [128, 16], F32), "c4": ("sbuf", [128, 2], F32),
+    "c16": ("sbuf", [128, 2], F32), "pg": ("sbuf", [128, 2], F32), "pw": ("sbuf", [128, 16], F32),
     "ul": ("sbuf", [128, 8], I32), "lu": ("sbuf", [128, 8], U16),
-    "coli": ("sbuf", [128, 2], F32), "colm": ("sbuf", [128, 2], F32),
-    "lz": ("sbuf", [128, 28], U16), "L3": ("sbuf", [128, 28], U16),
-    "yt": ("sbuf", [128, C], F32), "olt": ("sbuf", [128, C], F32),
+    "l4": ("sbuf", [128, C // 4], U16), "l16": ("sbuf", [128, 32], U16),
+    "roots": ("sbuf", [128, H + 2 * C], F32),
     "ps": ("psum", [128, 4096], F32),
 }
-for _p, (_a, _b) in zip("AB", PARTS):
-    SCRATCH["exs" + _p] = ("sbuf", [128, 3 * GAP], F32)
-    for _i in range(3):
-        SCRATCH["U%s%d" % (_p, _i)] = ("sbuf", [128, D + _b - _a], F32)
-        SCRATCH["X%s%d" % (_p, _i)] = ("sbuf", [128, D + _b - _a], F32)
-        SCRATCH["L%s%d" % (_p, _i)] = ("sbuf", [128, 12], U16)
-        for _n in ("ra", "tb", "td", "cc"):
-            SCRATCH["%s%s%d" % (_n, _p, _i)] = ("sbuf", [128, 12], F32)
-        SCRATCH["ti%s%d" % (_p, _i)] = ("sbuf", [128, 12], I32)
+for _n in ("par", "cr", "at", "ap", "yr", "pr", "kr", "fr", "hit", "sd", "sc", "ex", "yt"):
+    SCRATCH[_n] = ("sbuf", [128, C], F32)
+for _n in ("ta", "tb", "xa", "xb", "xc", "out"):
+    SCRATCH[_n] = ("sbuf", [128, NB], F32)
+for _h, _p in enumerate("AB"):
+    _s = shape(_h)
+    SCRATCH["way" + _p] = ("sbuf", [128, _s[7] + _s[2]], F32)
+    SCRATCH["t" + _p] = ("sbuf", [128, 16], F32)
+    SCRATCH["L" + _p] = ("sbuf", [128, 16], U16)
+    for _n, _k in (("a", 2), ("b", 4), ("c", 2)):
+        SCRATCH["j%s%s" % (_n, _p)] = ("sbuf", [128, _k], U16)
+        SCRATCH["r%s%s" % (_n, _p)] = ("sbuf", [128, 16 * _k], F32)
+        SCRATCH["s%s%s" % (_n, _p)] = ("sbuf", [128, 16 * _k], F32)
 for _i in range(3):
     SCRATCH["hq%d" % _i] = ("sbuf", [128, H], X4)
     SCRATCH["hs%d" % _i] = ("sbuf", [128, H], U8)
 for _i in range(4):
-    SCRATCH["F%d" % _i] = ("sbuf", [128, H + C], B16)
     SCRATCH["q%d" % _i] = ("sbuf", [128, C], X4)
     SCRATCH["s%d" % _i] = ("sbuf", [128, C], U8)
 for _i in range(1, R + 1):
     SCRATCH["t%d" % _i] = ("sbuf", [128, 4 * C], B16)
 
-SEMAPHORES = ["cv", "cs", "ct", "cp", "sent", "arr0", "arr1", "arr2", "ldxa", "ldxb", "ldu", "ldw", "ldb", "ldv", "out"]
+SEMAPHORES = ["cv", "cs", "ct", "cp", "sent", "arr0", "arr1", "arr2", "ldxa", "ldxb", "ldu", "ldw", "ldp", "ldb", "ldv", "done"]
 
 
 def rank_program(g, core, T, topo):
@@ -91,12 +89,20 @@ def rank_program(g, core, T, topo):
             clock[q][s] = max(clock[q].get(s, 0), m)
         clock[q][sem] = n
 
+    def meet(x, y):
+        if not (x[0] < y[1] and y[0] < x[1]):
+            return False
+        return x[2] != y[2] or (x[0] - y[0]) % x[2] == 0
+
+    def full(acc):
+        return acc if len(acc) == 4 else acc + (1,)
+
     def depend(q, outs, ins):
         need = {}
-        for acc, write in [(a, True) for a in outs] + [(a, False) for a in ins]:
-            name, a, b = acc
-            for (c, d, w, oq, tok) in log.get(name, []):
-                if not (a < d and c < b):
+        for acc, write in [(full(a), True) for a in outs] + [(full(a), False) for a in ins]:
+            name = acc[0]
+            for (run, w, oq, tok) in log.get(name, []):
+                if not meet(acc[1:], run):
                     continue
                 if name == "ps":
                     if oq == q and (q == "t" or not (w or write)):
@@ -110,12 +116,12 @@ def rank_program(g, core, T, topo):
             know(q, tok)
 
     def note(q, outs, ins, tok):
-        for acc, write in [(a, True) for a in outs] + [(a, False) for a in ins]:
-            name, a, b = acc
+        for acc, write in [(full(a), True) for a in outs] + [(full(a), False) for a in ins]:
+            name, a, b, st = acc
             old = log.setdefault(name, [])
             if write:
-                old[:] = [e for e in old if not (a <= e[0] and e[1] <= b)]
-            old.append((a, b, write, q, tok))
+                old[:] = [e for e in old if not (a <= e[0][0] and e[0][1] <= b and (st == 1 or (e[0][2] == st and (e[0][0] - a) % st == 0)))]
+            old.append((acc[1:], write, q, tok))
 
     def emit(q, outs, ins, call):
         depend(q, outs, ins)
@@ -124,45 +130,56 @@ def rank_program(g, core, T, topo):
         total[sem] += 1
         note(q, outs, ins, (sem, total[sem], dict(clock[q])))
 
-    def load(q, out, acc, in_, sem, upto):
+    def load(q, out, acc, in_, sem):
+        depend(q, [acc], [])
         queue[q].dma_start(out, in_).then_inc(T.sem[sem], 16)
         total[sem] += 16
-        note(q, [acc], [], (sem, upto, dict(clock[q])))
+        note(q, [acc], [], (sem, 16, dict(clock[q])))
 
     def store(q, out, in_, acc):
         depend(q, [], [acc])
-        queue[q].dma_start(out, in_).then_inc(T.sem["out"], 16)
-        total["out"] += 16
+        queue[q].dma_start(out, in_).then_inc(T.sem["done"], 16)
+        total["done"] += 16
 
-    def copy(q, out, oacc, in_, iacc, scale, bias=0.0):
-        if q == "v":
-            emit("v", [oacc], [iacc], lambda e: e.tensor_scalar(out, in_, scale, None, Op.mult))
+    def acc(x):
+        return (x, 0, SCRATCH[x][1][1]) if isinstance(x, str) else x
+
+    def view(x):
+        name, a, b, st = full(acc(x))
+        return T[name][:, a:b:st] if st > 1 else T[name][:, a:b]
+
+    def source(x, by):
+        return view(x) if by is None else view(x).indirect(view(by))
+
+    def copy(q, out, in_, scale=1.0, bias=0.0, by=None):
+        ins = [acc(in_)] + ([acc(by)] if by else [])
+        if q == "v" and (scale, bias) == (1.0, 0.0):
+            emit("v", [acc(out)], ins, lambda e: e.tensor_copy(view(out), source(in_, by)))
+        elif q == "v":
+            emit("v", [acc(out)], ins, lambda e: e.tensor_scalar(view(out), source(in_, by), scale, bias, Op.mult, Op.add))
         else:
-            emit("s", [oacc], [iacc], lambda e: e.activation(out, in_, Act.Copy, bias=bias, scale=scale))
+            emit("s", [acc(out)], ins, lambda e: e.activation(view(out), source(in_, by), Act.Copy, bias=bias, scale=scale))
 
-    def whole(name):
-        return (name, 0, SCRATCH[name][1][1])
-
-    def affine(out, in_, scale, bias=0.0):
-        copy("s", T[out][:], whole(out), T[in_][:], whole(in_), scale, bias)
-
-    def small(out, in_, s1, s2, *ops):
-        a1, a2 = [T[s][:, 0:1] if isinstance(s, str) else s for s in (s1, s2)]
-        ins = [whole(in_)] + [whole(s) for s in (s1, s2) if isinstance(s, str)]
-        emit("v", [whole(out)], ins, lambda e: e.tensor_scalar(T[out][:], T[in_][:], a1, a2, *ops))
+    def small(out, in_, s1, s2, *ops, by=None):
+        a1, a2 = [T[s][:, 0:1] if isinstance(s, str) else view(s) if isinstance(s, tuple) else s for s in (s1, s2)]
+        ins = [acc(in_)] + [acc(s) for s in (s1, s2) if isinstance(s, (str, tuple))] + ([acc(by)] if by else [])
+        emit("v", [acc(out)], ins, lambda e: e.tensor_scalar(view(out), source(in_, by), a1, a2, *ops))
 
     def both(out, a, b, op):
-        emit("v", [whole(out)], [whole(a), whole(b)], lambda e: e.tensor_tensor(T[out][:], T[a][:], T[b][:], op))
+        emit("v", [acc(out)], [acc(a), acc(b)], lambda e: e.tensor_tensor(view(out), view(a), view(b), op))
 
-    def cast(out, in_):
-        emit("v", [whole(out)], [whole(in_)], lambda e: e.tensor_copy(T[out][:], T[in_][:]))
+    def scan(out, a, b, first, op0, op1):
+        emit("v", [acc(out)], [acc(a), acc(b)], lambda e: e.tensor_tensor_scan(view(out), view(a), view(b), first, op0, op1))
 
-    def quant(qn, sn, tn, a, b):
-        emit("v", [(qn, a, b), (sn, a, b)], [(tn, 4 * a, 4 * b)],
-             lambda e: e.quantize_mx(T[qn][:, a:b], T[sn][:, a:b], T[tn][:, 4 * a:4 * b]))
+    def fill(out, value):
+        emit("v", [acc(out)], [], lambda e: e.memset(view(out), value))
 
-    def psum(bank):
-        return ("ps", 512 * bank, 512 * bank + 512)
+    def quant(qn, sn, a, b, tn, c):
+        emit("v", [(qn, a, b), (sn, a, b)], [(tn, c, c + 4 * (b - a))],
+             lambda e: e.quantize_mx(T[qn][:, a:b], T[sn][:, a:b], T[tn][:, c:c + 4 * (b - a)]))
+
+    def psum(bank, n=512):
+        return ("ps", 512 * bank, 512 * bank + n)
 
     def product(bank, st, c0, mv, a, b, start=True, stop=True):
         n = b - a
@@ -170,82 +187,100 @@ def rank_program(g, core, T, topo):
              lambda e: e.matmul_mx(T.ps[:, 512 * bank:512 * bank + n], T[st[0]][:, c0:c0 + 128], T[st[1]][:, c0:c0 + 128],
                                    T[mv[0]][:, a:b], T[mv[1]][:, a:b], start, stop))
 
-    def unpack(qn, b, c, d, bank):
-        n = d - c
-        copy(qn, T["F%d" % b][:, c:d], ("F%d" % b, c, d), T.ps[:, 512 * bank:512 * bank + n], psum(bank), 2.0 ** -6)
-
-    def iota(name, pattern, base, mult):
-        if SCRATCH[name][2] == I32:
-            emit("p", [whole(name)], [], lambda e: e.iota(T[name][:], pattern, base, mult))
+    def unpack(qn, out, bank, n, scale=2.0 ** -6):
+        in_ = view(psum(bank, n))
+        if qn == "v":
+            emit("v", [out], [psum(bank)], lambda e: e.tensor_scalar(view(out), in_, scale, None, Op.mult))
         else:
-            emit("p", [whole(name)], [], lambda e: e.iota(T[name][:], pattern, base, mult, allow_small_or_imprecise_dtypes=True))
+            emit("s", [out], [psum(bank)], lambda e: e.activation(view(out), in_, Act.Copy, scale=scale))
+
+    def iota(out, pattern, base, mult=0):
+        if SCRATCH[acc(out)[0]][2] == I32:
+            emit("p", [acc(out)], [], lambda e: e.iota(view(out), pattern, base, mult))
+        else:
+            emit("p", [acc(out)], [], lambda e: e.iota(view(out), pattern, base, mult, allow_small_or_imprecise_dtypes=True))
+
+    def ramp(out, first, step):
+        name, a, b = out
+        copy("s", out, ("wn", 0, b - a), float(step), float(first - step))
+
+    def nothing_before():
+        if rank == 0:
+            fill(("fz", 0, 4 * H), 0.0)
 
     E, W, U, V = ("eq", "es"), ("wq", "wp"), ("uq", "us"), ("vq", "vs")
 
-    load("y", T.dl[:], whole("dl"), T.dist[:], "ldb", 16)
-    load("y", T.xt[:, 0:4 * SPLIT], ("xt", 0, 4 * SPLIT), T.x[:, 0:4 * SPLIT], "ldxa", 16)
-    load("s", T.ut[:], ("ut", 0, 512), T.u[:], "ldu", 16)
-    load("s", T.xt[:, 4 * SPLIT:4 * C], ("xt", 4 * SPLIT, 4 * C), T.x[:, 4 * SPLIT:4 * C], "ldxb", 16)
-    load("y", T.wq[:].bitcast(dt.uint8), ("wq", 0, 512), T.wc[:], "ldw", 32)
-    load("y", T.wp[:], ("wp", 0, 512), T.ws[:], "ldw", 32)
-    load("y", T.vt[:], ("vt", 0, 512), T.v[:], "ldv", 16)
+    fixed = {}
 
-    iota("pa", [[0, 2]], 0, 1)
-    iota("gn", [[0, 3], [16, 4]], 0, 0)
-    iota("kt", [[0, 4], [1, 16]], 128, -1)
-    iota("wn", [[1, H]], 1, 0)
-    iota("ul", [[16, 8]], 0, 0)
-    iota("one", [[0, 516]], 64, 0)
-    emit("p", [whole("et")], [whole("one")], lambda e: e.affine_select(T.et[:], T.one[:], [[-1, 516]], Op.is_equal, 0.0, 3, 4))
-    emit("v", [whole("c1")], [], lambda e: e.memset(T.c1[:], 0.0))
-    if rank == 0:
-        for b in range(4):
-            emit("v", [("F%d" % b, 0, H)], [], lambda e: e.memset(T["F%d" % b][:, 0:H], 0.0))
-    small("pm", "pa", 15, None, Op.bitwise_and)
-    cast("pf", "pm")
-    small("kb", "kt", 15, None, Op.bitwise_and)
-    small("nn", "gn", "pf", None, Op.add)
-    small("colm", "pf", 1024.0, -15360.0, Op.mult, Op.add)
-    small("kd", "kb", 1.0, 1.0 - 2.0 ** -10, Op.min, Op.subtract)
+    def once(word, call, *args, **kw):
+        fixed["-" + word] = lambda: call(*args, **kw)
 
-    def nothing(name, value):
-        copy("s", T[name][:, 0:D], (name, 0, D), T.c1[:, 0:D], whole("c1"), 0.0, value)
-
-    def keep(a):
-        copy("s", T.ki[:, a:a + 64], ("ki", a, a + 64), T.kd[:], whole("kd"), 2.0 ** 20)
-
-    def count(h, i):
-        return (PARTS[h][1] - PARTS[h][0]) // LEVELS[i]
-
-    pairs = [(h, i) for i in range(3) for h in range(2)]
-    for h, i in pairs:
-        k, (a, b) = count(h, i), PARTS[h]
-        small("td%s%d" % ("AB"[h], i), "nn", (b - a - 1.0) / k, (k * (H + a) - D - 0.25) / k, Op.mult, Op.add)
-    for h, i in pairs:
-        k, n = count(h, i), "AB"[h] + str(i)
-        if i == 0:
-            small("cc" + n, "td" + n, "colm", None, Op.add)
-        else:
-            small("ti" + n, "nn", -(k - 1) / 2.0, 1.0 / k, Op.add, Op.mult)
-    for i in range(3):
-        for p in "AB":
-            nothing("X%s%d" % (p, i), -30000.0)
-            nothing("U%s%d" % (p, i), -1.0)
-    copy("s", T.exsA[:, GAP - 1:3 * GAP:GAP], whole("exsA"), T.c1[:, 0:3], whole("c1"), 0.0)
-    keep(0)
-    copy("s", T.pn[:, 0:H], ("pn", 0, H), T.wn[:], whole("wn"), 1.0, H - 1.0)
-    copy("s", T.pn[:, H:C], ("pn", H, C), T.wn[:, 0:C - H], whole("wn"), 1.0, 2 * H - 1.0)
-    for h, i in pairs[2:]:
-        n = "AB"[h] + str(i)
-        small("tb" + n, "ti" + n, -(PARTS[h][1] - PARTS[h][0] - 1.0), "colm", Op.mult, Op.add)
-    cast("lu", "ul")
-    for h, i in pairs[2:]:
-        n = "AB"[h] + str(i)
-        both("cc" + n, "td" + n, "tb" + n, Op.add)
-    affine("coli", "pf", -1024.0, 15360.0)
-    for a in (64, 128):
-        keep(a)
-    copy("s", T.MN[:, 0:H], ("MN", 0, H), T.wn[:], whole("wn"), 1.0, -1.0)
+    once("dl", load, "y", T.dl[:], acc("dl"), T.dist[:], "ldb")
+    once("ut", load, "s", T.ut[:], acc("ut"), T.u[:], "ldu")
+    once("xB", load, "y", T.xt[:, 4 * SPLIT:4 * C], ("xt", 4 * SPLIT, 4 * C), T.x[:, 4 * SPLIT:4 * C], "ldxb")
+    once("xA", load, "s", T.xt[:, 0:4 * SPLIT], ("xt", 0, 4 * SPLIT), T.x[:, 0:4 * SPLIT], "ldxa")
+    once("wq", load, "y", T.wq[:].bitcast(dt.uint8), acc("wq"), T.wc[:], "ldw")
+    once("wp", load, "y", T.wp[:], acc("wp"), T.ws[:], "ldp")
+    once("vt", load, "y", T.vt[:], acc("vt"), T.v[:], "ldv")
+    once("pa", iota, "pa", [[0, 2]], 0, 1)
+    once("ka", iota, "ka", [[0, 16], [1, 4]], 0)
+    once("kb", iota, "kb", [[0, 4], [1, 16]], 0)
+    once("c1", fill, "c1", 1.0)
+    once("two", fill, "two", 2.0)
+    once("pm", small, "pm", "pa", 15, None, Op.bitwise_and)
+    once("wn", scan, "wn", "c1", "c1", 0.0, Op.mult, Op.add)
+    once("pf", copy, "v", "pf", "pm")
+    once("tab1", scan, ("tab", H, H + 16), "two", ("c1", 0, 16), 512 * BIG, Op.mult, Op.max)
+    once("p4", small, "p4", "pm", 2, None, Op.arith_shift_right)
+    once("tabi", iota, "tab0", [[32, 16], [1, 16]], 0)
+    once("tab0", copy, "s", ("tab", 0, H), "tab0", BIG)
+    once("pd", fill, "pd", -2.0 ** 90)
+    once("top", small, "top", "pf", 15.0, None, Op.is_lt)
+    once("pg", small, "pg", "pf", float(H), None, Op.add)
+    once("pw0", small, "pw", ("kb", 0, 16), "pf", None, Op.is_equal)
+    once("p4f", copy, "v", "p4f", "p4")
+    once("ca", small, "ca", "top", 2.0 ** 90, None, Op.mult)
+    once("pw1", both, "pw", "pw", ("tab", H, H + 16), Op.mult)
+    once("ap", small, ("ap", 15, C, 16), ("c1", 0, NB), "ca", None, Op.mult)
+    once("cb", scan, "cb", "pw", "pw", 0.0, Op.max, Op.max)
+    once("one", fill, "one", 64.0)
+    once("ul", iota, "ul", [[16, 8]], 0)
+    once("et", emit, "p", [acc("et")], [acc("one")], lambda e: e.affine_select(T.et[:], T.one[:], [[-1, 516]], Op.is_equal, 0.0, 3, 4))
+    once("k16", small, ("k16", 0, 64), "kb", "pf", -2.0 ** 20, Op.is_equal, Op.mult)
+    once("k4", small, ("k4", 0, 64), "ka", "p4f", -2.0 ** 20, Op.is_equal, Op.mult)
+    once("k16a", copy, "s", ("k16", 0, 64), ("k16", 0, 64), 1.0, HOLD)
+    once("k4a", copy, "s", ("k4", 0, 64), ("k4", 0, 64), 1.0, HOLD)
+    for c in range(64, H, 64):
+        once("k4w%d" % c, copy, "s", ("k4", c, c + 64), ("k4", 0, 64))
+        once("k16w%d" % c, copy, "s", ("k16", c, c + 64), ("k16", 0, 64))
+    for c in range(0, H + C, H):
+        once("id%d" % c, ramp, ("roots", c, min(c + H, H + C)), c - H, 1)
+    once("c16", small, "c16", "pf", -HOLD, 15 * HOLD, Op.mult, Op.add)
+    once("pb", small, "pb", "p4f", 4 * HOLD - 4.0, -12 * HOLD, Op.mult, Op.add)
+    once("c4", both, "c4", "pb", "pf", Op.add)
+    once("lu", copy, "v", "lu", "ul")
+    once("sd", fill, "sd", -EPS)
+    once("nil", nothing_before)
+    for h, p in enumerate("AB"):
+        a, b, n, k, runs, span, wide, base = shape(h)
+        c, d = a // 16, b // 16
+        once("ta" + p, iota, ("ta", c, d), [[16, k], [32, runs]], n)
+        once("tb" + p, copy, "s", ("tb", c, d), ("ta", c, d), -EPS)
+        once("sd" + p, copy, "s", ("sd", a + 15, b, 16), ("wn", 0, n // 16), 16 * EPS, -1.0 - EPS * n)
+        once("lit" + p, ramp, ("way" + p, 0, n), H + b - 1, -1)
+        cuts = sorted({0, 16} | {min(16, max(0, (H - a - span * x) // 16)) for x in range(k)})
+        for x, y in zip(cuts, cuts[1:]):
+            e0, e1 = [e + (H if e < 0 else H + C) for e in (a - H + 16 * x, a - H + 16 * x + span)]
+            once("far%s%d" % (p, x), iota, ("way" + p, n + 32 * x, n + 32 * y), [[16, y - x], [e1 - e0, 2], [1, 16]], e0)
+        once("t" + p, fill, "t" + p, 0.0)
+        for x, m, pattern, first in (("a", runs * wide, [[1, runs], [runs, wide]], 0), ("b", n // 4, [[16, k], [16 * k, runs], [4, 4]], 3),
+                                     ("c", runs * k, [[16, k], [16 * k, runs]], 15)):
+            w, y = -(-m // 16) * 16, x + p
+            once("r" + y, iota, ("r" + y, 0, m), pattern, first)
+            if w > m:
+                once("z" + y, fill, ("r" + y, m, w), 0.0)
+            once("s" + y, scan, ("s" + y, 0, w), ("k16", 0, w), ("r" + y, 0, w), 0.0, Op.add, Op.max)
+            once("j" + y, small, ("j" + y, 0, w // 16), ("s" + y, 15, w, 16), "c16", None, Op.subtract)
 
     def send(t):
         if rank + 1 == n_ranks:
@@ -260,184 +295,149 @@ def rank_program(g, core, T, topo):
     if rank > 0:
         for t in range(R):
             for name in ("hq%d" % t, "hs%d" % t):
-                log[name] = [(0, H, True, "far", ("arr%d" % t, 2 * len(topo.engines(T.cores[rank - 1], core)), {}))]
+                log[name] = [((0, H, 1), True, "far", ("arr%d" % t, 2 * len(topo.engines(T.cores[rank - 1], core)), {}))]
 
-    def before(kind, h, i, s):
-        a, b = PARTS[h]
-        if i == 0:
-            return T.xn[:, a + s:b:4], ("xn", a, b)
-        src = "%s%s%d" % (kind, "AB"[h], i - 1)
-        return T[src][:, D + s:D + b - a:4], (src, D, D + b - a)
+    def at(i):
+        if i % 2 or i == 14:
+            return ("at", i, C, 16)
+        return ("pe", 32 * i + 2, 32 * i + 2 + 2 * NB - 1, 2)
 
-    def row(h, i):
-        p, (a, b) = "AB"[h], PARTS[h]
-        if i == 3:
-            k = count(h, 2)
-            for s in range(k):
-                c = a + 64 * s
-                emit("v", [("exn", c, c + 64)], [("ki", 0, 64), whole("X%s2" % p)],
-                     lambda e: e.tensor_tensor_scan(T.exn[:, c:c + 64], T.ki[:, 0:64], T["X%s2" % p][:, D + s:D + b - a:k], 0.0, Op.add, Op.max))
-            return
-        run = (b - a) // 4
-        for s in range(1, 4):
-            c = GAP * (s - 1)
-            src, acc = before("X", h, i, s)
-            emit("v", [("exs" + p, c, c + run)], [("ki", 0, run), acc],
-                 lambda e: e.tensor_tensor_scan(T["exs" + p][:, c:c + run], T.ki[:, 0:run], src, 0.0, Op.add, Op.max))
+    def col(name, i):
+        return (name, i, C, 16)
 
-    def sums(h, i):
-        n = "AB"[h] + str(i)
-        emit("v", [whole("ra" + n)], [whole("exs" + n[0]), whole("cc" + n)],
-             lambda e: e.tensor_tensor(T["ra" + n][:], T["exs" + n[0]][:, 15:3 * GAP:16], T["cc" + n][:], Op.add))
-
-    def listing(h, i):
-        if i == 3:
-            a, b = PARTS[h]
-            emit("v", [("L3", a // 16, b // 16)], [("exn", a, b), whole("coli")],
-                 lambda e: e.tensor_scalar(T.L3[:, a // 16:b // 16], T.exn[:, a + 15:b:16], T.coli[:, 0:1], -1.0, Op.subtract, Op.mult))
-        else:
-            n = "AB"[h] + str(i)
-            small("L" + n, "ra" + n, -float(count(h, i)), None, Op.mult)
-
-    def merge(kind, h, i, s):
-        n = "AB"[h] + str(i)
-        dst, run = kind + n, (PARTS[h][1] - PARTS[h][0]) // 4
-        if s in "0s":
-            old, iacc = before(kind, h, i, 0)
-            copy("v" if s == "0" else "s", T[dst][:, D:D + run], (dst, D, D + run), old, iacc, 1.0)
-            return
-        s = int(s)
-        a = D + run * s
-        out, oacc = T[dst][:, a:a + run], (dst, a, a + run)
-        old, iacc = (out, oacc) if kind + str(i) == "U0" else before(kind, h, i, s)
-        emit("v", [oacc], [(dst, 0, a), whole("L" + n), iacc],
-             lambda e: e.tensor_tensor(out, T[dst][:, 0:a].indirect(T["L" + n][:, 4 * s - 4:4 * s - 4 + run // 16]), old, Op.max))
-
-    def decide(h, qn):
-        a, b = PARTS[h]
-        in_, bank = T.ps[:, 2048 + 512 * h:2048 + 512 * h + b - a], psum(4 + h)
-        if qn == "v":
-            emit("v", [("ff", a, b)], [bank], lambda e: e.tensor_scalar(T.ff[:, a:b], in_, 0.0, None, Op.is_ge))
-        else:
-            emit("s", [("ff", a, b)], [bank], lambda e: e.activation(T.ff[:, a:b], in_, Act.Sign, bias=2.0 ** -100))
-
-    def places(h):
-        a, b = PARTS[h]
-        dst, run = "U%s0" % "AB"[h], (b - a) // 4
-        for s in range(4):
-            c = D + run * s
-            emit("v", [(dst, c, c + run)], [("ff", a, b), ("pn", a, b)],
-                 lambda e: e.tensor_tensor_scan(T[dst][:, c:c + run], T.pn[:, a + s:b:4], T.ff[:, a + s:b:4], 0.0, Op.max, Op.mult))
-
-    def block(i):
-        c, h = H + 64 * i, int(64 * i >= SPLIT)
-        src, s = "U%s2" % "AB"[h], i - PARTS[h][0] // 64
-        old = T[src][:, D + s:D + PARTS[h][1] - PARTS[h][0]:count(h, 2)]
-        emit("v", [("MN", c, c + 64)], [("MN", 0, c), ("L3", 4 * i, 4 * i + 4), whole(src)],
-             lambda e: e.tensor_tensor(T.MN[:, c:c + 64], T.MN[:, 0:c].indirect(T.L3[:, 4 * i:4 * i + 4]), old, Op.max))
-
-    def collect(a, b):
-        emit("v", [("ex", a, b)], [("ki", 0, b - a), ("MN", H + a, H + b)],
-             lambda e: e.tensor_tensor_scan(T.ex[:, a:b], T.ki[:, 0:b - a], T.MN[:, H + a:H + b], 0.0, Op.add, Op.max))
-
-    def listed(a, b):
-        emit("v", [("lz", a // 16, b // 16)], [("ex", a, b), whole("coli")],
-             lambda e: e.tensor_scalar(T.lz[:, a // 16:b // 16], T.ex[:, a + 15:b:16], T.coli[:, 0:1], None, Op.subtract))
-
-    def gather(qn, b, h):
-        a, e1 = PARTS[h]
-        out, src = T.z[:, 4 * a + b:4 * e1:4], T["F%d" % b][:, 0:H + e1].indirect(T.lz[:, a // 16:e1 // 16])
-        outs, ins = [("z", 4 * a + b, 4 * a + b + 1)], [("F%d" % b, 0, H + e1), ("lz", a // 16, e1 // 16)]
-        if qn == "v":
-            emit("v", outs, ins, lambda e: e.tensor_copy(out, src))
-        else:
-            emit("s", outs, ins, lambda e: e.activation(out, src, Act.Copy))
-
-    def finish(qn, new, h, b):
-        a, e1 = PARTS[h]
-        bank = 4 - 4 * h + b
-        copy(qn, T[new][:, 4 * a + b:4 * e1:4], (new, 4 * a + b, 4 * a + b + 1), T.ps[:, 512 * bank:512 * bank + e1 - a], psum(bank), 2.0 ** -6)
+    def mark_of(i):
+        return 1024 * BIG * 2 ** i
 
     def step(word):
         t, name = int(word[0]), word[1:]
         q = ("q%d" % t, "s%d" % t)
-        k, h = name[0], "AB".find(name[1:2])
-        a, b = PARTS[h]
-        n = int(name[2]) if name[2:3].isdigit() else None
-        if k in "UX":
-            merge(k, h, n, name[3])
-        elif k in "raL":
-            {"r": row, "a": sums, "L": listing}[k](h, n)
-        elif k == "m":
-            block(int(name[1]))
-        elif k == "c":
-            collect(64 * int(name[1]), 64 * n)
-        elif k == "l":
-            listed(a, b)
-        elif k == "o":
-            product(n if h else OWN[n], E, 128 * n, q, a, b)
-        elif k == "O":
-            unpack(name[3], n, H + a, H + b, n if h else OWN[n])
-        elif k == "h":
+        kind, h = name[0], "AB".find(name[1:2])
+        p = name[1:2]
+        a, b, n, k, runs, span, wide, base = shape(max(h, 0))
+        digits = "".join(c for c in name if c.isdigit())
+        i = int(digits) if digits else None
+        qn = name[-1]
+        if kind == "D":
+            small("du", "dl", -1.0, "pg", Op.mult, Op.add)
+        elif kind == "n":
+            copy(qn, ("par", 224 * i, 224 * i + 224), "tab", by=("du", 14 * i, 14 * i + 14))
+        elif name == "Wa":
+            small(at(14), col("par", 15), "ca", ("cb", 15, 16), Op.add, Op.min)
+        elif name == "Wb":
+            both(col("fr", 14), col("ap", 14), col("par", 14), Op.add)
+        elif name == "Wc":
+            both(at(13), col("fr", 14), at(14), Op.min)
+        elif name == "Wd":
+            both(col("fr", 13), col("cr", 13), at(13), Op.subtract)
+        elif name == "We":
+            both(at(12), col("fr", 13), at(13), Op.min)
+        elif name == "Wf":
+            both("xa", col("cr", 0), at(0), Op.subtract)
+        elif name == "Wg":
+            both("xb", "xa", at(0), Op.min)
+        elif name == "Wh":
+            small("xc", "xb", -EPS / BIG, None, Op.mult)
+        elif name == "Wi":
+            both("out", "xc", "tb", Op.add)
+        elif kind == "a":
+            copy(qn, col("ap", i), at(i), -1.0, mark_of(i))
+        elif kind == "C" and t == 0:
+            copy(qn, col("cr", i), col("par", i), 1.0, mark_of(i))
+        elif kind == "j":
+            both(col("yr", i), col("cr", i - 1), col("par", i), Op.subtract)
+        elif kind == "J":
+            both(col("pr", i), col("yr", i), col("par", i), Op.min)
+        elif kind == "K":
+            copy(qn, col("kr", i), col("pr", i), 1.0, -mark_of(i))
+        elif kind == "F":
+            both(("pd", 1, 2 * NB, 2), col("cr", i - 1), at(i), Op.subtract)
+        elif kind == "B":
+            both(("pe", 32 * i + 3, 32 * i + 2 + 2 * NB, 2), col("kr", i), at(i), Op.add)
+        elif kind == "w":
+            scan(("pe", 32 * i - 63, 32 * i - 63 + 2 * NB), "pd", ("pe", 32 * i + 2, 32 * i + 2 + 2 * NB), 0.0, Op.min, Op.max)
+        elif kind == "b":
+            both(col("fr", i), col("ap", i), col("par", i), Op.add)
+        elif kind == "M":
+            both(at(i - 1), col("fr", i), at(i), Op.min)
+        elif kind == "d":
+            emit("v", [("hit", a, b)], [psum(4 + h), ("ap", a, b)],
+                 lambda e: e.tensor_tensor(T.hit[:, a:b], view(psum(4 + h, n)), T.ap[:, a:b], Op.is_ge))
+        elif kind == "s":
+            scan(("sc", a, b), ("hit", a, b), ("sd", a, b), 0.0, Op.max, Op.add)
+        elif kind == "t":
+            both(("t" + p, 0, n // 16), ("sc", a + 15, b, 16), ("out", a // 16, b // 16), Op.max)
+        elif kind == "L":
+            small("L" + p, "t" + p, -1.0 / EPS, None, Op.mult, by=("ja" + p, 0, 1))
+        elif kind == "G":
+            c = base + 16 * k * i
+            copy(qn, ("way" + p, c, c + 16 * k), ("way" + p, 0, c), by=("L" + p, wide * i, wide * i + k))
+        elif kind == "c":
+            scan(("ex", a, b), ("k4", 0, n), ("way" + p, base, base + n), 0.0, Op.add, Op.max)
+        elif kind == "l":
+            small(("l4", a // 4, b // 4), ("ex", a, b), 4.0, "c4", Op.mult, Op.add, by=("jb" + p, 0, n // 64))
+        elif kind == "g":
+            s, piece = int(name[2]), int(name[3])
+            c0 = a + span * s
+            c, d = [c0 + span * x // PIECES for x in (piece, piece + 1)]
+            copy(qn, ("fz", 4 * (H + C + c), 4 * (H + C + d)), ("fz", 0, 4 * (H + C + c0)), by=("l4", c // 4, d // 4))
+        elif kind == "r":
+            scan(("sc", a, b), ("k16", 0, n), ("way" + p, base, base + n), 0.0, Op.add, Op.max)
+        elif kind == "R":
+            small(("l16", 16 * h, 16 * h + 16), ("sc", a, b), "c16", None, Op.subtract, by=("jc" + p, 0, 1))
+        elif kind == "p":
+            c = H + C + a + span * i
+            copy(qn, ("roots", c, c + span), ("roots", 0, c), by=("l16", 16 * h + runs * i, 16 * h + runs * i + runs))
+        elif kind == "o":
+            product(i, E, 128 * i, q, 0, C)
+        elif kind == "O":
+            unpack(qn, ("fz", 4 * H + i, 4 * (H + C), 4), i, C)
+        elif kind == "h":
             if rank > 0:
-                product(4 + n, E, 128 * n, ("hq%d" % t, "hs%d" % t), 0, H)
-        elif k == "H":
+                product(4 + i, E, 128 * i, ("hq%d" % t, "hs%d" % t), 0, H)
+        elif kind == "H":
             if rank > 0:
-                unpack(name[3], n, 0, H, 4 + n)
-        elif k == "e":
-            product(4 - 4 * h + n, E, 128 * n, q, a, b, True, False)
-        elif k == "g":
-            gather(name[3], n, h)
-        elif k == "z":
-            quant("zq", "zs", "z", a, b)
-        elif k == "w":
-            product(4 - 4 * h + n, W, 128 * n, ("zq", "zs"), a, b, False, True)
-        elif k == "f":
-            finish(name[3], "t%d" % (t + 1), h, n)
-        elif k == "q":
-            quant(q[0], q[1], "t%d" % t if t else "xt", a, b)
-        elif k == "x":
+                unpack(qn, ("fz", i, 4 * H, 4), 4 + i, H)
+        elif kind == "e":
+            product(4 - 4 * h + i, E, 128 * i, q, a, b, True, False)
+        elif kind == "z":
+            quant("zq", "zs", a, b, "fz", 4 * (H + C + a))
+        elif kind == "m":
+            product(4 - 4 * h + i, W, 128 * i, ("zq", "zs"), a, b, False, True)
+        elif kind == "f":
+            unpack(qn, ("t%d" % (t + 1), 4 * a + i, 4 * b, 4), 4 - 4 * h + i, n)
+        elif kind == "q":
+            quant(q[0], q[1], a, b, "t%d" % t if t else "xt", 4 * a)
+        elif kind == "x":
             send(t)
-        elif k == "u":
+        elif kind == "u":
             product(4 + h, V if t == R else U, 0, q, a, b)
-        elif k == "d":
-            decide(h, name[2])
-        elif k == "p":
-            places(h)
-        elif k == "y":
-            c = 2048 + 512 * h
-            copy(name[2], T.yt[:, a:b], ("yt", a, b), T.ps[:, c:c + b - a], psum(4 + h), 1.0)
-        elif k == "Y":
-            store(name[2], T.y[:, a:b], T.yt[:, a:b], ("yt", a, b))
-        elif k == "C":
-            store(name[2], T.oc[:, 4 * a:4 * b], T[q[0]][:, a:b].bitcast(dt.uint8), (q[0], a, b))
-        elif k == "S":
-            store(name[3], T.osc[4 * n:4 * n + 4, :], T[q[1]][32 * n:32 * n + 4, :], (q[1], 0, C))
-        elif k == "R":
-            copy("s", T.olt[:], whole("olt"), T.MN[:, H:H + C], ("MN", H, H + C), 1.0, -float(H))
-        elif k == "T":
-            store(name[2], T.ol[:], T.olt[0:128:16, :], whole("olt"))
-        elif k == "v":
-            quant("vq", "vs", "vt", 0, 128)
-        elif k == "D":
-            small("du", "dl", -1.0, None, Op.add)
-        elif k == "n":
-            emit("v", [("xn", a, b)], [whole("wn"), whole("du"), ("pn", a, b)],
-                 lambda e: e.tensor_tensor(T.xn[:, a:b], T.wn[:].indirect(T.du[:, a // 16:b // 16]), T.pn[:, a:b], Op.subtract))
+        elif kind == "y":
+            unpack(qn, ("yt", a, b), 4 + h, n, 1.0)
+        elif kind == "Y":
+            store(qn, T.y[:, a:b], T.yt[:, a:b], ("yt", a, b))
+        elif kind == "C":
+            store(qn, T.oc[:, 4 * a:4 * b], T[q[0]][:, a:b].bitcast(dt.uint8), (q[0], a, b))
+        elif kind == "S":
+            store(qn, T.osc[4 * i:4 * i + 4, :], T[q[1]][32 * i:32 * i + 4, :], (q[1], 0, C))
+        elif kind == "T":
+            store(qn, T.ol[:], T.roots[0:128:16, H + C:H + 2 * C], ("roots", H + C, H + 2 * C))
+        elif kind == "v":
+            quant("vq", "vs", 0, 128, "vt", 0)
         elif name == "i0":
-            quant("ua", "uas", "ut", 0, 128)
+            quant("ua", "uas", 0, 128, "ut", 0)
         elif name == "i1":
-            emit("s", [whole("us")], [whole("uas"), whole("lu")], lambda e: e.activation(T.us[:], T.uas[:].indirect(T.lu[:]), Act.Copy))
+            emit("s", [acc("us")], [acc("uas"), acc("lu")], lambda e: e.activation(T.us[:], T.uas[:].indirect(T.lu[:]), Act.Copy))
         elif name == "i2":
-            emit("v", [whole("uq")], [whole("ua"), whole("lu")],
+            emit("v", [acc("uq")], [acc("ua"), acc("lu")],
                  lambda e: e.tensor_copy(T.uq[:].bitcast(dt.uint32), T.ua[:].bitcast(dt.uint32).indirect(T.lu[:])))
-        elif k == "E":
-            c = 128 * n
-            emit("v", [("eq", c, c + 128), ("es", c, c + 128)], [whole("et")],
-                 lambda e: e.quantize_mx(T.eq[:, c:c + 128], T.es[:, c:c + 128], T.et[:, 3 - n:515 - n]))
+        elif kind == "E":
+            quant("eq", "es", 128 * i, 128 * i + 128, "et", 3 - i)
 
     for word in ORDER.split():
-        step(word)
+        if word in fixed:
+            fixed[word]()
+        else:
+            step(word)
 
     for sem in SEMAPHORES:
         if total[sem]:

@@ -7,19 +7,22 @@ SPLIT = 192
 PARTS = ((0, SPLIT), (SPLIT, C))
 SPANS = (2, 2)
 PIECES = 2
+CUTS = ((0, 192), (192, 320), (320, C))
+SENDS = {"P": (0, 128), "Q": (128, 256)}
+UB, OB, HB, EB = (0, 1, 2), 4, 0, (4, 0, 4)
 NB = C // 16
 EPS, BIG, HOLD = 2.0 ** -11, 2.0 ** 64, 2048.0
 ORDER = (
-    "-c1 -pa -tabi -two -one -tab0 -kb -dl -taB -xB -ut -pm -sd -pf -pd -tab1 -ul -xA -zcA -pg -top -k16 -pw0 -k16a 0D -tbB 0n0s -ca -p4 -pw1 -raA 0n1v 0C9s -cb 0C5s -et -wn 0Wa -p4f 0C11s 0qB 0C7s 0j10 0a14s -rbB 0j12 0j6 -litB 0Wb 0J10 0J12 0C1s 0j8 0Wc -k16w192 -lu 0j2 0C13s -vt 0E0 0Wd 0x 0C3s 0J8 -id512 0K12s 0i0 0We 0j4 0J2 -zaA 0F12 0a13s 0K2s 0B12 0i2 0K10s 0w12 0qA 0B10 -sdA 0F10 -raB -k16w128 0J6 0E3 -nil -sdB -ka 0w10 0a12s 0E2 -sbB 0K8s 0i1 0F8 0a10s 0B8 -saB 0b10 0K6s -farA0 -taA 0J4 0o2 0w8 0E1 0C0s -c16 0F6 0B6 -rbA 0uB 0a8s -k4 -jbB -id0 0K4s 0a6s 0M10 0w6 0b12 0b8 -pb -farB0 -tbA 0F4 -wq 0B4 0h3 0b6 0o3 0a4s 0M8 0b4 0w4 0O2s -saA 0M6 -k4a -ap -farB4 0uA 0o1 0a2s 0a9s 0M12 0F2 -rcA 0B2 0a5s 0M4 0a7s 0b2 -c4 -farA10 0w2 0a11s 0M2 0Wf 0a3s 0a0s -jaA 0a1s -tA -tB 0Wg 0dB 0H3s 0dA 0Wh 0sB 0Wi 0O1s 0sA 0O3s 0tB -k16w64 -litA -wp -jaB -sbA 0h1 0eB2 0tA 0o0 0LB 0O0s 0LA 0GB0v 0GA0v 0GB1v 0GA1v 0GB2v -k4w192 0GA2v 0GB3v 0h0 0eB3 0GA3v 0eA3 0H1s -k4w64 -jbA 0eA1 0GA4v -rcB 0GB4s -k4w128 0H0s 0eB0 0GB5v 0h2 0GA5v 0GB6v 0H2s 0eA0 0GB7s 0cA 0lA 0cB 0gA01s 0eA2 0gA00v 0lB 0gA10s 0gA11v -scA 0gB00v 0gB01s 0gB11s 0zA 0mA3 0gB10v 0mA1 0fA1s 0fA3s 0mA2 0mA0 0eB1 0fA2s 0zB 0mB2 0mB0 0fA0v 0fB0s -scB 0mB3 "
-    "1qA 0mB1 1uA 0fB2v 0fB1v 0fB3s 1dA 1qB 1sA 1uB 1o2 1tA 1dB 1LA 1x 1o0 1sB 1o1 1GA0s 1GA1s 1tB 1LB 1o3 1GA2v 1GB0v -jcB 1O0s 1h2 1h0 1GA3v 1GB1v 1O3v 1O2s 1h3 1GA4s 1GB2s 1GA5v 1O1s 1h1 1GB3v 1cA 1GB4s 1H0s 1H2v 1GB5v 1H3s 1lA 1eA2 1H1v 1eB1 1eA1 1gA00v 1GB6s 1eB3 1eB0 1GB7s 1cB 1gA01s -id256 1gA10s 1gA11v 1eA3 1lB -jcA 1eA0 1gB00s 1gB01v 1eB2 1zA 1mA1 1gB11v 1gB10s 1mA2 1mA3 1zB 1fA2s 1fA1v 1fA3s 1mA0 1fA0v 1mB3 2v 1mB2 1mB1 1mB0 "
-    "2qA 2uA 1fB3s 1fB2v 1fB0s 1fB1v 2dA 2qB 2uB 2o1 2o0 2sA 2dB 2tA 2x 2sB 2o3 2o2 2h0 2O1s 2LA 2tB 2GA0v 2h1 2LB 2GA1v 2O3s 2GB0v 2O0s 2GA2v 2GB1v 2GA3v 2O2v 2GB2s 2GA4s 2h2 2GB3s 2h3 2GB4s 2GA5v 2H0v 2eA0 2cA 2GB5v 2GB6v 2H1s 2H2s 2H3s 2lA 2eA3 2rA 2GB7s 2gA00s 2eA2 2gA01v 2gA10s 2eA1 2cB 2eB0 2gA11v 2lB 2gB01s 2eB3 2eB2 2eB1 2gB00v 2zA 2mA2 2gB11v 2mA0 2gB10s 2RA 2zB 2mA1 2rB 2fA1v 2RB 2mA3 2pA0s 2fA2s 2fA0s 2pA1s 2mB2 2fA3s 2fB2v 2mB3 2mB1 2fB3v 2mB0 2fB1v 2fB0s "
-    "3qA 3uA 3CAy 3qB 2pB0s 3yAs 3CBy 3S2s 3YAy 3S0s 3S1s 3uB 2pB1v 3S3s 3yBv 2Ty 3YBy")
+    "-pa -sd -dl -ul -tabi -pm -xA -kb -two -xB -tab0 -c1 -pf -ut -lu -pd -p4 -zaA -pg -wn -nil -tab1 -k16 0D -c16 0n1s -p4f -top -pw0 -litB 0n0v 0N13s -pw1 -taB -ca 0C1s -one -ka -cb 0C11s -k4 -farB0 0Wd 0qA 0N14s 0C9s -rbA 0C3s 0C13s 0C5s 0C6s 0Wa 0C7s 0We 0j12 -raA 0j6 0j10 0F14 0B14 0J12 -k4a 0Wb 0J10 -et -k16a 0j8 0w14 0K12s 0C12s 0j2 -sdA 0qB 0F12 0B12 0J6 0j4 0J2 0J8 -litA 0K10s -k4w128 0a12s 0w12 0i0 0K8s 0b12 0xP 0C0s 0B10 0K6s 0F10 0i2 0a14s 0w10 0E3 0J4 0F8 -taA -raB 0B8 0C2s 0E1 0Wc -id512 0w8 -sdB 0i1 0E2 0E0 0B6 0F6 0C10s 0a6s 0C8s -id256 0qC 0K4s 0M12 -wq 0uB 0a8s 0oP3 0w6 0C4s 0M14 0b6 0K2s 0a11s 0b10 0b8 0F4 0B4 -k4w64 0M6 -id0 -tbA -pb -rbB -tbB -farA10 0b4 0M10 0w4 0M8 -tA -ap 0oP1 0b2 -farA0 -wp 0F2 0uC 0OP3s 0a10s 0B2 0a2s 0a7s -saA 0M2 0M4 0uA 0w2 0oP0 -tB 0a1v -k4w192 0a9s 0a3v 0Wf -jaA 0a5s -saB -sbA 0oP2 0a4s 0a13s 0hP3 0a0s 0Wg 0OP1s 0dA 0eA1 0dB 0dC 0sA 0eA3 0hP1 0xQ 0hP2 0Wi 0sC 0hP0 0sB 0tA -jaB -farB4 0tB 0LA 0OP0s 0OP2s -rcA 0HP0s 0eA2 0hQ0 0LB 0HP3s 0GB0s 0HP1s 0GA0v 0GB1s -sbB 0hQ3 0GA1v 0GB2s 0HP2s -jbA 0GA2v 0HQ0v -c4 0GA3v 0GB3s 0HQ3s 0hQ2 -vt 0GB4s 0hQ1 0HQ1s 0GA4v 0eB0 0GB5s 0eA0 0GA5v 0cA 0lA -jbB 0HQ2s 0GB6s 0eB2 -k16w192 0GB7v 0eB3 0gA01v 0cB 0gA00s 0gA11v 0gA10s 0eB1 0lB 0zA 0mA1 0gB01s 0mA2 0mA3 0gB00v 2v 0zB 0mA0 0fA1s 0mB0 0gB11v 0mB1 0gB10s 0fA3v 0fA2s 0mB2 0zC 0fA0s 0fB1s 0eC1 0mB3 0eC2 0eC3 0eC0 0mC2 0mC3 0fB2s 0mC0 0fB0v 0fB3s 0mC1 "
+    "1qA 0fC2s 1qB 0fC0v 1uA 0fC3s 0fC1s 1uB 1dA -k16w128 -rcB 1qC 1dB 1uC 1sA 1oP0 1oP3 1sB 1tA 1xP 1OP0s 1dC 1LA 1sC 1GA0v 1tB 1oP2 1GA1v 1LB 1GA2s 1GB0s 1hP0 1hP1 1OP2v 1hP3 1hP2 1xQ 1GA3v 1GB1v 1OP3s 1oP1 1HP1s -zcA 1GA4v 1GB2v 1HP2v 1HP0s 1GB3v 1HP3v 1hQ2 1GA5s 1hQ0 1GB4v 1cA 1OP1s 1hQ1 1HQ1v 1hQ3 1GB5s 1HQ2v 1eB1 1HQ3v 1eA2 1HQ0s 1eB3 1lA -scB 1GB6s 1eA0 1GB7v 1gA01s 1gA00v 1cB 1gA11v 1gA10s 1lB 1zA -k16w64 1gB01s 1eA3 1eB0 1eA1 1gB00v 1mA1 1mA3 1fA3s 1fA1v 1mA0 1zB 1mA2 1gB10s 1gB11v 1eB2 1fA0v 1eC1 1fA2s 1mB0 1mB1 1mB3 1zC 1fB1v 1mB2 1eC3 "
+    "2qA 1fB0s 1fB2s 1eC0 1eC2 1fB3s 1mC2 1mC0 2qB 1fC2s 1mC3 1mC1 1fC0v 2uA 1fC3v 1fC1s 2dA 2qC 2sA 2uB -scA 2uC 2dB 2tA 2xP 2oP2 2dC 2oP3 2xQ 2oP0 2sB 2LA 2oP1 2sC 2hP0 2OP2s 2GA0v 2tB -jcA 2OP3s 2hP1 2OP0s 2HP1s 2hP3 2LB 2GA1v 2eA2 2GB0v 2hP2 2HP3s 2GA2v 2GB1v 2GA3v 2HP0s 2GB2v 2GA4v 2HP2s 2hQ3 2hQ0 2GB3v 2GA5v 2GB4v 2OP1s 2HQ0s 2cA 2hQ1 2hQ2 2GB5v 2HQ1s 2lA 2HQ2s 2HQ3s 2eB2 2eA3 2eA0 2eA1 2GB6v 2eB0 2rA 2GB7v 2gA01s 2gA00v 2cB 2eB3 2gA10v 2gA11s 2lB 2zA 2mA2 2mA1 2gB00v 2gB01s 2RA 2mA0 2fA2v 2gB10s 2zB 2mA3 2fA1s 2eB1 2eC2 2mB2 2mB0 2mB1 2gB11v 2fA0v 2mB3 -jcB 2eC1 2fA3s 2fB0s 2eC3 2zC 2fB2v "
+    "3qA 2pA0s 2eC0 3CAy 2mC0 2mC3 2rB 2fB1s 2fB3s 2pA1s 3qB 2mC2 2fC3s 3CBy 2fC0s 2mC1 3uA 2RB 3uB 2fC2s 2fC1v 3yAv 2pB0s 3qC 3YAy 3uC 3S3s 3S1s 3yBv 3CCy 2pB1v 3S0s 3YBy 2Ty 3yCs 3S2s 3YCy")
 
 
 def shape(h):
     a, b = PARTS[h]
     n, k = b - a, SPANS[h]
-    return a, b, n, k, n // 16 // k, n // k, k + k % 2, n + 2 * H
+    return a, b, n, k, n // 16 // k, n // k, n + 2 * H
 
 
 SCRATCH = {
@@ -33,7 +36,7 @@ SCRATCH = {
     "one": ("sbuf", [128, 516], B16), "et": ("sbuf", [128, 516], B16), "eq": ("sbuf", [128, 512], X4), "es": ("sbuf", [128, 512], U8),
     "c1": ("sbuf", [128, H], F32), "two": ("sbuf", [128, 16], F32), "wn": ("sbuf", [128, H], F32),
     "tab": ("sbuf", [128, H + 16], F32), "tab0": ("sbuf", [128, H], F32),
-    "pe": ("sbuf", [128, 7 * 64], F32), "pd": ("sbuf", [128, 2 * NB], F32),
+    "pe": ("sbuf", [128, 8 * 64], F32), "pd": ("sbuf", [128, 2 * NB], F32),
     "k4": ("sbuf", [128, H], F32), "k16": ("sbuf", [128, H], F32), "ka": ("sbuf", [128, 64], F32), "kb": ("sbuf", [128, 64], F32),
     "dl": ("sbuf", [128, NB], I32), "du": ("sbuf", [128, NB], U16),
     "pa": ("sbuf", [128, 2], I32), "pm": ("sbuf", [128, 2], I32), "pf": ("sbuf", [128, 2], F32),
@@ -47,11 +50,11 @@ SCRATCH = {
 }
 for _n in ("par", "cr", "at", "ap", "yr", "pr", "kr", "fr", "hit", "sd", "sc", "ex", "yt"):
     SCRATCH[_n] = ("sbuf", [128, C], F32)
-for _n in ("ta", "tb", "xa", "xb", "xc", "out"):
+for _n in ("ta", "tb", "xa", "xb", "out"):
     SCRATCH[_n] = ("sbuf", [128, NB], F32)
 for _h, _p in enumerate("AB"):
     _s = shape(_h)
-    SCRATCH["way" + _p] = ("sbuf", [128, _s[7] + _s[2]], F32)
+    SCRATCH["way" + _p] = ("sbuf", [128, _s[6] + _s[2]], F32)
     SCRATCH["t" + _p] = ("sbuf", [128, 16], F32)
     SCRATCH["L" + _p] = ("sbuf", [128, 16], U16)
     for _n, _k in (("a", 2), ("b", 4), ("c", 2)):
@@ -67,7 +70,8 @@ for _i in range(4):
 for _i in range(1, R + 1):
     SCRATCH["t%d" % _i] = ("sbuf", [128, 4 * C], B16)
 
-SEMAPHORES = ["cv", "cs", "ct", "cp", "sent", "arr0", "arr1", "arr2", "ldxa", "ldxb", "ldu", "ldw", "ldp", "ldb", "ldv", "done"]
+SEMAPHORES = (["cv", "cs", "ct", "cp", "sent", "ldxa", "ldxb", "ldu", "ldw", "ldp", "ldb", "ldv", "done"]
+              + ["arr%d%s" % (t, x) for t in range(R) for x in SENDS])
 
 
 def rank_program(g, core, T, topo):
@@ -230,19 +234,19 @@ def rank_program(g, core, T, topo):
     once("pm", small, "pm", "pa", 15, None, Op.bitwise_and)
     once("wn", scan, "wn", "c1", "c1", 0.0, Op.mult, Op.add)
     once("pf", copy, "v", "pf", "pm")
-    once("tab1", scan, ("tab", H, H + 16), "two", ("c1", 0, 16), 512 * BIG, Op.mult, Op.max)
+    once("tab1", scan, ("tab", H, H + 16), "two", ("c1", 0, 16), -512 * EPS, Op.mult, Op.min)
     once("p4", small, "p4", "pm", 2, None, Op.arith_shift_right)
     once("tabi", iota, "tab0", [[32, 16], [1, 16]], 0)
-    once("tab0", copy, "s", ("tab", 0, H), "tab0", BIG)
-    once("pd", fill, "pd", -2.0 ** 90)
+    once("tab0", copy, "s", ("tab", 0, H), "tab0", -EPS)
+    once("pd", fill, "pd", 2.0 ** 20)
     once("top", small, "top", "pf", 15.0, None, Op.is_lt)
     once("pg", small, "pg", "pf", float(H), None, Op.add)
     once("pw0", small, "pw", ("kb", 0, 16), "pf", None, Op.is_equal)
     once("p4f", copy, "v", "p4f", "p4")
-    once("ca", small, "ca", "top", 2.0 ** 90, None, Op.mult)
+    once("ca", small, "ca", "top", -2.0 ** 20, None, Op.mult)
     once("pw1", both, "pw", "pw", ("tab", H, H + 16), Op.mult)
-    once("ap", small, ("ap", 15, C, 16), ("c1", 0, NB), "ca", None, Op.mult)
-    once("cb", scan, "cb", "pw", "pw", 0.0, Op.max, Op.max)
+    once("ap", small, ("ap", 15, C, 16), ("c1", 0, NB), "top", 2.0 ** 90, Op.mult, Op.mult)
+    once("cb", scan, "cb", "pw", "pw", 0.0, Op.min, Op.min)
     once("one", fill, "one", 64.0)
     once("ul", iota, "ul", [[16, 8]], 0)
     once("et", emit, "p", [acc("et")], [acc("one")], lambda e: e.affine_select(T.et[:], T.one[:], [[-1, 516]], Op.is_equal, 0.0, 3, 4))
@@ -262,7 +266,7 @@ def rank_program(g, core, T, topo):
     once("sd", fill, "sd", -EPS)
     once("nil", nothing_before)
     for h, p in enumerate("AB"):
-        a, b, n, k, runs, span, wide, base = shape(h)
+        a, b, n, k, runs, span, base = shape(h)
         c, d = a // 16, b // 16
         once("ta" + p, iota, ("ta", c, d), [[16, k], [32, runs]], n)
         once("tb" + p, copy, "s", ("tb", c, d), ("ta", c, d), -EPS)
@@ -273,8 +277,8 @@ def rank_program(g, core, T, topo):
             e0, e1 = [e + (H if e < 0 else H + C) for e in (a - H + 16 * x, a - H + 16 * x + span)]
             once("far%s%d" % (p, x), iota, ("way" + p, n + 32 * x, n + 32 * y), [[16, y - x], [e1 - e0, 2], [1, 16]], e0)
         once("t" + p, fill, "t" + p, 0.0)
-        for x, m, pattern, first in (("a", runs * wide, [[1, runs], [runs, wide]], 0), ("b", n // 4, [[16, k], [16 * k, runs], [4, 4]], 3),
-                                     ("c", runs * k, [[16, k], [16 * k, runs]], 15)):
+        for x, m, pattern, first in (("a", runs * k, [[1, runs], [runs, k]], 0),
+                                     ("b", n // 4, [[16, k], [16 * k, runs], [4, 4]], 3), ("c", runs * k, [[16, k], [16 * k, runs]], 15)):
             w, y = -(-m // 16) * 16, x + p
             once("r" + y, iota, ("r" + y, 0, m), pattern, first)
             if w > m:
@@ -282,23 +286,26 @@ def rank_program(g, core, T, topo):
             once("s" + y, scan, ("s" + y, 0, w), ("k16", 0, w), ("r" + y, 0, w), 0.0, Op.add, Op.max)
             once("j" + y, small, ("j" + y, 0, w // 16), ("s" + y, 15, w, 16), "c16", None, Op.subtract)
 
-    def send(t):
+    def send(t, x):
         if rank + 1 == n_ranks:
             return
         dst = T.cores[rank + 1]
         rid, pid = topo.addr(dst)[:2]
-        depend("p", [], [("q%d" % t, LO, C), ("s%d" % t, LO, C)])
-        for out, in_ in ((T["hq%d" % t][:].bitcast(dt.uint8), T["q%d" % t][:, LO:C].bitcast(dt.uint8)), (T["hs%d" % t][:], T["s%d" % t][:, LO:C])):
-            g.remote_dma(out, in_, T.sem["arr%d" % t], T.sem.sent, pid, rid, topo.mask(core, dst))
+        a, b = SENDS[x]
+        depend("p", [], [("q%d" % t, LO + a, LO + b), ("s%d" % t, LO + a, LO + b)])
+        for out, in_ in ((T["hq%d" % t][:, a:b].bitcast(dt.uint8), T["q%d" % t][:, LO + a:LO + b].bitcast(dt.uint8)),
+                         (T["hs%d" % t][:, a:b], T["s%d" % t][:, LO + a:LO + b])):
+            g.remote_dma(out, in_, T.sem["arr%d%s" % (t, x)], T.sem.sent, pid, rid, topo.mask(core, dst))
             total["sent"] += len(topo.engines(core, dst))
 
     if rank > 0:
         for t in range(R):
             for name in ("hq%d" % t, "hs%d" % t):
-                log[name] = [((0, H, 1), True, "far", ("arr%d" % t, 2 * len(topo.engines(T.cores[rank - 1], core)), {}))]
+                log[name] = [(SENDS[x] + (1,), True, "far", ("arr%d%s" % (t, x), 2 * len(topo.engines(T.cores[rank - 1], core)), {}))
+                             for x in SENDS]
 
     def at(i):
-        if i % 2 or i == 14:
+        if i % 2:
             return ("at", i, C, 16)
         return ("pe", 32 * i + 2, 32 * i + 2 + 2 * NB - 1, 2)
 
@@ -306,14 +313,18 @@ def rank_program(g, core, T, topo):
         return (name, i, C, 16)
 
     def mark_of(i):
-        return 1024 * BIG * 2 ** i
+        return -1024 * EPS * 2 ** i
 
     def step(word):
         t, name = int(word[0]), word[1:]
         q = ("q%d" % t, "s%d" % t)
         kind, h = name[0], "AB".find(name[1:2])
         p = name[1:2]
-        a, b, n, k, runs, span, wide, base = shape(max(h, 0))
+        a, b, n, k, runs, span, base = shape(max(h, 0))
+        if kind in "qudszemfyYC" and p in "ABC":
+            h = "ABC".find(p)
+            a, b = CUTS[h]
+            n = b - a
         digits = "".join(c for c in name if c.isdigit())
         i = int(digits) if digits else None
         qn = name[-1]
@@ -322,31 +333,31 @@ def rank_program(g, core, T, topo):
         elif kind == "n":
             copy(qn, ("par", 224 * i, 224 * i + 224), "tab", by=("du", 14 * i, 14 * i + 14))
         elif name == "Wa":
-            small(at(14), col("par", 15), "ca", ("cb", 15, 16), Op.add, Op.min)
+            small(at(14), col("par", 15), "ca", ("cb", 15, 16), Op.add, Op.max)
         elif name == "Wb":
-            both(col("fr", 14), col("ap", 14), col("par", 14), Op.add)
+            small(col("pr", 14), at(14), -1.0, mark_of(14), Op.mult, Op.add)
         elif name == "Wc":
-            both(at(13), col("fr", 14), at(14), Op.min)
+            both(col("fr", 14), col("pr", 14), col("par", 14), Op.add)
         elif name == "Wd":
-            both(col("fr", 13), col("cr", 13), at(13), Op.subtract)
+            both(col("yr", 14), col("yr", 13), col("par", 14), Op.subtract)
         elif name == "We":
-            both(at(12), col("fr", 13), at(13), Op.min)
+            both(col("kr", 14), col("yr", 14), col("yr", 15), Op.max)
+        elif kind == "N":
+            copy(qn, col("yr", 2 * i - 13), col("par", i), 1.0, -mark_of(i))
         elif name == "Wf":
             both("xa", col("cr", 0), at(0), Op.subtract)
         elif name == "Wg":
-            both("xb", "xa", at(0), Op.min)
-        elif name == "Wh":
-            small("xc", "xb", -EPS / BIG, None, Op.mult)
+            both("xb", "xa", at(0), Op.max)
         elif name == "Wi":
-            both("out", "xc", "tb", Op.add)
+            both("out", "xb", "tb", Op.add)
         elif kind == "a":
-            copy(qn, col("ap", i), at(i), -1.0, mark_of(i))
+            copy(qn, col("ap", i), at(i), BIG / EPS, -mark_of(i) * BIG / EPS)
         elif kind == "C" and t == 0:
             copy(qn, col("cr", i), col("par", i), 1.0, mark_of(i))
         elif kind == "j":
             both(col("yr", i), col("cr", i - 1), col("par", i), Op.subtract)
         elif kind == "J":
-            both(col("pr", i), col("yr", i), col("par", i), Op.min)
+            both(col("pr", i), col("yr", i), col("par", i), Op.max)
         elif kind == "K":
             copy(qn, col("kr", i), col("pr", i), 1.0, -mark_of(i))
         elif kind == "F":
@@ -354,14 +365,14 @@ def rank_program(g, core, T, topo):
         elif kind == "B":
             both(("pe", 32 * i + 3, 32 * i + 2 + 2 * NB, 2), col("kr", i), at(i), Op.add)
         elif kind == "w":
-            scan(("pe", 32 * i - 63, 32 * i - 63 + 2 * NB), "pd", ("pe", 32 * i + 2, 32 * i + 2 + 2 * NB), 0.0, Op.min, Op.max)
+            scan(("pe", 32 * i - 63, 32 * i - 63 + 2 * NB), "pd", ("pe", 32 * i + 2, 32 * i + 2 + 2 * NB), 0.0, Op.max, Op.min)
         elif kind == "b":
-            both(col("fr", i), col("ap", i), col("par", i), Op.add)
+            both(col("fr", i), col("cr", i), at(i), Op.subtract)
         elif kind == "M":
-            both(at(i - 1), col("fr", i), at(i), Op.min)
+            both(at(i - 1), col("fr", i), at(i), Op.max)
         elif kind == "d":
-            emit("v", [("hit", a, b)], [psum(4 + h), ("ap", a, b)],
-                 lambda e: e.tensor_tensor(T.hit[:, a:b], view(psum(4 + h, n)), T.ap[:, a:b], Op.is_ge))
+            emit("v", [("hit", a, b)], [psum(UB[h]), ("ap", a, b)],
+                 lambda e: e.tensor_tensor(T.hit[:, a:b], view(psum(UB[h], n)), T.ap[:, a:b], Op.is_ge))
         elif kind == "s":
             scan(("sc", a, b), ("hit", a, b), ("sd", a, b), 0.0, Op.max, Op.add)
         elif kind == "t":
@@ -370,7 +381,7 @@ def rank_program(g, core, T, topo):
             small("L" + p, "t" + p, -1.0 / EPS, None, Op.mult, by=("ja" + p, 0, 1))
         elif kind == "G":
             c = base + 16 * k * i
-            copy(qn, ("way" + p, c, c + 16 * k), ("way" + p, 0, c), by=("L" + p, wide * i, wide * i + k))
+            copy(qn, ("way" + p, c, c + 16 * k), ("way" + p, 0, c), by=("L" + p, k * i, k * i + k))
         elif kind == "c":
             scan(("ex", a, b), ("k4", 0, n), ("way" + p, base, base + n), 0.0, Op.add, Op.max)
         elif kind == "l":
@@ -388,31 +399,31 @@ def rank_program(g, core, T, topo):
             c = H + C + a + span * i
             copy(qn, ("roots", c, c + span), ("roots", 0, c), by=("l16", 16 * h + runs * i, 16 * h + runs * i + runs))
         elif kind == "o":
-            product(i, E, 128 * i, q, 0, C)
+            product(OB + i, E, 128 * i, q, 0, C)
         elif kind == "O":
-            unpack(qn, ("fz", 4 * H + i, 4 * (H + C), 4), i, C)
+            unpack(qn, ("fz", 4 * H + i, 4 * (H + C), 4), OB + i, C)
         elif kind == "h":
             if rank > 0:
-                product(4 + i, E, 128 * i, ("hq%d" % t, "hs%d" % t), 0, H)
+                product(HB + i, E, 128 * i, ("hq%d" % t, "hs%d" % t), *SENDS[p])
         elif kind == "H":
             if rank > 0:
-                unpack(qn, ("fz", i, 4 * H, 4), 4 + i, H)
+                unpack(qn, ("fz", 4 * SENDS[p][0] + i, 4 * SENDS[p][1], 4), HB + i, SENDS[p][1] - SENDS[p][0])
         elif kind == "e":
-            product(4 - 4 * h + i, E, 128 * i, q, a, b, True, False)
+            product(EB[h] + i, E, 128 * i, q, a, b, True, False)
         elif kind == "z":
             quant("zq", "zs", a, b, "fz", 4 * (H + C + a))
         elif kind == "m":
-            product(4 - 4 * h + i, W, 128 * i, ("zq", "zs"), a, b, False, True)
+            product(EB[h] + i, W, 128 * i, ("zq", "zs"), a, b, False, True)
         elif kind == "f":
-            unpack(qn, ("t%d" % (t + 1), 4 * a + i, 4 * b, 4), 4 - 4 * h + i, n)
+            unpack(qn, ("t%d" % (t + 1), 4 * a + i, 4 * b, 4), EB[h] + i, n)
         elif kind == "q":
             quant(q[0], q[1], a, b, "t%d" % t if t else "xt", 4 * a)
         elif kind == "x":
-            send(t)
+            send(t, p)
         elif kind == "u":
-            product(4 + h, V if t == R else U, 0, q, a, b)
+            product(UB[h], V if t == R else U, 0, q, a, b)
         elif kind == "y":
-            unpack(qn, ("yt", a, b), 4 + h, n, 1.0)
+            unpack(qn, ("yt", a, b), UB[h], n, 1.0)
         elif kind == "Y":
             store(qn, T.y[:, a:b], T.yt[:, a:b], ("yt", a, b))
         elif kind == "C":

@@ -3,27 +3,17 @@ from concourse.mybir import AluOpType as Op, ActivationFunctionType as Act, dt
 F32, B16, I32, U16, U8, X4 = "float32", "bfloat16", "int32", "uint16", "uint8", "float8_e4m3fn_x4"
 C, H, R = 448, 256, 3
 LO = C - H
-SPLIT = 192
-PARTS = ((0, SPLIT), (SPLIT, C))
-SPANS = (2, 2)
-PIECES = 2
-CUTS = ((0, 192), (192, 320), (320, C))
+SPANS = {"A": (0, 96), "B": (96, 192), "C": (192, 320), "D": (320, C)}
+CUTS = {"A": (0, 192), "B": (192, 320), "C": (320, C)}
 SENDS = {"P": (0, 128), "Q": (128, 256)}
 UB, OB, HB, EB = (0, 1, 2), 4, 0, (4, 0, 4)
 NB = C // 16
-EPS, BIG, HOLD = 2.0 ** -11, 2.0 ** 64, 2048.0
+EPS, BIG, HOLD, FAR = 2.0 ** -11, 2.0 ** 64, 2048.0, 2.0 ** 20
 ORDER = (
-    "-pa -sd -dl -ul -tabi -pm -xA -kb -two -xB -tab0 -c1 -pf -ut -lu -pd -p4 -zaA -pg -wn -nil -tab1 -k16 0D -c16 0n1s -p4f -top -pw0 -litB 0n0v 0N13s -pw1 -taB -ca 0C1s -one -ka -cb 0C11s -k4 -farB0 0Wd 0qA 0N14s 0C9s -rbA 0C3s 0C13s 0C5s 0C6s 0Wa 0C7s 0We 0j12 -raA 0j6 0j10 0F14 0B14 0J12 -k4a 0Wb 0J10 -et -k16a 0j8 0w14 0K12s 0C12s 0j2 -sdA 0qB 0F12 0B12 0J6 0j4 0J2 0J8 -litA 0K10s -k4w128 0a12s 0w12 0i0 0K8s 0b12 0xP 0C0s 0B10 0K6s 0F10 0i2 0a14s 0w10 0E3 0J4 0F8 -taA -raB 0B8 0C2s 0E1 0Wc -id512 0w8 -sdB 0i1 0E2 0E0 0B6 0F6 0C10s 0a6s 0C8s -id256 0qC 0K4s 0M12 -wq 0uB 0a8s 0oP3 0w6 0C4s 0M14 0b6 0K2s 0a11s 0b10 0b8 0F4 0B4 -k4w64 0M6 -id0 -tbA -pb -rbB -tbB -farA10 0b4 0M10 0w4 0M8 -tA -ap 0oP1 0b2 -farA0 -wp 0F2 0uC 0OP3s 0a10s 0B2 0a2s 0a7s -saA 0M2 0M4 0uA 0w2 0oP0 -tB 0a1v -k4w192 0a9s 0a3v 0Wf -jaA 0a5s -saB -sbA 0oP2 0a4s 0a13s 0hP3 0a0s 0Wg 0OP1s 0dA 0eA1 0dB 0dC 0sA 0eA3 0hP1 0xQ 0hP2 0Wi 0sC 0hP0 0sB 0tA -jaB -farB4 0tB 0LA 0OP0s 0OP2s -rcA 0HP0s 0eA2 0hQ0 0LB 0HP3s 0GB0s 0HP1s 0GA0v 0GB1s -sbB 0hQ3 0GA1v 0GB2s 0HP2s -jbA 0GA2v 0HQ0v -c4 0GA3v 0GB3s 0HQ3s 0hQ2 -vt 0GB4s 0hQ1 0HQ1s 0GA4v 0eB0 0GB5s 0eA0 0GA5v 0cA 0lA -jbB 0HQ2s 0GB6s 0eB2 -k16w192 0GB7v 0eB3 0gA01v 0cB 0gA00s 0gA11v 0gA10s 0eB1 0lB 0zA 0mA1 0gB01s 0mA2 0mA3 0gB00v 2v 0zB 0mA0 0fA1s 0mB0 0gB11v 0mB1 0gB10s 0fA3v 0fA2s 0mB2 0zC 0fA0s 0fB1s 0eC1 0mB3 0eC2 0eC3 0eC0 0mC2 0mC3 0fB2s 0mC0 0fB0v 0fB3s 0mC1 "
-    "1qA 0fC2s 1qB 0fC0v 1uA 0fC3s 0fC1s 1uB 1dA -k16w128 -rcB 1qC 1dB 1uC 1sA 1oP0 1oP3 1sB 1tA 1xP 1OP0s 1dC 1LA 1sC 1GA0v 1tB 1oP2 1GA1v 1LB 1GA2s 1GB0s 1hP0 1hP1 1OP2v 1hP3 1hP2 1xQ 1GA3v 1GB1v 1OP3s 1oP1 1HP1s -zcA 1GA4v 1GB2v 1HP2v 1HP0s 1GB3v 1HP3v 1hQ2 1GA5s 1hQ0 1GB4v 1cA 1OP1s 1hQ1 1HQ1v 1hQ3 1GB5s 1HQ2v 1eB1 1HQ3v 1eA2 1HQ0s 1eB3 1lA -scB 1GB6s 1eA0 1GB7v 1gA01s 1gA00v 1cB 1gA11v 1gA10s 1lB 1zA -k16w64 1gB01s 1eA3 1eB0 1eA1 1gB00v 1mA1 1mA3 1fA3s 1fA1v 1mA0 1zB 1mA2 1gB10s 1gB11v 1eB2 1fA0v 1eC1 1fA2s 1mB0 1mB1 1mB3 1zC 1fB1v 1mB2 1eC3 "
-    "2qA 1fB0s 1fB2s 1eC0 1eC2 1fB3s 1mC2 1mC0 2qB 1fC2s 1mC3 1mC1 1fC0v 2uA 1fC3v 1fC1s 2dA 2qC 2sA 2uB -scA 2uC 2dB 2tA 2xP 2oP2 2dC 2oP3 2xQ 2oP0 2sB 2LA 2oP1 2sC 2hP0 2OP2s 2GA0v 2tB -jcA 2OP3s 2hP1 2OP0s 2HP1s 2hP3 2LB 2GA1v 2eA2 2GB0v 2hP2 2HP3s 2GA2v 2GB1v 2GA3v 2HP0s 2GB2v 2GA4v 2HP2s 2hQ3 2hQ0 2GB3v 2GA5v 2GB4v 2OP1s 2HQ0s 2cA 2hQ1 2hQ2 2GB5v 2HQ1s 2lA 2HQ2s 2HQ3s 2eB2 2eA3 2eA0 2eA1 2GB6v 2eB0 2rA 2GB7v 2gA01s 2gA00v 2cB 2eB3 2gA10v 2gA11s 2lB 2zA 2mA2 2mA1 2gB00v 2gB01s 2RA 2mA0 2fA2v 2gB10s 2zB 2mA3 2fA1s 2eB1 2eC2 2mB2 2mB0 2mB1 2gB11v 2fA0v 2mB3 -jcB 2eC1 2fA3s 2fB0s 2eC3 2zC 2fB2v "
-    "3qA 2pA0s 2eC0 3CAy 2mC0 2mC3 2rB 2fB1s 2fB3s 2pA1s 3qB 2mC2 2fC3s 3CBy 2fC0s 2mC1 3uA 2RB 3uB 2fC2s 2fC1v 3yAv 2pB0s 3qC 3YAy 3uC 3S3s 3S1s 3yBv 3CCy 2pB1v 3S0s 3YBy 2Ty 3yCs 3S2s 3YCy")
-
-
-def shape(h):
-    a, b = PARTS[h]
-    n, k = b - a, SPANS[h]
-    return a, b, n, k, n // 16 // k, n // k, n + 2 * H
-
+    "-c1 -h0 -pa -pm -dl -sd0 -xB -h1 -wn -kb -two -taD -pf -p4 -one -pd -p4f -top -pg -tab0 -ca -tab1 -ka -ut -tbD -pw0 -pw1 -ul -sd1 -xA 0D -cb 0n1v -k4 0n0s -sdC -cc -taB -lu -cd 0C11s 0qB -farC0 0N14s 0C13s 0Wd 0Wa 0C7s 0C3s -taC 0Wh 0j12 0C9s 0We 0F14 0j8 -litA 0j4 0J12 0C5s 0B14 -sdA 0j10 0K12s 0qC 0w14 0J8 -tbB 0j6 -taA 0J10 0B12 0C1s 0F12 0a12s 0i0 0J6 0C6s 0w12 0j2 0K10s 0C0s 0K8s -k4a 0C12s -sdD 0Wb 0J4 -et 0F10 0C10s -id256 0B10 0b12 0E1 0K6s 0w10 0i2 0a10s 0F8 0B8 -tbA 0C8s 0a14s 0xP 0xQ -litD 0qA 0C2s -id0 -litB 0w8 0E2 0b10 -farD0 0B6 -tbC 0K4s 0F6 0E3 0Wc 0w6 -k4w 0i1 0oP2 0J2 0M12 -farA0 0b6 0B4 -sdB 0F4 0a8s 0E0 -farB0 0C4s 0K2s 0b8 0uA 0w4 0b4 0M6 0M14 0hP3 0a6s 0OP2s 0HP3s 0oP1 -wp -litC 0F2 0uC 0B2 0a13s 0a11s 0b2 0a5s 0M4 0a2s 0M8 -pb 0M10 0uB 0w2 0M2 0a4v -farC4 0a7v -ap 0a3s 0Wf 0a9s 0a0s 0oP0 0oP3 0a1v -c4 0Wg 0dA 0hP0 0OP1s 0OP3s 0hQ3 0OP0s 0dB 0Wi 0sA 0dC 0sB -farB10 0hP2 0IA0 0eA3 0tA 0tB 0IB0 0IC0 -vt 0GA0s 0hP1 0tC 0GB0s 0GC0s 0LA 0LB 0sC 0GA1s 0LC 0GB1v 0ID0 0tD 0HP0s 0GC1s 0GA2v 0GB2v 0eA1 0GD0s 0LD 0GC2s 0GA3v 0GB3v 0HP1s 0GD1v 0HP2s 0GA4v 0GC3v 0GD2v 0GA5v 0GB4s 0hQ0 0HQ0s 0hQ2 0GB5v 0GC4s 0hQ1 0HQ2s 0GD3v 0eA0 0cA 0cB -wq 0eB2 0GC5v 0HQ3s 0HQ1s 0GD4s 0lA 0lB 0GC6v 0gA00v 0gA01s 0eB1 0GD5s 0gB01v 0GD6v 0GC7s 0cC 0gB00s 0zA 0eA2 0GD7s 0lC -c16 0eB3 0gC01s 0mA3 0eB0 0mA2 0mA0 0mA1 0cD 0gC00v 0lD 0fA3s 0fA2s 0eC3 2v 0zB 0gD00v 0mB2 0fA1v 0mB1 0gD01s 0fA0s 0mB3 0mB0 0eC2 0eC1 0zC 0fB1v 0eC0 "
+    "1qA 0mC1 0fB2s 0fB3s 0mC3 0fB0s 0fC1s 0fC3s -k16 0mC0 1qB 0mC2 1uA 0fC2v 1uB 1dA 0fC0s 1qC 1uC 1sA 1dB 1IA0 1xP 1IB0 1sB 1tA 1oP0 1tB 1dC 1LA 1tC 1GA0s 1IC0 1oP1 1OP0s 1sC 1GB0v 1LC 1xQ 1GA1s 1LB 1oP3 1oP2 1GC0s 1hP3 1hP2 1hP0 1ID0 1tD 1OP1s 1GA2v 1GA3s 1GC1v 1GC2s 1GB1v 1LD 1GD0v 1GB2s 1OP3v 1HP3v 1GD1s 1GC3s 1eA0 1GA4s 1GB3v 1hP1 1GD2v 1hQ3 1HP0s 1hQ0 1GC4s 1HP2v 1GA5s 1HP1v 1GD3v 1GC5v 1cA 1GB4s 1OP2s 1HQ0s 1hQ2 1GD4v 1hQ1 1GB5s 1eB0 1HQ3v 1GC6v 1eA3 1HQ2s 1GC7s 1eB3 1lA 1HQ1v 1cB 1gA01v 1GD5s 1lB 1cC 1gA00s 1GD6s 1gB00v 1lC 1eB2 1gB01s 1GD7v 1eA1 1eB1 1zA 1cD 1gC00s 1eA2 1gC01v 1lD 1mA3 1zB 1mA0 1fA3s 1mA1 1mA2 1mB0 1gD01v 1mB2 1mB3 1fA0s 1fA2v 1gD00s 1fA1s 1mB1 1eC3 1eC0 1zC 1fB0s 1fB2s 1eC1 1eC2 1mC1 1fB1s 1mC3 1fB3s -k16a "
+    "2qA 1mC2 -id512 1mC0 2qB 1fC1v 1fC0v 2uA 2dA 1fC3s 1fC2s 2uB 2qC 2dB 2xP 2uC 2sA -k16w 2sB 2dC 2oP0 2tB 2OP0s 2IB0 2IC0 2oP1 2oP3 2tC 2oP2 2sC 2tA 2IA0 2LC 2hP1 2GB0s 2GC0v 2hP2 2ID0 2OP1s 2xQ 2hP0 2LA 2GA0v 2hP3 2GD0s 2eA1 2LB 2GC1v 2OP2s 2tD 2GA1v 2HP1s 2HP2s 2eA0 2GB1v 2GC2v 2hQ1 2LD 2HP0s 2GA2v 2HP3s 2GB2v 2GC3v 2hQ2 2GD1v 2GA3v 2hQ3 2hQ0 2GB3v 2GD2v 2GA4v 2GC4v 2OP3s 2GB4v 2GD3v 2GA5v 2HQ1s 2GC5v 2GB5v 2GD4v 2HQ2s 2cA 2GC6v 2eA3 2GD5s 2cB 2HQ3v 2lA 2HQ0s 2eB2 2GC7s 2lB 2GD6s 2rA 2gA01v 2cC 2gA00s 2rB 2eB1 2gB00v 2GD7s 2cD 2lC 2eB0 2gB01s 2eB3 2zA 2mA1 2gC01v 2gC00s 2eA2 2mA3 2lD 2rC 2fA1s 2zB 2gD01s 2mA2 2mA0 2mB0 2fA2s 2mB3 2gD00v 2fA3v 2fA0s 2mB2 2fB0s 2fB2s 2RA 2zC 2eC1 2fB3v 2mB1 2eC2 "
+    "3qA 2fB1s 2RB 2pA0s 2RC 2eC3 2eC0 2mC2 3CAy 2rD 2mC1 2mC0 2mC3 3qB 2fC0v 2fC2s 3CBy 2fC1s 3uA 3uB 2fC3s 3yAs 2pB0v 3yBs 3qC 3uC 3YAs 3S1y 2RD 2pC0v 3yCs 3S0y 2pD0v 3S2y 3YBy 3CCy 3S3y 3YCs 2Ts")
 
 SCRATCH = {
     "fz": ("sbuf", [128, 4 * (H + 2 * C)], B16), "xt": ("sbuf", [128, 4 * C], B16),
@@ -34,33 +24,28 @@ SCRATCH = {
     "uq": ("sbuf", [128, 128], X4), "us": ("sbuf", [128, 128], U8),
     "vq": ("sbuf", [128, 128], X4), "vs": ("sbuf", [128, 128], U8),
     "one": ("sbuf", [128, 516], B16), "et": ("sbuf", [128, 516], B16), "eq": ("sbuf", [128, 512], X4), "es": ("sbuf", [128, 512], U8),
-    "c1": ("sbuf", [128, H], F32), "two": ("sbuf", [128, 16], F32), "wn": ("sbuf", [128, H], F32),
-    "tab": ("sbuf", [128, H + 16], F32), "tab0": ("sbuf", [128, H], F32),
-    "pe": ("sbuf", [128, 8 * 64], F32), "pd": ("sbuf", [128, 2 * NB], F32),
-    "k4": ("sbuf", [128, H], F32), "k16": ("sbuf", [128, H], F32), "ka": ("sbuf", [128, 64], F32), "kb": ("sbuf", [128, 64], F32),
+    "c1": ("sbuf", [128, H], F32), "two": ("sbuf", [128, 16], F32), "wn": ("sbuf", [128, H], F32), "tab": ("sbuf", [128, H + 16], F32),
+    "pe": ("sbuf", [128, 8 * 64], F32),
+    "k4": ("sbuf", [128, 128], F32), "k16": ("sbuf", [128, 128], F32), "ka": ("sbuf", [128, 64], F32), "kb": ("sbuf", [128, 64], F32),
     "dl": ("sbuf", [128, NB], I32), "du": ("sbuf", [128, NB], U16),
-    "pa": ("sbuf", [128, 2], I32), "pm": ("sbuf", [128, 2], I32), "pf": ("sbuf", [128, 2], F32),
-    "p4": ("sbuf", [128, 2], I32), "p4f": ("sbuf", [128, 2], F32), "pb": ("sbuf", [128, 2], F32),
-    "top": ("sbuf", [128, 2], F32), "ca": ("sbuf", [128, 2], F32), "cb": ("sbuf", [128, 16], F32), "c4": ("sbuf", [128, 2], F32),
-    "c16": ("sbuf", [128, 2], F32), "pg": ("sbuf", [128, 2], F32), "pw": ("sbuf", [128, 16], F32),
-    "ul": ("sbuf", [128, 8], I32), "lu": ("sbuf", [128, 8], U16),
-    "l4": ("sbuf", [128, C // 4], U16), "l16": ("sbuf", [128, 32], U16),
+    "pa": ("sbuf", [128, 2], I32), "pm": ("sbuf", [128, 2], I32), "p4": ("sbuf", [128, 2], I32),
+    "cb": ("sbuf", [128, 16], F32), "pw": ("sbuf", [128, 16], F32),
+    "ul": ("sbuf", [128, 8], I32), "lu": ("sbuf", [128, 8], U16), "L0": ("sbuf", [128, 8], U16),
+    "l4": ("sbuf", [128, C // 4], U16), "l16": ("sbuf", [128, NB], U16),
     "roots": ("sbuf", [128, H + 2 * C], F32),
     "ps": ("psum", [128, 4096], F32),
 }
-for _n in ("par", "cr", "at", "ap", "yr", "pr", "kr", "fr", "hit", "sd", "sc", "ex", "yt"):
+for _n in ("par", "cr", "at", "ap", "yr", "pr", "kr", "fr", "hit", "sd", "sc", "sr", "ex", "yt"):
     SCRATCH[_n] = ("sbuf", [128, C], F32)
-for _n in ("ta", "tb", "xa", "xb", "out"):
+for _n in ("pd", "h0", "h1", "h2"):
+    SCRATCH[_n] = ("sbuf", [128, 2 * NB], F32)
+for _n in ("ta", "tb", "xa", "xb", "out", "tm"):
     SCRATCH[_n] = ("sbuf", [128, NB], F32)
-for _h, _p in enumerate("AB"):
-    _s = shape(_h)
-    SCRATCH["way" + _p] = ("sbuf", [128, _s[6] + _s[2]], F32)
-    SCRATCH["t" + _p] = ("sbuf", [128, 16], F32)
+for _n in ("pf", "p4f", "pb", "top", "ca", "cc", "cd", "c4", "c16", "pg"):
+    SCRATCH[_n] = ("sbuf", [128, 2], F32)
+for _p, (_a, _b) in SPANS.items():
+    SCRATCH["way" + _p] = ("sbuf", [128, H + 2 * (_b - _a)], F32)
     SCRATCH["L" + _p] = ("sbuf", [128, 16], U16)
-    for _n, _k in (("a", 2), ("b", 4), ("c", 2)):
-        SCRATCH["j%s%s" % (_n, _p)] = ("sbuf", [128, _k], U16)
-        SCRATCH["r%s%s" % (_n, _p)] = ("sbuf", [128, 16 * _k], F32)
-        SCRATCH["s%s%s" % (_n, _p)] = ("sbuf", [128, 16 * _k], F32)
 for _i in range(3):
     SCRATCH["hq%d" % _i] = ("sbuf", [128, H], X4)
     SCRATCH["hs%d" % _i] = ("sbuf", [128, H], U8)
@@ -164,10 +149,10 @@ def rank_program(g, core, T, topo):
         else:
             emit("s", [acc(out)], ins, lambda e: e.activation(view(out), source(in_, by), Act.Copy, bias=bias, scale=scale))
 
-    def small(out, in_, s1, s2, *ops, by=None):
+    def small(out, in_, s1, s2, *ops):
         a1, a2 = [T[s][:, 0:1] if isinstance(s, str) else view(s) if isinstance(s, tuple) else s for s in (s1, s2)]
-        ins = [acc(in_)] + [acc(s) for s in (s1, s2) if isinstance(s, (str, tuple))] + ([acc(by)] if by else [])
-        emit("v", [acc(out)], ins, lambda e: e.tensor_scalar(view(out), source(in_, by), a1, a2, *ops))
+        ins = [acc(in_)] + [acc(s) for s in (s1, s2) if isinstance(s, (str, tuple))]
+        emit("v", [acc(out)], ins, lambda e: e.tensor_scalar(view(out), view(in_), a1, a2, *ops))
 
     def both(out, a, b, op):
         emit("v", [acc(out)], [acc(a), acc(b)], lambda e: e.tensor_tensor(view(out), view(a), view(b), op))
@@ -208,9 +193,8 @@ def rank_program(g, core, T, topo):
         name, a, b = out
         copy("s", out, ("wn", 0, b - a), float(step), float(first - step))
 
-    def nothing_before():
-        if rank == 0:
-            fill(("fz", 0, 4 * H), 0.0)
+    def mark_of(i):
+        return -1024 * EPS * 2 ** i
 
     E, W, U, V = ("eq", "es"), ("wq", "wp"), ("uq", "us"), ("vq", "vs")
 
@@ -221,8 +205,8 @@ def rank_program(g, core, T, topo):
 
     once("dl", load, "y", T.dl[:], acc("dl"), T.dist[:], "ldb")
     once("ut", load, "s", T.ut[:], acc("ut"), T.u[:], "ldu")
-    once("xB", load, "y", T.xt[:, 4 * SPLIT:4 * C], ("xt", 4 * SPLIT, 4 * C), T.x[:, 4 * SPLIT:4 * C], "ldxb")
-    once("xA", load, "s", T.xt[:, 0:4 * SPLIT], ("xt", 0, 4 * SPLIT), T.x[:, 0:4 * SPLIT], "ldxa")
+    once("xB", load, "y", T.xt[:, 4 * LO:4 * C], ("xt", 4 * LO, 4 * C), T.x[:, 4 * LO:4 * C], "ldxb")
+    once("xA", load, "s", T.xt[:, 0:4 * LO], ("xt", 0, 4 * LO), T.x[:, 0:4 * LO], "ldxa")
     once("wq", load, "y", T.wq[:].bitcast(dt.uint8), acc("wq"), T.wc[:], "ldw")
     once("wp", load, "y", T.wp[:], acc("wp"), T.ws[:], "ldp")
     once("vt", load, "y", T.vt[:], acc("vt"), T.v[:], "ldv")
@@ -230,61 +214,52 @@ def rank_program(g, core, T, topo):
     once("ka", iota, "ka", [[0, 16], [1, 4]], 0)
     once("kb", iota, "kb", [[0, 4], [1, 16]], 0)
     once("c1", fill, "c1", 1.0)
-    once("two", fill, "two", 2.0)
+    once("two", copy, "s", "two", ("c1", 0, 16), 2.0)
     once("pm", small, "pm", "pa", 15, None, Op.bitwise_and)
     once("wn", scan, "wn", "c1", "c1", 0.0, Op.mult, Op.add)
     once("pf", copy, "v", "pf", "pm")
-    once("tab1", scan, ("tab", H, H + 16), "two", ("c1", 0, 16), -512 * EPS, Op.mult, Op.min)
+    once("tab1", scan, ("tab", H, H + 16), "two", ("c1", 0, 16), mark_of(-1), Op.mult, Op.min)
+    once("tab0", copy, "s", ("tab", 0, H), "wn", -EPS, EPS)
     once("p4", small, "p4", "pm", 2, None, Op.arith_shift_right)
-    once("tabi", iota, "tab0", [[32, 16], [1, 16]], 0)
-    once("tab0", copy, "s", ("tab", 0, H), "tab0", -EPS)
-    once("pd", fill, "pd", 2.0 ** 20)
+    once("pd", copy, "s", "pd", ("c1", 0, 2 * NB), FAR)
     once("top", small, "top", "pf", 15.0, None, Op.is_lt)
-    once("pg", small, "pg", "pf", float(H), None, Op.add)
+    once("pg", copy, "s", "pg", "pf", 1.0, float(H))
     once("pw0", small, "pw", ("kb", 0, 16), "pf", None, Op.is_equal)
     once("p4f", copy, "v", "p4f", "p4")
-    once("ca", small, "ca", "top", -2.0 ** 20, None, Op.mult)
+    once("ca", copy, "s", "ca", "top", -FAR)
     once("pw1", both, "pw", "pw", ("tab", H, H + 16), Op.mult)
     once("ap", small, ("ap", 15, C, 16), ("c1", 0, NB), "top", 2.0 ** 90, Op.mult, Op.mult)
     once("cb", scan, "cb", "pw", "pw", 0.0, Op.min, Op.min)
+    once("cc", copy, "s", "cc", "top", -FAR, -mark_of(14))
+    once("cd", copy, "s", ("cd", 0, 1), ("cb", 15, 16), 1.0, -mark_of(14))
+    once("h0", copy, "s", ("h0", 0, 2 * NB - 1, 2), ("c1", 0, NB), -FAR)
+    once("h1", copy, "s", ("h0", 1, 2 * NB, 2), ("c1", 0, NB), mark_of(13))
     once("one", fill, "one", 64.0)
     once("ul", iota, "ul", [[16, 8]], 0)
     once("et", emit, "p", [acc("et")], [acc("one")], lambda e: e.affine_select(T.et[:], T.one[:], [[-1, 516]], Op.is_equal, 0.0, 3, 4))
-    once("k16", small, ("k16", 0, 64), "kb", "pf", -2.0 ** 20, Op.is_equal, Op.mult)
-    once("k4", small, ("k4", 0, 64), "ka", "p4f", -2.0 ** 20, Op.is_equal, Op.mult)
+    once("k16", small, ("k16", 0, 64), "kb", "pf", -FAR, Op.is_equal, Op.mult)
+    once("k4", small, ("k4", 0, 64), "ka", "p4f", -FAR, Op.is_equal, Op.mult)
     once("k16a", copy, "s", ("k16", 0, 64), ("k16", 0, 64), 1.0, HOLD)
     once("k4a", copy, "s", ("k4", 0, 64), ("k4", 0, 64), 1.0, HOLD)
-    for c in range(64, H, 64):
-        once("k4w%d" % c, copy, "s", ("k4", c, c + 64), ("k4", 0, 64))
-        once("k16w%d" % c, copy, "s", ("k16", c, c + 64), ("k16", 0, 64))
+    once("k4w", copy, "s", ("k4", 64, 128), ("k4", 0, 64))
+    once("k16w", copy, "s", ("k16", 64, 128), ("k16", 0, 64))
     for c in range(0, H + C, H):
         once("id%d" % c, ramp, ("roots", c, min(c + H, H + C)), c - H, 1)
-    once("c16", small, "c16", "pf", -HOLD, 15 * HOLD, Op.mult, Op.add)
-    once("pb", small, "pb", "p4f", 4 * HOLD - 4.0, -12 * HOLD, Op.mult, Op.add)
+    once("c16", copy, "s", "c16", "pf", -HOLD, 15 * HOLD)
+    once("pb", copy, "s", "pb", "p4f", 4 * HOLD - 4.0, -12 * HOLD)
     once("c4", both, "c4", "pb", "pf", Op.add)
     once("lu", copy, "v", "lu", "ul")
-    once("sd", fill, "sd", -EPS)
-    once("nil", nothing_before)
-    for h, p in enumerate("AB"):
-        a, b, n, k, runs, span, base = shape(h)
-        c, d = a // 16, b // 16
-        once("ta" + p, iota, ("ta", c, d), [[16, k], [32, runs]], n)
+    once("sd0", copy, "s", ("sd", 0, H), "c1", -EPS)
+    once("sd1", copy, "s", ("sd", H, C), ("c1", 0, C - H), -EPS)
+    for p, (a, b) in SPANS.items():
+        n, c, d = b - a, a // 16, b // 16
+        once("ta" + p, iota, ("ta", c, d), [[16, d - c]], n)
         once("tb" + p, copy, "s", ("tb", c, d), ("ta", c, d), -EPS)
-        once("sd" + p, copy, "s", ("sd", a + 15, b, 16), ("wn", 0, n // 16), 16 * EPS, -1.0 - EPS * n)
+        once("sd" + p, copy, "s", ("sd", a + 15, b, 16), ("wn", 0, d - c), 16 * EPS, -1.0 - EPS * n)
         once("lit" + p, ramp, ("way" + p, 0, n), H + b - 1, -1)
-        cuts = sorted({0, 16} | {min(16, max(0, (H - a - span * x) // 16)) for x in range(k)})
+        cuts = sorted({0, H, max(0, H - a)})
         for x, y in zip(cuts, cuts[1:]):
-            e0, e1 = [e + (H if e < 0 else H + C) for e in (a - H + 16 * x, a - H + 16 * x + span)]
-            once("far%s%d" % (p, x), iota, ("way" + p, n + 32 * x, n + 32 * y), [[16, y - x], [e1 - e0, 2], [1, 16]], e0)
-        once("t" + p, fill, "t" + p, 0.0)
-        for x, m, pattern, first in (("a", runs * k, [[1, runs], [runs, k]], 0),
-                                     ("b", n // 4, [[16, k], [16 * k, runs], [4, 4]], 3), ("c", runs * k, [[16, k], [16 * k, runs]], 15)):
-            w, y = -(-m // 16) * 16, x + p
-            once("r" + y, iota, ("r" + y, 0, m), pattern, first)
-            if w > m:
-                once("z" + y, fill, ("r" + y, m, w), 0.0)
-            once("s" + y, scan, ("s" + y, 0, w), ("k16", 0, w), ("r" + y, 0, w), 0.0, Op.add, Op.max)
-            once("j" + y, small, ("j" + y, 0, w // 16), ("s" + y, 15, w, 16), "c16", None, Op.subtract)
+            once("far%s%d" % (p, x // 16), iota, ("way" + p, n + x, n + y), [[1, y - x]], a + x + (0 if a + x < H else C))
 
     def send(t, x):
         if rank + 1 == n_ranks:
@@ -312,22 +287,16 @@ def rank_program(g, core, T, topo):
     def col(name, i):
         return (name, i, C, 16)
 
-    def mark_of(i):
-        return -1024 * EPS * 2 ** i
-
     def step(word):
         t, name = int(word[0]), word[1:]
         q = ("q%d" % t, "s%d" % t)
-        kind, h = name[0], "AB".find(name[1:2])
-        p = name[1:2]
-        a, b, n, k, runs, span, base = shape(max(h, 0))
-        if kind in "qudszemfyYC" and p in "ABC":
-            h = "ABC".find(p)
-            a, b = CUTS[h]
-            n = b - a
+        kind, p, qn = name[0], name[1:2], name[-1]
+        where = CUTS if kind in "qudszemfyYC" else SPANS
+        a, b = where.get(p, (0, C))
+        n, h = b - a, "ABCD".find(p)
+        base = n + H
         digits = "".join(c for c in name if c.isdigit())
         i = int(digits) if digits else None
-        qn = name[-1]
         if kind == "D":
             small("du", "dl", -1.0, "pg", Op.mult, Op.add)
         elif kind == "n":
@@ -339,11 +308,13 @@ def rank_program(g, core, T, topo):
         elif name == "Wc":
             both(col("fr", 14), col("pr", 14), col("par", 14), Op.add)
         elif name == "Wd":
-            both(col("yr", 14), col("yr", 13), col("par", 14), Op.subtract)
-        elif name == "We":
-            both(col("kr", 14), col("yr", 14), col("yr", 15), Op.max)
+            both(("h1", 0, 2 * NB - 1, 2), col("par", 13), col("par", 14), Op.subtract)
         elif kind == "N":
-            copy(qn, col("yr", 2 * i - 13), col("par", i), 1.0, -mark_of(i))
+            copy(qn, ("h1", 1, 2 * NB, 2), col("par", 14))
+        elif name == "We":
+            scan("h2", "h0", "h1", 0.0, Op.add, Op.max)
+        elif name == "Wh":
+            small(col("yr", 14), col("par", 15), "cc", ("cd", 0, 1), Op.add, Op.max)
         elif name == "Wf":
             both("xa", col("cr", 0), at(0), Op.subtract)
         elif name == "Wg":
@@ -363,7 +334,8 @@ def rank_program(g, core, T, topo):
         elif kind == "F":
             both(("pd", 1, 2 * NB, 2), col("cr", i - 1), at(i), Op.subtract)
         elif kind == "B":
-            both(("pe", 32 * i + 3, 32 * i + 2 + 2 * NB, 2), col("kr", i), at(i), Op.add)
+            x, y = (("h2", 1, 2 * NB, 2), col("yr", 14)) if i == 14 else (col("kr", i), at(i))
+            both(("pe", 32 * i + 3, 32 * i + 2 + 2 * NB, 2), x, y, Op.add)
         elif kind == "w":
             scan(("pe", 32 * i - 63, 32 * i - 63 + 2 * NB), "pd", ("pe", 32 * i + 2, 32 * i + 2 + 2 * NB), 0.0, Op.max, Op.min)
         elif kind == "b":
@@ -375,29 +347,28 @@ def rank_program(g, core, T, topo):
                  lambda e: e.tensor_tensor(T.hit[:, a:b], view(psum(UB[h], n)), T.ap[:, a:b], Op.is_ge))
         elif kind == "s":
             scan(("sc", a, b), ("hit", a, b), ("sd", a, b), 0.0, Op.max, Op.add)
+        elif kind == "I":
+            small(("L0", 2 * h, 2 * h + 1), ("sc", a + 15, a + 16), ("out", a // 16, a // 16 + 1), -1.0 / EPS, Op.max, Op.mult)
         elif kind == "t":
-            both(("t" + p, 0, n // 16), ("sc", a + 15, b, 16), ("out", a // 16, b // 16), Op.max)
+            both(("tm", a // 16, b // 16), ("sc", a + 15, b, 16), ("out", a // 16, b // 16), Op.max)
         elif kind == "L":
-            small("L" + p, "t" + p, -1.0 / EPS, None, Op.mult, by=("ja" + p, 0, 1))
+            small(("L" + p, 0, n // 8 - 1, 2), ("tm", a // 16, b // 16), -1.0 / EPS, None, Op.mult)
         elif kind == "G":
-            c = base + 16 * k * i
-            copy(qn, ("way" + p, c, c + 16 * k), ("way" + p, 0, c), by=("L" + p, k * i, k * i + k))
+            c = base + 16 * i
+            copy(qn, ("way" + p, c, c + 16), ("way" + p, 0, c), by=("L" + p, 2 * i, 2 * i + 1) if i else ("L0", 2 * h, 2 * h + 1))
         elif kind == "c":
             scan(("ex", a, b), ("k4", 0, n), ("way" + p, base, base + n), 0.0, Op.add, Op.max)
         elif kind == "l":
-            small(("l4", a // 4, b // 4), ("ex", a, b), 4.0, "c4", Op.mult, Op.add, by=("jb" + p, 0, n // 64))
+            small(("l4", a // 4, b // 4), ("ex", a + 3, b, 4), 4.0, "c4", Op.mult, Op.add)
         elif kind == "g":
-            s, piece = int(name[2]), int(name[3])
-            c0 = a + span * s
-            c, d = [c0 + span * x // PIECES for x in (piece, piece + 1)]
-            copy(qn, ("fz", 4 * (H + C + c), 4 * (H + C + d)), ("fz", 0, 4 * (H + C + c0)), by=("l4", c // 4, d // 4))
+            c, d = a + n // 2 * i, a + n // 2 * (i + 1)
+            copy(qn, ("fz", 4 * (H + C + c), 4 * (H + C + d)), ("fz", 0, 4 * (H + C + a)), by=("l4", c // 4, d // 4))
         elif kind == "r":
-            scan(("sc", a, b), ("k16", 0, n), ("way" + p, base, base + n), 0.0, Op.add, Op.max)
+            scan(("sr", a, b), ("k16", 0, n), ("way" + p, base, base + n), 0.0, Op.add, Op.max)
         elif kind == "R":
-            small(("l16", 16 * h, 16 * h + 16), ("sc", a, b), "c16", None, Op.subtract, by=("jc" + p, 0, 1))
+            small(("l16", a // 16, b // 16), ("sr", a + 15, b, 16), "c16", None, Op.subtract)
         elif kind == "p":
-            c = H + C + a + span * i
-            copy(qn, ("roots", c, c + span), ("roots", 0, c), by=("l16", 16 * h + runs * i, 16 * h + runs * i + runs))
+            copy(qn, ("roots", H + C + a, H + C + b), ("roots", 0, H + C + a), by=("l16", a // 16, b // 16))
         elif kind == "o":
             product(OB + i, E, 128 * i, q, 0, C)
         elif kind == "O":
@@ -406,8 +377,11 @@ def rank_program(g, core, T, topo):
             if rank > 0:
                 product(HB + i, E, 128 * i, ("hq%d" % t, "hs%d" % t), *SENDS[p])
         elif kind == "H":
+            a, b = SENDS[p]
             if rank > 0:
-                unpack(qn, ("fz", 4 * SENDS[p][0] + i, 4 * SENDS[p][1], 4), HB + i, SENDS[p][1] - SENDS[p][0])
+                unpack(qn, ("fz", 4 * a + i, 4 * b, 4), HB + i, b - a)
+            elif t == 0:
+                copy(qn, ("fz", 4 * a + i, 4 * b, 4), ("c1", 0, b - a), 0.0)
         elif kind == "e":
             product(EB[h] + i, E, 128 * i, q, a, b, True, False)
         elif kind == "z":

@@ -1,22 +1,32 @@
 from concourse.mybir import AluOpType as Op, ActivationFunctionType as Act, dt
 
-F32, B16, I32, U16, U8, X4 = "float32", "bfloat16", "int32", "uint16", "uint8", "float8_e4m3fn_x4"
+F32, F16, B16, I32, U16, U8, X4 = "float32", "float16", "bfloat16", "int32", "uint16", "uint8", "float8_e4m3fn_x4"
 C, H, R = 448, 256, 3
 LO = C - H
-SPANS = {"A": (0, 96), "B": (96, 192), "C": (192, 320), "D": (320, C)}
-CUTS = {"A": (0, 192), "B": (192, 320), "C": (320, C)}
-SENDS = {"P": (0, 128), "Q": (128, 256)}
-UB, OB, HB, EB = (0, 1, 2), 4, 0, (4, 0, 4)
 NB = C // 16
+SPANS = ((0, 64), (64, 128), (128, 224), (224, 320), (320, C))
+QC = ((0, 128), (128, 320), (320, C))
+TC = ((0, 128), (128, 320), (320, C))
+ZC = ((0, 128), (128, 320), (320, C))
+FC = ((0, 128), (128, 320), (320, C))
+OC = ((0, 128), (128, 320), (320, C))
+XC = ((0, 128), (128, 256))
+HC = ((0, 128), (128, 256))
 EPS, BIG, HOLD, FAR = 2.0 ** -11, 2.0 ** 64, 2048.0, 2.0 ** 20
 ORDER = (
-    "-c1 -h0 -pa -pm -dl -sd0 -xB -h1 -wn -kb -two -taD -pf -p4 -one -pd -p4f -top -pg -tab0 -ca -tab1 -ka -ut -tbD -pw0 -pw1 -ul -sd1 -xA 0D -cb 0n1v -k4 0n0s -sdC -cc -taB -lu -cd 0C11s 0qB -farC0 0N14s 0C13s 0Wd 0Wa 0C7s 0C3s -taC 0Wh 0j12 0C9s 0We 0F14 0j8 -litA 0j4 0J12 0C5s 0B14 -sdA 0j10 0K12s 0qC 0w14 0J8 -tbB 0j6 -taA 0J10 0B12 0C1s 0F12 0a12s 0i0 0J6 0C6s 0w12 0j2 0K10s 0C0s 0K8s -k4a 0C12s -sdD 0Wb 0J4 -et 0F10 0C10s -id256 0B10 0b12 0E1 0K6s 0w10 0i2 0a10s 0F8 0B8 -tbA 0C8s 0a14s 0xP 0xQ -litD 0qA 0C2s -id0 -litB 0w8 0E2 0b10 -farD0 0B6 -tbC 0K4s 0F6 0E3 0Wc 0w6 -k4w 0i1 0oP2 0J2 0M12 -farA0 0b6 0B4 -sdB 0F4 0a8s 0E0 -farB0 0C4s 0K2s 0b8 0uA 0w4 0b4 0M6 0M14 0hP3 0a6s 0OP2s 0HP3s 0oP1 -wp -litC 0F2 0uC 0B2 0a13s 0a11s 0b2 0a5s 0M4 0a2s 0M8 -pb 0M10 0uB 0w2 0M2 0a4v -farC4 0a7v -ap 0a3s 0Wf 0a9s 0a0s 0oP0 0oP3 0a1v -c4 0Wg 0dA 0hP0 0OP1s 0OP3s 0hQ3 0OP0s 0dB 0Wi 0sA 0dC 0sB -farB10 0hP2 0IA0 0eA3 0tA 0tB 0IB0 0IC0 -vt 0GA0s 0hP1 0tC 0GB0s 0GC0s 0LA 0LB 0sC 0GA1s 0LC 0GB1v 0ID0 0tD 0HP0s 0GC1s 0GA2v 0GB2v 0eA1 0GD0s 0LD 0GC2s 0GA3v 0GB3v 0HP1s 0GD1v 0HP2s 0GA4v 0GC3v 0GD2v 0GA5v 0GB4s 0hQ0 0HQ0s 0hQ2 0GB5v 0GC4s 0hQ1 0HQ2s 0GD3v 0eA0 0cA 0cB -wq 0eB2 0GC5v 0HQ3s 0HQ1s 0GD4s 0lA 0lB 0GC6v 0gA00v 0gA01s 0eB1 0GD5s 0gB01v 0GD6v 0GC7s 0cC 0gB00s 0zA 0eA2 0GD7s 0lC -c16 0eB3 0gC01s 0mA3 0eB0 0mA2 0mA0 0mA1 0cD 0gC00v 0lD 0fA3s 0fA2s 0eC3 2v 0zB 0gD00v 0mB2 0fA1v 0mB1 0gD01s 0fA0s 0mB3 0mB0 0eC2 0eC1 0zC 0fB1v 0eC0 "
-    "1qA 0mC1 0fB2s 0fB3s 0mC3 0fB0s 0fC1s 0fC3s -k16 0mC0 1qB 0mC2 1uA 0fC2v 1uB 1dA 0fC0s 1qC 1uC 1sA 1dB 1IA0 1xP 1IB0 1sB 1tA 1oP0 1tB 1dC 1LA 1tC 1GA0s 1IC0 1oP1 1OP0s 1sC 1GB0v 1LC 1xQ 1GA1s 1LB 1oP3 1oP2 1GC0s 1hP3 1hP2 1hP0 1ID0 1tD 1OP1s 1GA2v 1GA3s 1GC1v 1GC2s 1GB1v 1LD 1GD0v 1GB2s 1OP3v 1HP3v 1GD1s 1GC3s 1eA0 1GA4s 1GB3v 1hP1 1GD2v 1hQ3 1HP0s 1hQ0 1GC4s 1HP2v 1GA5s 1HP1v 1GD3v 1GC5v 1cA 1GB4s 1OP2s 1HQ0s 1hQ2 1GD4v 1hQ1 1GB5s 1eB0 1HQ3v 1GC6v 1eA3 1HQ2s 1GC7s 1eB3 1lA 1HQ1v 1cB 1gA01v 1GD5s 1lB 1cC 1gA00s 1GD6s 1gB00v 1lC 1eB2 1gB01s 1GD7v 1eA1 1eB1 1zA 1cD 1gC00s 1eA2 1gC01v 1lD 1mA3 1zB 1mA0 1fA3s 1mA1 1mA2 1mB0 1gD01v 1mB2 1mB3 1fA0s 1fA2v 1gD00s 1fA1s 1mB1 1eC3 1eC0 1zC 1fB0s 1fB2s 1eC1 1eC2 1mC1 1fB1s 1mC3 1fB3s -k16a "
-    "2qA 1mC2 -id512 1mC0 2qB 1fC1v 1fC0v 2uA 2dA 1fC3s 1fC2s 2uB 2qC 2dB 2xP 2uC 2sA -k16w 2sB 2dC 2oP0 2tB 2OP0s 2IB0 2IC0 2oP1 2oP3 2tC 2oP2 2sC 2tA 2IA0 2LC 2hP1 2GB0s 2GC0v 2hP2 2ID0 2OP1s 2xQ 2hP0 2LA 2GA0v 2hP3 2GD0s 2eA1 2LB 2GC1v 2OP2s 2tD 2GA1v 2HP1s 2HP2s 2eA0 2GB1v 2GC2v 2hQ1 2LD 2HP0s 2GA2v 2HP3s 2GB2v 2GC3v 2hQ2 2GD1v 2GA3v 2hQ3 2hQ0 2GB3v 2GD2v 2GA4v 2GC4v 2OP3s 2GB4v 2GD3v 2GA5v 2HQ1s 2GC5v 2GB5v 2GD4v 2HQ2s 2cA 2GC6v 2eA3 2GD5s 2cB 2HQ3v 2lA 2HQ0s 2eB2 2GC7s 2lB 2GD6s 2rA 2gA01v 2cC 2gA00s 2rB 2eB1 2gB00v 2GD7s 2cD 2lC 2eB0 2gB01s 2eB3 2zA 2mA1 2gC01v 2gC00s 2eA2 2mA3 2lD 2rC 2fA1s 2zB 2gD01s 2mA2 2mA0 2mB0 2fA2s 2mB3 2gD00v 2fA3v 2fA0s 2mB2 2fB0s 2fB2s 2RA 2zC 2eC1 2fB3v 2mB1 2eC2 "
-    "3qA 2fB1s 2RB 2pA0s 2RC 2eC3 2eC0 2mC2 3CAy 2rD 2mC1 2mC0 2mC3 3qB 2fC0v 2fC2s 3CBy 2fC1s 3uA 3uB 2fC3s 3yAs 2pB0v 3yBs 3qC 3uC 3YAs 3S1y 2RD 2pC0v 3yCs 3S0y 2pD0v 3S2y 3YBy 3CCy 3S3y 3YCs 2Ts")
+    "-pap -c1v -kbp -kap -pmv -dly -sdv -pds -twos -pfv -pgs -wnv -tab1v -wps -h1s -pw0v -onev -ulp -pw1v -ta1p -h0s 0D -tab0s 0n0s -topv -ccs -p4v -cas -cbv -x1y -ta4p -cds 0n1v -vts 0Nes 0Abs 0A9s 0A8s -x0y 0Ads 0q1 0A7s 0W3 -luv 0W0 0W5 0W4 -se0s -wqs 0jc -etp -uty 0ja 0aes 0Fe -id1s -se3s 0Be 0A3s 0Jc 0i0 0we 0A1s 0Ja 0x0 0W1 0j8 0Kcs 0Fc 0Bc -lit4p 0i2 0wc 0J8 0q2 -se4s 0Fa 0A5s -se2s 0Kas 0A0s 0x1 0Ba 0acs 0j6 0Aas -id2s 0q0 0wa 0E3 -idhs 0K8s 0j4 0F8 0i1s 0B8 0A4s 0J6 -far4s 0E0 0w8 0A6s 0o031 -lit3p 0K6s 0O03s 0Acs -far2p 0J4 -far3p 0E1 0h033 0h002 0K4s 0o007 0F6 0B6 0a6s 0H03s 0o105 -ta3p 0a8s -p4fv 0j2 0bc 0h016 -ta0p 0b8 0w6 0ba 0J2 0W2 -lit0p 0h103 0F4 0B4 0M8 0E2 0O00s 0A2s -ta2p 0o010 0w4 -far1p 0H00s -se1s 0H01s 0a4s 0b6 0u01 0Ma 0Mc 0b4 0h126 0K2s 0B2 0H10s 0F2 0a7s 0b2 0O01s 0O10s 0o113 0M6 0a9s 0aas 0H12s 0a2s 0a5s 0M4 0Me 0u17 0u25 0w2 0M2 0abs -apv -k4v 0o022 0W6 0a3s 0a0v -lit2p 0ads -far0p 0a1s 0o124 0V 0W7 0d0 0h020 0d1 -tbs 0h116 0d2 0s0 0W8 0O11s -k4as 0H11s 0s1 0s2 0h136 0I0 0O12s 0H02s 0O02s -lit1p 0o131 -pbs 0H13s 0O13s 0t0 0G00s 0I2 0G20s 0t1 0I1 -id0p 0I3 0L0 0G10s 0G30s 0t2 0o235 0L1 0I4 -k16v 0G01v 0G21s 0G11s 0G31s 0e134 0G22s 0G12s 0L2 0G40v -k4bv 0e112 0G02v 0o207 0G41v 0G03s 0O20v 0G32v 0G23s 0G42v -c4v 0G13s 0c0 0G33s 0o223 0G24v 0c1 0l0 0G25v 0G43s 0G34s 0l1 0G44s 0g01v 0g00s 0o216 0c2 0O23v 0G45s 0G35s 0g10v 0g11s 0G46v 0l2 0c3 0O22s 0z0 0O21s 0G47s 0g21v 0e027 0l3 0e011 0c4 0g20s 0m01 0m02 0g31v -k16as 0f02v 0e003 0l4 0m00 0e035 0m03 0g30s 0z1 0f01s 0e107 0e121 0e236 0m12 0m13 0m10 0f00s 0f03s 0g40v "
+    "1q0 0m11 0g41s 0f12s 0e203 0z2 0f13s 0f11s 0e220 0f10v 1u05 -k16bs 0m22 0m20 1d0 0m23 0f22s 0f20s 1q1 0e217 1s0 0m21 0f23s 1o031 0f21v 1o025 1I0 1t0 1O03s 1q2 1o004 1u10 1o103 1x0 1d1 1O00s 1G00s 1o122 1I1 1o016 1O02v 1O10s 1o137 1L0 1O12s 1u24 1O13s 1s1 1o111 1G10v 1d2 1G01s 1I3 1o203 1o217 1I2 1t1 1o232 1s2 1x1 1O01s 1h005 1O11v 1L1 1I4 1G11s 1h016 1t2 1G02s 1G20s 1G30s 1O20s 1G12v 1O23s 1h030 1h023 1G21v 1G03s 1G40s 1G31v 1L2 1O21v 1H00v 1H03v 1h131 1G13s 1h114 1G22s 1h102 1G32s 1G41v 1H02s 1G23s 1G33s 1c0 1c1 1H01v 1h125 1H13v 1G42s 1l0 1G24v 1e017 1H11s 1H10s 1G43s 1H12v 1e223 1l1 1G34v 1G25v 1o224 1e000 1e021 1g00v 1g01s 1c2 -c16s 1G44s 1g11s 1G45s 1O22s 1G46s 1G35v 1g10v 1l2 1c3 1z0 1e202 1g21s 1g20v 1m01 1m00 1e036 1G47v 1l3 1g30s 1c4 1m03 1f03s 1e104 1g31v 1m02 1l4 1f02s 1f01s 1g41s 1e125 1e116 1z1 1g40v 1e131 1m13 1f00v 1f13s 1z2 1m11 1f11s 1m12 1m10 1f10s 1e210 1e237 1m20 1f12v 1f20s "
+    "2q0 1m23 1f23s 2q1 1m21 1m22 2u05 1f21v 2o011 2o034 1f22s 2d0 2q2 2O01s 2O03s 2o026 2u17 2s0 2O02s 2d1 2I1 2o122 2O12s 2o130 2O13s 2I0 2t0 2u25 2s1 2d2 2G10s 2L0 2I2 2x0 2t1 2s2 2o103 2G00s 2o117 2o004 2I3 2G11v 2O10s 2o215 2h010 2G01s 2L1 2G20s 2t2 2I4 2O00s 2G02s 2G21s 2G40s 2h036 2G30v 2G12v 2O11v 2G31s 2G03s 2L2 2H03s 2H01s 2O21v 2G22v 2G32s 2h001 2G41v 2G13v 2x1 2G23s 2G42s 2h132 2h114 2H11s 2h105 2h127 2h026 2G24s 2c0 2H00v 2G43s 2H13v 2H10s 2e020 2c1 2G33v 2H12v 2o221 2G25s 2H02v 2O22s 2o236 2l0 2g00s 2G34v 2G44v 2G35s 2O23s 2l1 2o201 2g01v 2G45v 2e105 2r0 2c2 2g11s 2r1 2g10v 2l2 2c3 2R0 2z0 2G46s 2e017 2g21v 2O20s 2l3 2G47s 2g20s 2r4 2p0s 2e034 2c4 2g30v 2m02 2g31s 2m01 2f01s 2f02s 2l4 2e006 2g40s 2m03 2R1 2m00 2f00s 2f03s 2r2 2e122 2z1 2g41v 2e133 2e110 2e207 2m11 2r3 2R4 2m10 2R2 2m13 2p1s 2f10s 2z2 2f13v 2m12 2f12s 2p2s "
+    "3q0 2R3 2f11v 2e224 2e231 2e216 2m22 2m23 2f23s 2m21 2f22v 2f21s 2p3s 2m20 3u00 2f20v 3q1 3q2 3S3y 3u15 3C1s 3y0s 2p4v 3C2s 3C0y 3u22 3S0s 3y1s 3S1y 3Y0s 3y2v 3Y1s 3Y2y 2Ts 3S2y")
+
+
+def front(a):
+    x, y = [c for c in OC if c[0] <= a < c[1]][0]
+    return C - y, x
+
 
 SCRATCH = {
-    "fz": ("sbuf", [128, 4 * (H + 2 * C)], B16), "xt": ("sbuf", [128, 4 * C], B16),
+    "xt": ("sbuf", [128, 4 * C], B16),
     "zq": ("sbuf", [128, C], X4), "zs": ("sbuf", [128, C], U8),
     "wq": ("sbuf", [128, 512], X4), "wp": ("sbuf", [128, 512], U8),
     "ut": ("sbuf", [128, 512], B16), "vt": ("sbuf", [128, 512], B16),
@@ -30,12 +40,13 @@ SCRATCH = {
     "dl": ("sbuf", [128, NB], I32), "du": ("sbuf", [128, NB], U16),
     "pa": ("sbuf", [128, 2], I32), "pm": ("sbuf", [128, 2], I32), "p4": ("sbuf", [128, 2], I32),
     "cb": ("sbuf", [128, 16], F32), "pw": ("sbuf", [128, 16], F32),
-    "ul": ("sbuf", [128, 8], I32), "lu": ("sbuf", [128, 8], U16), "L0": ("sbuf", [128, 8], U16),
-    "l4": ("sbuf", [128, C // 4], U16), "l16": ("sbuf", [128, NB], U16),
+    "ul": ("sbuf", [128, 8], I32), "lu": ("sbuf", [128, 8], U16), "LI": ("sbuf", [128, 16], U16), "LL": ("sbuf", [128, 2 * NB], U16),
+    "l4": ("sbuf", [128, C // 4], U16), "l16": ("sbuf", [128, 64], U16),
     "roots": ("sbuf", [128, H + 2 * C], F32),
+    "hit": ("sbuf", [128, C], B16), "sd": ("sbuf", [128, C], B16), "sc": ("sbuf", [128, C], F16),
     "ps": ("psum", [128, 4096], F32),
 }
-for _n in ("par", "cr", "at", "ap", "yr", "pr", "kr", "fr", "hit", "sd", "sc", "sr", "ex", "yt"):
+for _n in ("par", "cr", "at", "ap", "yr", "pr", "kr", "fr", "sr", "ex", "yt"):
     SCRATCH[_n] = ("sbuf", [128, C], F32)
 for _n in ("pd", "h0", "h1", "h2"):
     SCRATCH[_n] = ("sbuf", [128, 2 * NB], F32)
@@ -43,20 +54,19 @@ for _n in ("ta", "tb", "xa", "xb", "out", "tm"):
     SCRATCH[_n] = ("sbuf", [128, NB], F32)
 for _n in ("pf", "p4f", "pb", "top", "ca", "cc", "cd", "c4", "c16", "pg"):
     SCRATCH[_n] = ("sbuf", [128, 2], F32)
-for _p, (_a, _b) in SPANS.items():
-    SCRATCH["way" + _p] = ("sbuf", [128, H + 2 * (_b - _a)], F32)
-    SCRATCH["L" + _p] = ("sbuf", [128, 16], U16)
-for _i in range(3):
+for _p, (_a, _b) in enumerate(SPANS):
+    SCRATCH["way%d" % _p] = ("sbuf", [128, H + 2 * (_b - _a)], F32)
+for _i in range(R):
+    SCRATCH["fz%d" % _i] = ("sbuf", [128, 4 * (H + 2 * C)], B16)
     SCRATCH["hq%d" % _i] = ("sbuf", [128, H], X4)
     SCRATCH["hs%d" % _i] = ("sbuf", [128, H], U8)
-for _i in range(4):
+    SCRATCH["t%d" % (_i + 1)] = ("sbuf", [128, 4 * C], B16)
+for _i in range(R + 1):
     SCRATCH["q%d" % _i] = ("sbuf", [128, C], X4)
     SCRATCH["s%d" % _i] = ("sbuf", [128, C], U8)
-for _i in range(1, R + 1):
-    SCRATCH["t%d" % _i] = ("sbuf", [128, 4 * C], B16)
 
-SEMAPHORES = (["cv", "cs", "ct", "cp", "sent", "ldxa", "ldxb", "ldu", "ldw", "ldp", "ldb", "ldv", "done"]
-              + ["arr%d%s" % (t, x) for t in range(R) for x in SENDS])
+SEMAPHORES = (["cv", "cs", "ct", "cp", "sent", "ldx0", "ldx1", "ldu", "ldw", "ldp", "ldb", "ldv", "done"]
+              + ["arr%d%d" % (t, x) for t in range(R) for x in range(len(XC))])
 
 
 def rank_program(g, core, T, topo):
@@ -68,6 +78,7 @@ def rank_program(g, core, T, topo):
     total = {s: 0 for s in SEMAPHORES}
     clock = {q: {} for q in queue}
     log = {}
+    banks = {}
 
     def know(q, tok):
         sem, n, snap = tok
@@ -140,8 +151,11 @@ def rank_program(g, core, T, topo):
     def source(x, by):
         return view(x) if by is None else view(x).indirect(view(by))
 
+    def scalar(s):
+        return T[s][:, 0:1] if isinstance(s, str) else view(s) if isinstance(s, tuple) else s
+
     def copy(q, out, in_, scale=1.0, bias=0.0, by=None):
-        ins = [acc(in_)] + ([acc(by)] if by else [])
+        ins = [acc(x) for x in (in_, by) if x]
         if q == "v" and (scale, bias) == (1.0, 0.0):
             emit("v", [acc(out)], ins, lambda e: e.tensor_copy(view(out), source(in_, by)))
         elif q == "v":
@@ -150,9 +164,8 @@ def rank_program(g, core, T, topo):
             emit("s", [acc(out)], ins, lambda e: e.activation(view(out), source(in_, by), Act.Copy, bias=bias, scale=scale))
 
     def small(out, in_, s1, s2, *ops):
-        a1, a2 = [T[s][:, 0:1] if isinstance(s, str) else view(s) if isinstance(s, tuple) else s for s in (s1, s2)]
         ins = [acc(in_)] + [acc(s) for s in (s1, s2) if isinstance(s, (str, tuple))]
-        emit("v", [acc(out)], ins, lambda e: e.tensor_scalar(view(out), view(in_), a1, a2, *ops))
+        emit("v", [acc(out)], ins, lambda e: e.tensor_scalar(view(out), view(in_), scalar(s1), scalar(s2), *ops))
 
     def both(out, a, b, op):
         emit("v", [acc(out)], [acc(a), acc(b)], lambda e: e.tensor_tensor(view(out), view(a), view(b), op))
@@ -189,10 +202,6 @@ def rank_program(g, core, T, topo):
         else:
             emit("p", [acc(out)], [], lambda e: e.iota(view(out), pattern, base, mult, allow_small_or_imprecise_dtypes=True))
 
-    def ramp(out, first, step):
-        name, a, b = out
-        copy("s", out, ("wn", 0, b - a), float(step), float(first - step))
-
     def mark_of(i):
         return -1024 * EPS * 2 ** i
 
@@ -203,81 +212,89 @@ def rank_program(g, core, T, topo):
     def once(word, call, *args, **kw):
         fixed["-" + word] = lambda: call(*args, **kw)
 
-    once("dl", load, "y", T.dl[:], acc("dl"), T.dist[:], "ldb")
-    once("ut", load, "s", T.ut[:], acc("ut"), T.u[:], "ldu")
-    once("xB", load, "y", T.xt[:, 4 * LO:4 * C], ("xt", 4 * LO, 4 * C), T.x[:, 4 * LO:4 * C], "ldxb")
-    once("xA", load, "s", T.xt[:, 0:4 * LO], ("xt", 0, 4 * LO), T.x[:, 0:4 * LO], "ldxa")
-    once("wq", load, "y", T.wq[:].bitcast(dt.uint8), acc("wq"), T.wc[:], "ldw")
-    once("wp", load, "y", T.wp[:], acc("wp"), T.ws[:], "ldp")
-    once("vt", load, "y", T.vt[:], acc("vt"), T.v[:], "ldv")
-    once("pa", iota, "pa", [[0, 2]], 0, 1)
-    once("ka", iota, "ka", [[0, 16], [1, 4]], 0)
-    once("kb", iota, "kb", [[0, 4], [1, 16]], 0)
-    once("c1", fill, "c1", 1.0)
-    once("two", copy, "s", "two", ("c1", 0, 16), 2.0)
-    once("pm", small, "pm", "pa", 15, None, Op.bitwise_and)
-    once("wn", scan, "wn", "c1", "c1", 0.0, Op.mult, Op.add)
-    once("pf", copy, "v", "pf", "pm")
-    once("tab1", scan, ("tab", H, H + 16), "two", ("c1", 0, 16), mark_of(-1), Op.mult, Op.min)
-    once("tab0", copy, "s", ("tab", 0, H), "wn", -EPS, EPS)
-    once("p4", small, "p4", "pm", 2, None, Op.arith_shift_right)
-    once("pd", copy, "s", "pd", ("c1", 0, 2 * NB), FAR)
-    once("top", small, "top", "pf", 15.0, None, Op.is_lt)
-    once("pg", copy, "s", "pg", "pf", 1.0, float(H))
-    once("pw0", small, "pw", ("kb", 0, 16), "pf", None, Op.is_equal)
-    once("p4f", copy, "v", "p4f", "p4")
-    once("ca", copy, "s", "ca", "top", -FAR)
-    once("pw1", both, "pw", "pw", ("tab", H, H + 16), Op.mult)
-    once("ap", small, ("ap", 15, C, 16), ("c1", 0, NB), "top", 2.0 ** 90, Op.mult, Op.mult)
-    once("cb", scan, "cb", "pw", "pw", 0.0, Op.min, Op.min)
-    once("cc", copy, "s", "cc", "top", -FAR, -mark_of(14))
-    once("cd", copy, "s", ("cd", 0, 1), ("cb", 15, 16), 1.0, -mark_of(14))
-    once("h0", copy, "s", ("h0", 0, 2 * NB - 1, 2), ("c1", 0, NB), -FAR)
-    once("h1", copy, "s", ("h0", 1, 2 * NB, 2), ("c1", 0, NB), mark_of(13))
-    once("one", fill, "one", 64.0)
-    once("ul", iota, "ul", [[16, 8]], 0)
-    once("et", emit, "p", [acc("et")], [acc("one")], lambda e: e.affine_select(T.et[:], T.one[:], [[-1, 516]], Op.is_equal, 0.0, 3, 4))
-    once("k16", small, ("k16", 0, 64), "kb", "pf", -FAR, Op.is_equal, Op.mult)
-    once("k4", small, ("k4", 0, 64), "ka", "p4f", -FAR, Op.is_equal, Op.mult)
-    once("k16a", copy, "s", ("k16", 0, 64), ("k16", 0, 64), 1.0, HOLD)
-    once("k4a", copy, "s", ("k4", 0, 64), ("k4", 0, 64), 1.0, HOLD)
-    once("k4w", copy, "s", ("k4", 64, 128), ("k4", 0, 64))
-    once("k16w", copy, "s", ("k16", 64, 128), ("k16", 0, 64))
-    for c in range(0, H + C, H):
-        once("id%d" % c, ramp, ("roots", c, min(c + H, H + C)), c - H, 1)
-    once("c16", copy, "s", "c16", "pf", -HOLD, 15 * HOLD)
-    once("pb", copy, "s", "pb", "p4f", 4 * HOLD - 4.0, -12 * HOLD)
-    once("c4", both, "c4", "pb", "pf", Op.add)
-    once("lu", copy, "v", "lu", "ul")
-    once("sd0", copy, "s", ("sd", 0, H), "c1", -EPS)
-    once("sd1", copy, "s", ("sd", H, C), ("c1", 0, C - H), -EPS)
-    for p, (a, b) in SPANS.items():
+    def either(word, *args, **kw):
+        for q in "vs":
+            once(word + q, copy, q, *args, **kw)
+
+    def ramp(word, out, first, step):
+        n = out[2] - out[1]
+        once(word + "p", iota, out, [[step, n]], first)
+        either(word, out, ("wn", 0, n), float(step), float(first - step))
+
+    for q in "ys":
+        once("dl" + q, load, q, T.dl[:], acc("dl"), T.dist[:], "ldb")
+        once("ut" + q, load, q, T.ut[:], acc("ut"), T.u[:], "ldu")
+        for i, (a, b) in enumerate(((0, LO), (LO, C))):
+            once("x%d%s" % (i, q), load, q, T.xt[:, 4 * a:4 * b], ("xt", 4 * a, 4 * b), T.x[:, 4 * a:4 * b], "ldx%d" % i)
+        once("wq" + q, load, q, T.wq[:].bitcast(dt.uint8), acc("wq"), T.wc[:], "ldw")
+        once("wp" + q, load, q, T.wp[:], acc("wp"), T.ws[:], "ldp")
+        once("vt" + q, load, q, T.vt[:], acc("vt"), T.v[:], "ldv")
+    once("pap", iota, "pa", [[0, 2]], 0, 1)
+    once("kap", iota, "ka", [[0, 16], [1, 4]], 0)
+    once("kbp", iota, "kb", [[0, 4], [1, 16]], 0)
+    once("c1v", fill, "c1", 1.0)
+    either("two", "two", ("c1", 0, 16), 2.0)
+    once("pmv", small, "pm", "pa", 15, None, Op.bitwise_and)
+    once("wnv", scan, "wn", "c1", "c1", 0.0, Op.mult, Op.add)
+    once("wnp", iota, "wn", [[1, H]], 1)
+    once("pfv", copy, "v", "pf", "pm")
+    once("tab1v", scan, ("tab", H, H + 16), "two", ("c1", 0, 16), mark_of(-1), Op.mult, Op.min)
+    either("tab0", ("tab", 0, H), "wn", -EPS, EPS)
+    once("p4v", small, "p4", "pm", 2, None, Op.arith_shift_right)
+    either("pd", "pd", ("c1", 0, 2 * NB), FAR)
+    once("topv", small, "top", "pf", 15.0, None, Op.is_lt)
+    either("pg", "pg", "pf", 1.0, float(H))
+    once("pw0v", small, "pw", ("kb", 0, 16), "pf", None, Op.is_equal)
+    once("p4fv", copy, "v", "p4f", "p4")
+    either("ca", "ca", "top", -FAR)
+    once("pw1v", both, "pw", "pw", ("tab", H, H + 16), Op.mult)
+    once("apv", small, ("ap", 15, C, 16), ("c1", 0, NB), "top", 2.0 ** 90, Op.mult, Op.mult)
+    once("cbv", scan, "cb", "pw", "pw", 0.0, Op.min, Op.min)
+    either("cc", "cc", "top", -FAR, -mark_of(14))
+    either("cd", ("cd", 0, 1), ("cb", 15, 16), 1.0, -mark_of(14))
+    either("h0", ("h0", 0, 2 * NB - 1, 2), ("c1", 0, NB), -FAR)
+    either("h1", ("h0", 1, 2 * NB, 2), ("c1", 0, NB), mark_of(13))
+    once("onev", fill, "one", 64.0)
+    once("ulp", iota, "ul", [[16, 8]], 0)
+    once("luv", copy, "v", "lu", "ul")
+    once("etp", emit, "p", [acc("et")], [acc("one")], lambda e: e.affine_select(T.et[:], T.one[:], [[-1, 516]], Op.is_equal, 0.0, 3, 4))
+    once("k16v", small, ("k16", 0, 64), "kb", "pf", -FAR, Op.is_equal, Op.mult)
+    once("k4v", small, ("k4", 0, 64), "ka", "p4f", -FAR, Op.is_equal, Op.mult)
+    for k in ("k4", "k16"):
+        either(k + "a", (k, 64, 128), (k, 0, 64), 1.0, HOLD)
+        either(k + "b", (k, 0, 64), (k, 64, 128))
+    either("c16", "c16", "pf", -HOLD, 15 * HOLD)
+    either("pb", "pb", "p4f", 4 * HOLD - 4.0, -12 * HOLD)
+    once("c4v", both, "c4", "pb", "pf", Op.add)
+    once("sdv", fill, "sd", -EPS)
+    either("tb", "tb", "ta", -EPS)
+    ramp("idh", ("roots", C, C + H), -H, 1)
+    for i, (a, b) in enumerate(OC):
+        ramp("id%d" % i, ("roots", C - b, C - a), a, 1)
+    for p, (a, b) in enumerate(SPANS):
         n, c, d = b - a, a // 16, b // 16
-        once("ta" + p, iota, ("ta", c, d), [[16, d - c]], n)
-        once("tb" + p, copy, "s", ("tb", c, d), ("ta", c, d), -EPS)
-        once("sd" + p, copy, "s", ("sd", a + 15, b, 16), ("wn", 0, d - c), 16 * EPS, -1.0 - EPS * n)
-        once("lit" + p, ramp, ("way" + p, 0, n), H + b - 1, -1)
-        cuts = sorted({0, H, max(0, H - a)})
-        for x, y in zip(cuts, cuts[1:]):
-            once("far%s%d" % (p, x // 16), iota, ("way" + p, n + x, n + y), [[1, y - x]], a + x + (0 if a + x < H else C))
+        once("ta%dp" % p, iota, ("ta", c, d), [[16, d - c]], n)
+        either("se%d" % p, ("sd", a + 15, b, 16), ("wn", 0, d - c), 16 * EPS, -1.0 - EPS * n)
+        ramp("lit%d" % p, ("way%d" % p, 0, n), b - 1 - front(a)[1], -1)
+        ramp("far%d" % p, ("way%d" % p, n, n + H), C + a - front(a)[0], 1)
 
     def send(t, x):
         if rank + 1 == n_ranks:
             return
         dst = T.cores[rank + 1]
         rid, pid = topo.addr(dst)[:2]
-        a, b = SENDS[x]
+        a, b = XC[x]
         depend("p", [], [("q%d" % t, LO + a, LO + b), ("s%d" % t, LO + a, LO + b)])
         for out, in_ in ((T["hq%d" % t][:, a:b].bitcast(dt.uint8), T["q%d" % t][:, LO + a:LO + b].bitcast(dt.uint8)),
                          (T["hs%d" % t][:, a:b], T["s%d" % t][:, LO + a:LO + b])):
-            g.remote_dma(out, in_, T.sem["arr%d%s" % (t, x)], T.sem.sent, pid, rid, topo.mask(core, dst))
+            g.remote_dma(out, in_, T.sem["arr%d%d" % (t, x)], T.sem.sent, pid, rid, topo.mask(core, dst))
             total["sent"] += len(topo.engines(core, dst))
 
     if rank > 0:
         for t in range(R):
             for name in ("hq%d" % t, "hs%d" % t):
-                log[name] = [(SENDS[x] + (1,), True, "far", ("arr%d%s" % (t, x), 2 * len(topo.engines(T.cores[rank - 1], core)), {}))
-                             for x in SENDS]
+                log[name] = [(XC[x] + (1,), True, "far", ("arr%d%d" % (t, x), 2 * len(topo.engines(T.cores[rank - 1], core)), {}))
+                             for x in range(len(XC))]
 
     def at(i):
         if i % 2:
@@ -287,43 +304,26 @@ def rank_program(g, core, T, topo):
     def col(name, i):
         return (name, i, C, 16)
 
-    def step(word):
-        t, name = int(word[0]), word[1:]
-        q = ("q%d" % t, "s%d" % t)
-        kind, p, qn = name[0], name[1:2], name[-1]
-        where = CUTS if kind in "qudszemfyYC" else SPANS
-        a, b = where.get(p, (0, C))
-        n, h = b - a, "ABCD".find(p)
-        base = n + H
-        digits = "".join(c for c in name if c.isdigit())
-        i = int(digits) if digits else None
+    def walk(kind, i, qn):
         if kind == "D":
             small("du", "dl", -1.0, "pg", Op.mult, Op.add)
         elif kind == "n":
             copy(qn, ("par", 224 * i, 224 * i + 224), "tab", by=("du", 14 * i, 14 * i + 14))
-        elif name == "Wa":
-            small(at(14), col("par", 15), "ca", ("cb", 15, 16), Op.add, Op.max)
-        elif name == "Wb":
-            small(col("pr", 14), at(14), -1.0, mark_of(14), Op.mult, Op.add)
-        elif name == "Wc":
-            both(col("fr", 14), col("pr", 14), col("par", 14), Op.add)
-        elif name == "Wd":
-            both(("h1", 0, 2 * NB - 1, 2), col("par", 13), col("par", 14), Op.subtract)
         elif kind == "N":
             copy(qn, ("h1", 1, 2 * NB, 2), col("par", 14))
-        elif name == "We":
-            scan("h2", "h0", "h1", 0.0, Op.add, Op.max)
-        elif name == "Wh":
-            small(col("yr", 14), col("par", 15), "cc", ("cd", 0, 1), Op.add, Op.max)
-        elif name == "Wf":
-            both("xa", col("cr", 0), at(0), Op.subtract)
-        elif name == "Wg":
-            both("xb", "xa", at(0), Op.max)
-        elif name == "Wi":
-            both("out", "xb", "tb", Op.add)
+        elif kind == "W":
+            [lambda: small(at(14), col("par", 15), "ca", ("cb", 15, 16), Op.add, Op.max),
+             lambda: small(col("pr", 14), at(14), -1.0, mark_of(14), Op.mult, Op.add),
+             lambda: both(col("fr", 14), col("pr", 14), col("par", 14), Op.add),
+             lambda: both(("h1", 0, 2 * NB - 1, 2), col("par", 13), col("par", 14), Op.subtract),
+             lambda: scan("h2", "h0", "h1", 0.0, Op.add, Op.max),
+             lambda: small(col("yr", 14), col("par", 15), "cc", ("cd", 0, 1), Op.add, Op.max),
+             lambda: both("xa", col("cr", 0), at(0), Op.subtract),
+             lambda: both("xb", "xa", at(0), Op.max),
+             lambda: both("out", "xb", "tb", Op.add)][i]()
         elif kind == "a":
             copy(qn, col("ap", i), at(i), BIG / EPS, -mark_of(i) * BIG / EPS)
-        elif kind == "C" and t == 0:
+        elif kind == "A":
             copy(qn, col("cr", i), col("par", i), 1.0, mark_of(i))
         elif kind == "j":
             both(col("yr", i), col("cr", i - 1), col("par", i), Op.subtract)
@@ -342,81 +342,97 @@ def rank_program(g, core, T, topo):
             both(col("fr", i), col("cr", i), at(i), Op.subtract)
         elif kind == "M":
             both(at(i - 1), col("fr", i), at(i), Op.max)
-        elif kind == "d":
-            emit("v", [("hit", a, b)], [psum(UB[h]), ("ap", a, b)],
-                 lambda e: e.tensor_tensor(T.hit[:, a:b], view(psum(UB[h], n)), T.ap[:, a:b], Op.is_ge))
+
+    def step(word):
+        t, kind, qn = int(word[0]), word[1], word[-1]
+        nums = [int(c, 16) for c in word[2:] if c not in "vsy"]
+        p, i = (nums + [0, 0])[:2]
+        if kind in "DnNWaAjJKFBwbM":
+            return walk(kind, p, qn)
+        q = ("q%d" % t, "s%d" % t)
+        if kind in "uohe":
+            banks[kind, p, 0 if kind == "u" else i] = nums[-1]
+        bank = banks.get(({"d": "u", "y": "u", "O": "o", "H": "h", "m": "e", "f": "e"}.get(kind, kind), p, 0 if kind == "u" else i))
+        a, b = (FC if t == R and kind != "S" else QC if kind in "quds" else ZC if kind in "zemf" else OC if kind in "oO" else HC if kind in "hH"
+                else TC if kind in "tL" else SPANS if kind in "IGclgrRp" else [(0, 0)] * 4)[p]
+        n = b - a
+        z = C + H
+        fz, way, base = "fz%d" % t, "way%d" % p, n + H
+        if kind == "d":
+            emit("v", [("hit", a, b)], [psum(bank), ("ap", a, b)],
+                 lambda e: e.tensor_tensor(T.hit[:, a:b], view(psum(bank, n)), T.ap[:, a:b], Op.is_ge))
         elif kind == "s":
             scan(("sc", a, b), ("hit", a, b), ("sd", a, b), 0.0, Op.max, Op.add)
         elif kind == "I":
-            small(("L0", 2 * h, 2 * h + 1), ("sc", a + 15, a + 16), ("out", a // 16, a // 16 + 1), -1.0 / EPS, Op.max, Op.mult)
+            small(("LI", 2 * p, 2 * p + 1), ("sc", a + 15, a + 16), ("out", a // 16, a // 16 + 1), -1.0 / EPS, Op.max, Op.mult)
         elif kind == "t":
             both(("tm", a // 16, b // 16), ("sc", a + 15, b, 16), ("out", a // 16, b // 16), Op.max)
         elif kind == "L":
-            small(("L" + p, 0, n // 8 - 1, 2), ("tm", a // 16, b // 16), -1.0 / EPS, None, Op.mult)
+            small(("LL", a // 8, b // 8 - 1, 2), ("tm", a // 16, b // 16), -1.0 / EPS, None, Op.mult)
         elif kind == "G":
             c = base + 16 * i
-            copy(qn, ("way" + p, c, c + 16), ("way" + p, 0, c), by=("L" + p, 2 * i, 2 * i + 1) if i else ("L0", 2 * h, 2 * h + 1))
+            copy(qn, (way, c, c + 16), (way, 0, c), by=("LL", a // 8 + 2 * i, a // 8 + 2 * i + 1) if i else ("LI", 2 * p, 2 * p + 1))
         elif kind == "c":
-            scan(("ex", a, b), ("k4", 0, n), ("way" + p, base, base + n), 0.0, Op.add, Op.max)
+            scan(("ex", a, b), ("k4", 0, n), (way, base, base + n), 0.0, Op.add, Op.max)
         elif kind == "l":
             small(("l4", a // 4, b // 4), ("ex", a + 3, b, 4), 4.0, "c4", Op.mult, Op.add)
         elif kind == "g":
             c, d = a + n // 2 * i, a + n // 2 * (i + 1)
-            copy(qn, ("fz", 4 * (H + C + c), 4 * (H + C + d)), ("fz", 0, 4 * (H + C + a)), by=("l4", c // 4, d // 4))
+            copy(qn, (fz, 4 * (z + c), 4 * (z + d)), (fz, 4 * front(a)[0], 4 * (z + a)), by=("l4", c // 4, d // 4))
         elif kind == "r":
-            scan(("sr", a, b), ("k16", 0, n), ("way" + p, base, base + n), 0.0, Op.add, Op.max)
+            scan(("sr", a, b), ("k16", 0, n), (way, base, base + n), 0.0, Op.add, Op.max)
         elif kind == "R":
-            small(("l16", a // 16, b // 16), ("sr", a + 15, b, 16), "c16", None, Op.subtract)
+            small(("l16", 8 * p, 8 * p + n // 16), ("sr", a + 15, b, 16), "c16", None, Op.subtract)
         elif kind == "p":
-            copy(qn, ("roots", H + C + a, H + C + b), ("roots", 0, H + C + a), by=("l16", a // 16, b // 16))
+            copy(qn, ("roots", z + a, z + b), ("roots", front(a)[0], z + a), by=("l16", 8 * p, 8 * p + n // 16))
         elif kind == "o":
-            product(OB + i, E, 128 * i, q, 0, C)
+            product(bank, E, 128 * i, q, a, b)
         elif kind == "O":
-            unpack(qn, ("fz", 4 * H + i, 4 * (H + C), 4), OB + i, C)
+            unpack(qn, (fz, 4 * (C - b) + i, 4 * (C - a), 4), bank, n)
         elif kind == "h":
             if rank > 0:
-                product(HB + i, E, 128 * i, ("hq%d" % t, "hs%d" % t), *SENDS[p])
+                product(bank, E, 128 * i, ("hq%d" % t, "hs%d" % t), a, b)
         elif kind == "H":
-            a, b = SENDS[p]
             if rank > 0:
-                unpack(qn, ("fz", 4 * a + i, 4 * b, 4), HB + i, b - a)
-            elif t == 0:
-                copy(qn, ("fz", 4 * a + i, 4 * b, 4), ("c1", 0, b - a), 0.0)
+                unpack(qn, (fz, 4 * (C + a) + i, 4 * (C + b), 4), bank, n)
+            elif i == 0:
+                fill((fz, 4 * (C + a), 4 * (C + b)), 0.0)
         elif kind == "e":
-            product(EB[h] + i, E, 128 * i, q, a, b, True, False)
+            product(bank, E, 128 * i, q, a, b, True, False)
         elif kind == "z":
-            quant("zq", "zs", a, b, "fz", 4 * (H + C + a))
+            quant("zq", "zs", a, b, fz, 4 * (z + a))
         elif kind == "m":
-            product(EB[h] + i, W, 128 * i, ("zq", "zs"), a, b, False, True)
+            product(bank, W, 128 * i, ("zq", "zs"), a, b, False, True)
         elif kind == "f":
-            unpack(qn, ("t%d" % (t + 1), 4 * a + i, 4 * b, 4), EB[h] + i, n)
+            unpack(qn, ("t%d" % (t + 1), 4 * a + i, 4 * b, 4), bank, n)
         elif kind == "q":
             quant(q[0], q[1], a, b, "t%d" % t if t else "xt", 4 * a)
+        elif kind == "u":
+            product(bank, V if t == R else U, 0, q, a, b)
         elif kind == "x":
             send(t, p)
-        elif kind == "u":
-            product(UB[h], V if t == R else U, 0, q, a, b)
         elif kind == "y":
-            unpack(qn, ("yt", a, b), UB[h], n, 1.0)
+            unpack(qn, ("yt", a, b), bank, n, 1.0)
         elif kind == "Y":
             store(qn, T.y[:, a:b], T.yt[:, a:b], ("yt", a, b))
         elif kind == "C":
             store(qn, T.oc[:, 4 * a:4 * b], T[q[0]][:, a:b].bitcast(dt.uint8), (q[0], a, b))
         elif kind == "S":
-            store(qn, T.osc[4 * i:4 * i + 4, :], T[q[1]][32 * i:32 * i + 4, :], (q[1], 0, C))
+            store(qn, T.osc[4 * p:4 * p + 4, :], T[q[1]][32 * p:32 * p + 4, :], (q[1], 0, C))
         elif kind == "T":
-            store(qn, T.ol[:], T.roots[0:128:16, H + C:H + 2 * C], ("roots", H + C, H + 2 * C))
-        elif kind == "v":
+            store(qn, T.ol[:], T.roots[0:128:16, z:z + C], ("roots", z, z + C))
+        elif kind == "V":
             quant("vq", "vs", 0, 128, "vt", 0)
-        elif name == "i0":
+        elif kind == "i" and p == 0:
             quant("ua", "uas", 0, 128, "ut", 0)
-        elif name == "i1":
-            emit("s", [acc("us")], [acc("uas"), acc("lu")], lambda e: e.activation(T.us[:], T.uas[:].indirect(T.lu[:]), Act.Copy))
-        elif name == "i2":
+        elif kind == "i" and p == 1:
+            emit(qn, [acc("us")], [acc("uas"), acc("lu")], (lambda e: e.activation(T.us[:], T.uas[:].indirect(T.lu[:]), Act.Copy)) if qn == "s"
+                 else lambda e: e.tensor_copy(T.us[:], T.uas[:].indirect(T.lu[:])))
+        elif kind == "i":
             emit("v", [acc("uq")], [acc("ua"), acc("lu")],
                  lambda e: e.tensor_copy(T.uq[:].bitcast(dt.uint32), T.ua[:].bitcast(dt.uint32).indirect(T.lu[:])))
         elif kind == "E":
-            quant("eq", "es", 128 * i, 128 * i + 128, "et", 3 - i)
+            quant("eq", "es", 128 * p, 128 * p + 128, "et", 3 - p)
 
     for word in ORDER.split():
         if word in fixed:

from concourse.mybir import AluOpType as Op, ActivationFunctionType as Act, dt

F32, F16, B16, I32, U16, U8, X4 = "float32", "float16", "bfloat16", "int32", "uint16", "uint8", "float8_e4m3fn_x4"
C, H, R = 448, 256, 3
LO = C - H
NB = C // 16
SPANS = ((0, 64), (64, 128), (128, 224), (224, 320), (320, C))
QC = ((0, 128), (128, 320), (320, C))
TC = ((0, 128), (128, 320), (320, C))
ZC = ((0, 128), (128, 320), (320, C))
FC = ((0, 128), (128, 320), (320, C))
OC = ((0, 128), (128, 320), (320, C))
XC = ((0, 128), (128, 256))
HC = ((0, 128), (128, 256))
EPS, BIG, HOLD, FAR = 2.0 ** -11, 2.0 ** 64, 2048.0, 2.0 ** 20
ORDER = (
    "-pap -c1v -kbp -kap -pmv -dly -sdv -pds -twos -pfv -pgs -wnv -tab1v -wps -h1s -pw0v -onev -ulp -pw1v -ta1p -h0s 0D -tab0s 0n0s -topv -ccs -p4v -cas -cbv -x1y -ta4p -cds 0n1v -vts 0Nes 0Abs 0A9s 0A8s -x0y 0Ads 0q1 0A7s 0W3 -luv 0W0 0W5 0W4 -se0s -wqs 0jc -etp -uty 0ja 0aes 0Fe -id1s -se3s 0Be 0A3s 0Jc 0i0 0we 0A1s 0Ja 0x0 0W1 0j8 0Kcs 0Fc 0Bc -lit4p 0i2 0wc 0J8 0q2 -se4s 0Fa 0A5s -se2s 0Kas 0A0s 0x1 0Ba 0acs 0j6 0Aas -id2s 0q0 0wa 0E3 -idhs 0K8s 0j4 0F8 0i1s 0B8 0A4s 0J6 -far4s 0E0 0w8 0A6s 0o031 -lit3p 0K6s 0O03s 0Acs -far2p 0J4 -far3p 0E1 0h033 0h002 0K4s 0o007 0F6 0B6 0a6s 0H03s 0o105 -ta3p 0a8s -p4fv 0j2 0bc 0h016 -ta0p 0b8 0w6 0ba 0J2 0W2 -lit0p 0h103 0F4 0B4 0M8 0E2 0O00s 0A2s -ta2p 0o010 0w4 -far1p 0H00s -se1s 0H01s 0a4s 0b6 0u01 0Ma 0Mc 0b4 0h126 0K2s 0B2 0H10s 0F2 0a7s 0b2 0O01s 0O10s 0o113 0M6 0a9s 0aas 0H12s 0a2s 0a5s 0M4 0Me 0u17 0u25 0w2 0M2 0abs -apv -k4v 0o022 0W6 0a3s 0a0v -lit2p 0ads -far0p 0a1s 0o124 0V 0W7 0d0 0h020 0d1 -tbs 0h116 0d2 0s0 0W8 0O11s -k4as 0H11s 0s1 0s2 0h136 0I0 0O12s 0H02s 0O02s -lit1p 0o131 -pbs 0H13s 0O13s 0t0 0G00s 0I2 0G20s 0t1 0I1 -id0p 0I3 0L0 0G10s 0G30s 0t2 0o235 0L1 0I4 -k16v 0G01v 0G21s 0G11s 0G31s 0e134 0G22s 0G12s 0L2 0G40v -k4bv 0e112 0G02v 0o207 0G41v 0G03s 0O20v 0G32v 0G23s 0G42v -c4v 0G13s 0c0 0G33s 0o223 0G24v 0c1 0l0 0G25v 0G43s 0G34s 0l1 0G44s 0g01v 0g00s 0o216 0c2 0O23v 0G45s 0G35s 0g10v 0g11s 0G46v 0l2 0c3 0O22s 0z0 0O21s 0G47s 0g21v 0e027 0l3 0e011 0c4 0g20s 0m01 0m02 0g31v -k16as 0f02v 0e003 0l4 0m00 0e035 0m03 0g30s 0z1 0f01s 0e107 0e121 0e236 0m12 0m13 0m10 0f00s 0f03s 0g40v "
    "1q0 0m11 0g41s 0f12s 0e203 0z2 0f13s 0f11s 0e220 0f10v 1u05 -k16bs 0m22 0m20 1d0 0m23 0f22s 0f20s 1q1 0e217 1s0 0m21 0f23s 1o031 0f21v 1o025 1I0 1t0 1O03s 1q2 1o004 1u10 1o103 1x0 1d1 1O00s 1G00s 1o122 1I1 1o016 1O02v 1O10s 1o137 1L0 1O12s 1u24 1O13s 1s1 1o111 1G10v 1d2 1G01s 1I3 1o203 1o217 1I2 1t1 1o232 1s2 1x1 1O01s 1h005 1O11v 1L1 1I4 1G11s 1h016 1t2 1G02s 1G20s 1G30s 1O20s 1G12v 1O23s 1h030 1h023 1G21v 1G03s 1G40s 1G31v 1L2 1O21v 1H00v 1H03v 1h131 1G13s 1h114 1G22s 1h102 1G32s 1G41v 1H02s 1G23s 1G33s 1c0 1c1 1H01v 1h125 1H13v 1G42s 1l0 1G24v 1e017 1H11s 1H10s 1G43s 1H12v 1e223 1l1 1G34v 1G25v 1o224 1e000 1e021 1g00v 1g01s 1c2 -c16s 1G44s 1g11s 1G45s 1O22s 1G46s 1G35v 1g10v 1l2 1c3 1z0 1e202 1g21s 1g20v 1m01 1m00 1e036 1G47v 1l3 1g30s 1c4 1m03 1f03s 1e104 1g31v 1m02 1l4 1f02s 1f01s 1g41s 1e125 1e116 1z1 1g40v 1e131 1m13 1f00v 1f13s 1z2 1m11 1f11s 1m12 1m10 1f10s 1e210 1e237 1m20 1f12v 1f20s "
    "2q0 1m23 1f23s 2q1 1m21 1m22 2u05 1f21v 2o011 2o034 1f22s 2d0 2q2 2O01s 2O03s 2o026 2u17 2s0 2O02s 2d1 2I1 2o122 2O12s 2o130 2O13s 2I0 2t0 2u25 2s1 2d2 2G10s 2L0 2I2 2x0 2t1 2s2 2o103 2G00s 2o117 2o004 2I3 2G11v 2O10s 2o215 2h010 2G01s 2L1 2G20s 2t2 2I4 2O00s 2G02s 2G21s 2G40s 2h036 2G30v 2G12v 2O11v 2G31s 2G03s 2L2 2H03s 2H01s 2O21v 2G22v 2G32s 2h001 2G41v 2G13v 2x1 2G23s 2G42s 2h132 2h114 2H11s 2h105 2h127 2h026 2G24s 2c0 2H00v 2G43s 2H13v 2H10s 2e020 2c1 2G33v 2H12v 2o221 2G25s 2H02v 2O22s 2o236 2l0 2g00s 2G34v 2G44v 2G35s 2O23s 2l1 2o201 2g01v 2G45v 2e105 2r0 2c2 2g11s 2r1 2g10v 2l2 2c3 2R0 2z0 2G46s 2e017 2g21v 2O20s 2l3 2G47s 2g20s 2r4 2p0s 2e034 2c4 2g30v 2m02 2g31s 2m01 2f01s 2f02s 2l4 2e006 2g40s 2m03 2R1 2m00 2f00s 2f03s 2r2 2e122 2z1 2g41v 2e133 2e110 2e207 2m11 2r3 2R4 2m10 2R2 2m13 2p1s 2f10s 2z2 2f13v 2m12 2f12s 2p2s "
    "3q0 2R3 2f11v 2e224 2e231 2e216 2m22 2m23 2f23s 2m21 2f22v 2f21s 2p3s 2m20 3u00 2f20v 3q1 3q2 3S3y 3u15 3C1s 3y0s 2p4v 3C2s 3C0y 3u22 3S0s 3y1s 3S1y 3Y0s 3y2v 3Y1s 3Y2y 2Ts 3S2y")


def front(a):
    x, y = [c for c in OC if c[0] <= a < c[1]][0]
    return C - y, x


SCRATCH = {
    "xt": ("sbuf", [128, 4 * C], B16),
    "zq": ("sbuf", [128, C], X4), "zs": ("sbuf", [128, C], U8),
    "wq": ("sbuf", [128, 512], X4), "wp": ("sbuf", [128, 512], U8),
    "ut": ("sbuf", [128, 512], B16), "vt": ("sbuf", [128, 512], B16),
    "ua": ("sbuf", [128, 128], X4), "uas": ("sbuf", [128, 128], U8),
    "uq": ("sbuf", [128, 128], X4), "us": ("sbuf", [128, 128], U8),
    "vq": ("sbuf", [128, 128], X4), "vs": ("sbuf", [128, 128], U8),
    "one": ("sbuf", [128, 516], B16), "et": ("sbuf", [128, 516], B16), "eq": ("sbuf", [128, 512], X4), "es": ("sbuf", [128, 512], U8),
    "c1": ("sbuf", [128, H], F32), "two": ("sbuf", [128, 16], F32), "wn": ("sbuf", [128, H], F32), "tab": ("sbuf", [128, H + 16], F32),
    "pe": ("sbuf", [128, 8 * 64], F32),
    "k4": ("sbuf", [128, 128], F32), "k16": ("sbuf", [128, 128], F32), "ka": ("sbuf", [128, 64], F32), "kb": ("sbuf", [128, 64], F32),
    "dl": ("sbuf", [128, NB], I32), "du": ("sbuf", [128, NB], U16),
    "pa": ("sbuf", [128, 2], I32), "pm": ("sbuf", [128, 2], I32), "p4": ("sbuf", [128, 2], I32),
    "cb": ("sbuf", [128, 16], F32), "pw": ("sbuf", [128, 16], F32),
    "ul": ("sbuf", [128, 8], I32), "lu": ("sbuf", [128, 8], U16), "LI": ("sbuf", [128, 16], U16), "LL": ("sbuf", [128, 2 * NB], U16),
    "l4": ("sbuf", [128, C // 4], U16), "l16": ("sbuf", [128, 64], U16),
    "roots": ("sbuf", [128, H + 2 * C], F32),
    "hit": ("sbuf", [128, C], B16), "sd": ("sbuf", [128, C], B16), "sc": ("sbuf", [128, C], F16),
    "ps": ("psum", [128, 4096], F32),
}
for _n in ("par", "cr", "at", "ap", "yr", "pr", "kr", "fr", "sr", "ex", "yt"):
    SCRATCH[_n] = ("sbuf", [128, C], F32)
for _n in ("pd", "h0", "h1", "h2"):
    SCRATCH[_n] = ("sbuf", [128, 2 * NB], F32)
for _n in ("ta", "tb", "xa", "xb", "out", "tm"):
    SCRATCH[_n] = ("sbuf", [128, NB], F32)
for _n in ("pf", "p4f", "pb", "top", "ca", "cc", "cd", "c4", "c16", "pg"):
    SCRATCH[_n] = ("sbuf", [128, 2], F32)
for _p, (_a, _b) in enumerate(SPANS):
    SCRATCH["way%d" % _p] = ("sbuf", [128, H + 2 * (_b - _a)], F32)
for _i in range(R):
    SCRATCH["fz%d" % _i] = ("sbuf", [128, 4 * (H + 2 * C)], B16)
    SCRATCH["hq%d" % _i] = ("sbuf", [128, H], X4)
    SCRATCH["hs%d" % _i] = ("sbuf", [128, H], U8)
    SCRATCH["t%d" % (_i + 1)] = ("sbuf", [128, 4 * C], B16)
for _i in range(R + 1):
    SCRATCH["q%d" % _i] = ("sbuf", [128, C], X4)
    SCRATCH["s%d" % _i] = ("sbuf", [128, C], U8)

SEMAPHORES = (["cv", "cs", "ct", "cp", "sent", "ldx0", "ldx1", "ldu", "ldw", "ldp", "ldb", "ldv", "done"]
              + ["arr%d%d" % (t, x) for t in range(R) for x in range(len(XC))])


def rank_program(g, core, T, topo):
    rank = T.rank_of(core)
    if rank is None:
        return
    n_ranks = len(T.cores)
    queue = {"v": g.vector, "s": g.scalar, "t": g.tensor, "p": g, "y": g.sync}
    total = {s: 0 for s in SEMAPHORES}
    clock = {q: {} for q in queue}
    log = {}
    banks = {}

    def know(q, tok):
        sem, n, snap = tok
        if clock[q].get(sem, 0) >= n:
            return
        queue[q].wait_ge(T.sem[sem], n)
        for s, m in snap.items():
            clock[q][s] = max(clock[q].get(s, 0), m)
        clock[q][sem] = n

    def meet(x, y):
        if not (x[0] < y[1] and y[0] < x[1]):
            return False
        return x[2] != y[2] or (x[0] - y[0]) % x[2] == 0

    def full(acc):
        return acc if len(acc) == 4 else acc + (1,)

    def depend(q, outs, ins):
        need = {}
        for acc, write in [(full(a), True) for a in outs] + [(full(a), False) for a in ins]:
            name = acc[0]
            for (run, w, oq, tok) in log.get(name, []):
                if not meet(acc[1:], run):
                    continue
                if name == "ps":
                    if oq == q and (q == "t" or not (w or write)):
                        continue
                elif not (w or write):
                    continue
                old = need.get(tok[0])
                if old is None or old[1] < tok[1]:
                    need[tok[0]] = tok
        for tok in sorted(need.values(), key=lambda t: -len(t[2])):
            know(q, tok)

    def note(q, outs, ins, tok):
        for acc, write in [(full(a), True) for a in outs] + [(full(a), False) for a in ins]:
            name, a, b, st = acc
            old = log.setdefault(name, [])
            if write:
                old[:] = [e for e in old if not (a <= e[0][0] and e[0][1] <= b and (st == 1 or (e[0][2] == st and (e[0][0] - a) % st == 0)))]
            old.append((acc[1:], write, q, tok))

    def emit(q, outs, ins, call):
        depend(q, outs, ins)
        sem = "c" + q
        call(queue[q]).then_inc(T.sem[sem], 1)
        total[sem] += 1
        note(q, outs, ins, (sem, total[sem], dict(clock[q])))

    def load(q, out, acc, in_, sem):
        depend(q, [acc], [])
        queue[q].dma_start(out, in_).then_inc(T.sem[sem], 16)
        total[sem] += 16
        note(q, [acc], [], (sem, 16, dict(clock[q])))

    def store(q, out, in_, acc):
        depend(q, [], [acc])
        queue[q].dma_start(out, in_).then_inc(T.sem["done"], 16)
        total["done"] += 16

    def acc(x):
        return (x, 0, SCRATCH[x][1][1]) if isinstance(x, str) else x

    def view(x):
        name, a, b, st = full(acc(x))
        return T[name][:, a:b:st] if st > 1 else T[name][:, a:b]

    def source(x, by):
        return view(x) if by is None else view(x).indirect(view(by))

    def scalar(s):
        return T[s][:, 0:1] if isinstance(s, str) else view(s) if isinstance(s, tuple) else s

    def copy(q, out, in_, scale=1.0, bias=0.0, by=None):
        ins = [acc(x) for x in (in_, by) if x]
        if q == "v" and (scale, bias) == (1.0, 0.0):
            emit("v", [acc(out)], ins, lambda e: e.tensor_copy(view(out), source(in_, by)))
        elif q == "v":
            emit("v", [acc(out)], ins, lambda e: e.tensor_scalar(view(out), source(in_, by), scale, bias, Op.mult, Op.add))
        else:
            emit("s", [acc(out)], ins, lambda e: e.activation(view(out), source(in_, by), Act.Copy, bias=bias, scale=scale))

    def small(out, in_, s1, s2, *ops):
        ins = [acc(in_)] + [acc(s) for s in (s1, s2) if isinstance(s, (str, tuple))]
        emit("v", [acc(out)], ins, lambda e: e.tensor_scalar(view(out), view(in_), scalar(s1), scalar(s2), *ops))

    def both(out, a, b, op):
        emit("v", [acc(out)], [acc(a), acc(b)], lambda e: e.tensor_tensor(view(out), view(a), view(b), op))

    def scan(out, a, b, first, op0, op1):
        emit("v", [acc(out)], [acc(a), acc(b)], lambda e: e.tensor_tensor_scan(view(out), view(a), view(b), first, op0, op1))

    def fill(out, value):
        emit("v", [acc(out)], [], lambda e: e.memset(view(out), value))

    def quant(qn, sn, a, b, tn, c):
        emit("v", [(qn, a, b), (sn, a, b)], [(tn, c, c + 4 * (b - a))],
             lambda e: e.quantize_mx(T[qn][:, a:b], T[sn][:, a:b], T[tn][:, c:c + 4 * (b - a)]))

    def psum(bank, n=512):
        return ("ps", 512 * bank, 512 * bank + n)

    def product(bank, st, c0, mv, a, b, start=True, stop=True):
        n = b - a
        emit("t", [psum(bank)], [(st[0], c0, c0 + 128), (st[1], c0, c0 + 128), (mv[0], a, b), (mv[1], a, b)],
             lambda e: e.matmul_mx(T.ps[:, 512 * bank:512 * bank + n], T[st[0]][:, c0:c0 + 128], T[st[1]][:, c0:c0 + 128],
                                   T[mv[0]][:, a:b], T[mv[1]][:, a:b], start, stop))

    def unpack(qn, out, bank, n, scale=2.0 ** -6):
        in_ = view(psum(bank, n))
        if qn == "v":
            emit("v", [out], [psum(bank)], lambda e: e.tensor_scalar(view(out), in_, scale, None, Op.mult))
        else:
            emit("s", [out], [psum(bank)], lambda e: e.activation(view(out), in_, Act.Copy, scale=scale))

    def iota(out, pattern, base, mult=0):
        if SCRATCH[acc(out)[0]][2] == I32:
            emit("p", [acc(out)], [], lambda e: e.iota(view(out), pattern, base, mult))
        else:
            emit("p", [acc(out)], [], lambda e: e.iota(view(out), pattern, base, mult, allow_small_or_imprecise_dtypes=True))

    def mark_of(i):
        return -1024 * EPS * 2 ** i

    E, W, U, V = ("eq", "es"), ("wq", "wp"), ("uq", "us"), ("vq", "vs")

    fixed = {}

    def once(word, call, *args, **kw):
        fixed["-" + word] = lambda: call(*args, **kw)

    def either(word, *args, **kw):
        for q in "vs":
            once(word + q, copy, q, *args, **kw)

    def ramp(word, out, first, step):
        n = out[2] - out[1]
        once(word + "p", iota, out, [[step, n]], first)
        either(word, out, ("wn", 0, n), float(step), float(first - step))

    for q in "ys":
        once("dl" + q, load, q, T.dl[:], acc("dl"), T.dist[:], "ldb")
        once("ut" + q, load, q, T.ut[:], acc("ut"), T.u[:], "ldu")
        for i, (a, b) in enumerate(((0, LO), (LO, C))):
            once("x%d%s" % (i, q), load, q, T.xt[:, 4 * a:4 * b], ("xt", 4 * a, 4 * b), T.x[:, 4 * a:4 * b], "ldx%d" % i)
        once("wq" + q, load, q, T.wq[:].bitcast(dt.uint8), acc("wq"), T.wc[:], "ldw")
        once("wp" + q, load, q, T.wp[:], acc("wp"), T.ws[:], "ldp")
        once("vt" + q, load, q, T.vt[:], acc("vt"), T.v[:], "ldv")
    once("pap", iota, "pa", [[0, 2]], 0, 1)
    once("kap", iota, "ka", [[0, 16], [1, 4]], 0)
    once("kbp", iota, "kb", [[0, 4], [1, 16]], 0)
    once("c1v", fill, "c1", 1.0)
    either("two", "two", ("c1", 0, 16), 2.0)
    once("pmv", small, "pm", "pa", 15, None, Op.bitwise_and)
    once("wnv", scan, "wn", "c1", "c1", 0.0, Op.mult, Op.add)
    once("wnp", iota, "wn", [[1, H]], 1)
    once("pfv", copy, "v", "pf", "pm")
    once("tab1v", scan, ("tab", H, H + 16), "two", ("c1", 0, 16), mark_of(-1), Op.mult, Op.min)
    either("tab0", ("tab", 0, H), "wn", -EPS, EPS)
    once("p4v", small, "p4", "pm", 2, None, Op.arith_shift_right)
    either("pd", "pd", ("c1", 0, 2 * NB), FAR)
    once("topv", small, "top", "pf", 15.0, None, Op.is_lt)
    either("pg", "pg", "pf", 1.0, float(H))
    once("pw0v", small, "pw", ("kb", 0, 16), "pf", None, Op.is_equal)
    once("p4fv", copy, "v", "p4f", "p4")
    either("ca", "ca", "top", -FAR)
    once("pw1v", both, "pw", "pw", ("tab", H, H + 16), Op.mult)
    once("apv", small, ("ap", 15, C, 16), ("c1", 0, NB), "top", 2.0 ** 90, Op.mult, Op.mult)
    once("cbv", scan, "cb", "pw", "pw", 0.0, Op.min, Op.min)
    either("cc", "cc", "top", -FAR, -mark_of(14))
    either("cd", ("cd", 0, 1), ("cb", 15, 16), 1.0, -mark_of(14))
    either("h0", ("h0", 0, 2 * NB - 1, 2), ("c1", 0, NB), -FAR)
    either("h1", ("h0", 1, 2 * NB, 2), ("c1", 0, NB), mark_of(13))
    once("onev", fill, "one", 64.0)
    once("ulp", iota, "ul", [[16, 8]], 0)
    once("luv", copy, "v", "lu", "ul")
    once("etp", emit, "p", [acc("et")], [acc("one")], lambda e: e.affine_select(T.et[:], T.one[:], [[-1, 516]], Op.is_equal, 0.0, 3, 4))
    once("k16v", small, ("k16", 0, 64), "kb", "pf", -FAR, Op.is_equal, Op.mult)
    once("k4v", small, ("k4", 0, 64), "ka", "p4f", -FAR, Op.is_equal, Op.mult)
    for k in ("k4", "k16"):
        either(k + "a", (k, 64, 128), (k, 0, 64), 1.0, HOLD)
        either(k + "b", (k, 0, 64), (k, 64, 128))
    either("c16", "c16", "pf", -HOLD, 15 * HOLD)
    either("pb", "pb", "p4f", 4 * HOLD - 4.0, -12 * HOLD)
    once("c4v", both, "c4", "pb", "pf", Op.add)
    once("sdv", fill, "sd", -EPS)
    either("tb", "tb", "ta", -EPS)
    ramp("idh", ("roots", C, C + H), -H, 1)
    for i, (a, b) in enumerate(OC):
        ramp("id%d" % i, ("roots", C - b, C - a), a, 1)
    for p, (a, b) in enumerate(SPANS):
        n, c, d = b - a, a // 16, b // 16
        once("ta%dp" % p, iota, ("ta", c, d), [[16, d - c]], n)
        either("se%d" % p, ("sd", a + 15, b, 16), ("wn", 0, d - c), 16 * EPS, -1.0 - EPS * n)
        ramp("lit%d" % p, ("way%d" % p, 0, n), b - 1 - front(a)[1], -1)
        ramp("far%d" % p, ("way%d" % p, n, n + H), C + a - front(a)[0], 1)

    def send(t, x):
        if rank + 1 == n_ranks:
            return
        dst = T.cores[rank + 1]
        rid, pid = topo.addr(dst)[:2]
        a, b = XC[x]
        depend("p", [], [("q%d" % t, LO + a, LO + b), ("s%d" % t, LO + a, LO + b)])
        for out, in_ in ((T["hq%d" % t][:, a:b].bitcast(dt.uint8), T["q%d" % t][:, LO + a:LO + b].bitcast(dt.uint8)),
                         (T["hs%d" % t][:, a:b], T["s%d" % t][:, LO + a:LO + b])):
            g.remote_dma(out, in_, T.sem["arr%d%d" % (t, x)], T.sem.sent, pid, rid, topo.mask(core, dst))
            total["sent"] += len(topo.engines(core, dst))

    if rank > 0:
        for t in range(R):
            for name in ("hq%d" % t, "hs%d" % t):
                log[name] = [(XC[x] + (1,), True, "far", ("arr%d%d" % (t, x), 2 * len(topo.engines(T.cores[rank - 1], core)), {}))
                             for x in range(len(XC))]

    def at(i):
        if i % 2:
            return ("at", i, C, 16)
        return ("pe", 32 * i + 2, 32 * i + 2 + 2 * NB - 1, 2)

    def col(name, i):
        return (name, i, C, 16)

    def walk(kind, i, qn):
        if kind == "D":
            small("du", "dl", -1.0, "pg", Op.mult, Op.add)
        elif kind == "n":
            copy(qn, ("par", 224 * i, 224 * i + 224), "tab", by=("du", 14 * i, 14 * i + 14))
        elif kind == "N":
            copy(qn, ("h1", 1, 2 * NB, 2), col("par", 14))
        elif kind == "W":
            [lambda: small(at(14), col("par", 15), "ca", ("cb", 15, 16), Op.add, Op.max),
             lambda: small(col("pr", 14), at(14), -1.0, mark_of(14), Op.mult, Op.add),
             lambda: both(col("fr", 14), col("pr", 14), col("par", 14), Op.add),
             lambda: both(("h1", 0, 2 * NB - 1, 2), col("par", 13), col("par", 14), Op.subtract),
             lambda: scan("h2", "h0", "h1", 0.0, Op.add, Op.max),
             lambda: small(col("yr", 14), col("par", 15), "cc", ("cd", 0, 1), Op.add, Op.max),
             lambda: both("xa", col("cr", 0), at(0), Op.subtract),
             lambda: both("xb", "xa", at(0), Op.max),
             lambda: both("out", "xb", "tb", Op.add)][i]()
        elif kind == "a":
            copy(qn, col("ap", i), at(i), BIG / EPS, -mark_of(i) * BIG / EPS)
        elif kind == "A":
            copy(qn, col("cr", i), col("par", i), 1.0, mark_of(i))
        elif kind == "j":
            both(col("yr", i), col("cr", i - 1), col("par", i), Op.subtract)
        elif kind == "J":
            both(col("pr", i), col("yr", i), col("par", i), Op.max)
        elif kind == "K":
            copy(qn, col("kr", i), col("pr", i), 1.0, -mark_of(i))
        elif kind == "F":
            both(("pd", 1, 2 * NB, 2), col("cr", i - 1), at(i), Op.subtract)
        elif kind == "B":
            x, y = (("h2", 1, 2 * NB, 2), col("yr", 14)) if i == 14 else (col("kr", i), at(i))
            both(("pe", 32 * i + 3, 32 * i + 2 + 2 * NB, 2), x, y, Op.add)
        elif kind == "w":
            scan(("pe", 32 * i - 63, 32 * i - 63 + 2 * NB), "pd", ("pe", 32 * i + 2, 32 * i + 2 + 2 * NB), 0.0, Op.max, Op.min)
        elif kind == "b":
            both(col("fr", i), col("cr", i), at(i), Op.subtract)
        elif kind == "M":
            both(at(i - 1), col("fr", i), at(i), Op.max)

    def step(word):
        t, kind, qn = int(word[0]), word[1], word[-1]
        nums = [int(c, 16) for c in word[2:] if c not in "vsy"]
        p, i = (nums + [0, 0])[:2]
        if kind in "DnNWaAjJKFBwbM":
            return walk(kind, p, qn)
        q = ("q%d" % t, "s%d" % t)
        if kind in "uohe":
            banks[kind, p, 0 if kind == "u" else i] = nums[-1]
        bank = banks.get(({"d": "u", "y": "u", "O": "o", "H": "h", "m": "e", "f": "e"}.get(kind, kind), p, 0 if kind == "u" else i))
        a, b = (FC if t == R and kind != "S" else QC if kind in "quds" else ZC if kind in "zemf" else OC if kind in "oO" else HC if kind in "hH"
                else TC if kind in "tL" else SPANS if kind in "IGclgrRp" else [(0, 0)] * 4)[p]
        n = b - a
        z = C + H
        fz, way, base = "fz%d" % t, "way%d" % p, n + H
        if kind == "d":
            emit("v", [("hit", a, b)], [psum(bank), ("ap", a, b)],
                 lambda e: e.tensor_tensor(T.hit[:, a:b], view(psum(bank, n)), T.ap[:, a:b], Op.is_ge))
        elif kind == "s":
            scan(("sc", a, b), ("hit", a, b), ("sd", a, b), 0.0, Op.max, Op.add)
        elif kind == "I":
            small(("LI", 2 * p, 2 * p + 1), ("sc", a + 15, a + 16), ("out", a // 16, a // 16 + 1), -1.0 / EPS, Op.max, Op.mult)
        elif kind == "t":
            both(("tm", a // 16, b // 16), ("sc", a + 15, b, 16), ("out", a // 16, b // 16), Op.max)
        elif kind == "L":
            small(("LL", a // 8, b // 8 - 1, 2), ("tm", a // 16, b // 16), -1.0 / EPS, None, Op.mult)
        elif kind == "G":
            c = base + 16 * i
            copy(qn, (way, c, c + 16), (way, 0, c), by=("LL", a // 8 + 2 * i, a // 8 + 2 * i + 1) if i else ("LI", 2 * p, 2 * p + 1))
        elif kind == "c":
            scan(("ex", a, b), ("k4", 0, n), (way, base, base + n), 0.0, Op.add, Op.max)
        elif kind == "l":
            small(("l4", a // 4, b // 4), ("ex", a + 3, b, 4), 4.0, "c4", Op.mult, Op.add)
        elif kind == "g":
            c, d = a + n // 2 * i, a + n // 2 * (i + 1)
            copy(qn, (fz, 4 * (z + c), 4 * (z + d)), (fz, 4 * front(a)[0], 4 * (z + a)), by=("l4", c // 4, d // 4))
        elif kind == "r":
            scan(("sr", a, b), ("k16", 0, n), (way, base, base + n), 0.0, Op.add, Op.max)
        elif kind == "R":
            small(("l16", 8 * p, 8 * p + n // 16), ("sr", a + 15, b, 16), "c16", None, Op.subtract)
        elif kind == "p":
            copy(qn, ("roots", z + a, z + b), ("roots", front(a)[0], z + a), by=("l16", 8 * p, 8 * p + n // 16))
        elif kind == "o":
            product(bank, E, 128 * i, q, a, b)
        elif kind == "O":
            unpack(qn, (fz, 4 * (C - b) + i, 4 * (C - a), 4), bank, n)
        elif kind == "h":
            if rank > 0:
                product(bank, E, 128 * i, ("hq%d" % t, "hs%d" % t), a, b)
        elif kind == "H":
            if rank > 0:
                unpack(qn, (fz, 4 * (C + a) + i, 4 * (C + b), 4), bank, n)
            elif i == 0:
                fill((fz, 4 * (C + a), 4 * (C + b)), 0.0)
        elif kind == "e":
            product(bank, E, 128 * i, q, a, b, True, False)
        elif kind == "z":
            quant("zq", "zs", a, b, fz, 4 * (z + a))
        elif kind == "m":
            product(bank, W, 128 * i, ("zq", "zs"), a, b, False, True)
        elif kind == "f":
            unpack(qn, ("t%d" % (t + 1), 4 * a + i, 4 * b, 4), bank, n)
        elif kind == "q":
            quant(q[0], q[1], a, b, "t%d" % t if t else "xt", 4 * a)
        elif kind == "u":
            product(bank, V if t == R else U, 0, q, a, b)
        elif kind == "x":
            send(t, p)
        elif kind == "y":
            unpack(qn, ("yt", a, b), bank, n, 1.0)
        elif kind == "Y":
            store(qn, T.y[:, a:b], T.yt[:, a:b], ("yt", a, b))
        elif kind == "C":
            store(qn, T.oc[:, 4 * a:4 * b], T[q[0]][:, a:b].bitcast(dt.uint8), (q[0], a, b))
        elif kind == "S":
            store(qn, T.osc[4 * p:4 * p + 4, :], T[q[1]][32 * p:32 * p + 4, :], (q[1], 0, C))
        elif kind == "T":
            store(qn, T.ol[:], T.roots[0:128:16, z:z + C], ("roots", z, z + C))
        elif kind == "V":
            quant("vq", "vs", 0, 128, "vt", 0)
        elif kind == "i" and p == 0:
            quant("ua", "uas", 0, 128, "ut", 0)
        elif kind == "i" and p == 1:
            emit(qn, [acc("us")], [acc("uas"), acc("lu")], (lambda e: e.activation(T.us[:], T.uas[:].indirect(T.lu[:]), Act.Copy)) if qn == "s"
                 else lambda e: e.tensor_copy(T.us[:], T.uas[:].indirect(T.lu[:])))
        elif kind == "i":
            emit("v", [acc("uq")], [acc("ua"), acc("lu")],
                 lambda e: e.tensor_copy(T.uq[:].bitcast(dt.uint32), T.ua[:].bitcast(dt.uint32).indirect(T.lu[:])))
        elif kind == "E":
            quant("eq", "es", 128 * p, 128 * p + 128, "et", 3 - p)

    for word in ORDER.split():
        if word in fixed:
            fixed[word]()
        else:
            step(word)

    for sem in SEMAPHORES:
        if total[sem]:
            g.wait_ge(T.sem[sem], total[sem])
